import numpy as np, ml_dtypes
CORES = [23,119,17,113]
N = 4
BF = ml_dtypes.bfloat16
Q, W, ND, T, S, SH, KS, WM, DM = 256, 4096, 1024, 5, 1, 5, 37, 16, 4
def pick(a, i):
    return np.take_along_axis(a, i.reshape(N, 8, 1, -1), 3).reshape((N, 8, 16) + i.shape[2:])
def bf(a):
    return np.ascontiguousarray(a).astype(np.float32).astype(BF)
def limits(rng, X, lo, hi):
    s = np.sort(np.add.reduce(np.abs(pick(X, rng.integers(0, W, (N, 8, 512))) - pick(X, rng.integers(0, W, (N, 8, 512)))), axis=2), axis=2)
    return np.concatenate([np.take_along_axis(s, rng.choice(np.array(v), (N, 8, 1)), 2) for v in (lo, hi)], axis=2)
def parts(rng):
    top = rng.choice(np.array([64, 128, 256]), (1, 8, 1, 1)) - 1
    X = rng.integers(0, 256, (N, 8, 16, W)) & top; z = rng.integers(0, 256, (N, 8, 16, Q)) & top
    DL = rng.integers(0, 256, (N, 8, 16, ND)); L = rng.integers(0, 256, (N, 8, 16, Q)); R = rng.integers(0, 256, (N, 8, 16, Q))
    n = rng.integers(1, 5, (N, 8, Q)); kp = rng.integers(0, 256, (N, 8, 16, 1)); w = rng.integers(0, 256, (N, 8, 16, 1))
    return X, DL, L, R, z, n, kp, w, limits(rng, X, [10, 26, 51, 77], [410, 450, 480])
def pack(X, DL, L, R, z, n, kp, w, lm):
    return {"stock": bf(X.reshape(N, 128, W)), "donor": bf(DL.reshape(N, 128, ND)), "lend": bf(L.reshape(N, 128, Q)), "rend": bf(R.reshape(N, 128, Q)), "zed": bf(z.reshape(N, 128, Q)),
            "cnt": n.astype(np.int32), "kap": kp.reshape(N, 128, 1).astype(np.int32), "wt": w.reshape(N, 128, 1).astype(np.int32), "lim": lm.astype(np.int32)}
def setup_inputs(rng):
    return pack(*parts(rng))
def setup_inputs_spread(rng):
    def col(m): return (np.exp2(8 * rng.random((N, 8, 1, m))) * rng.random((N, 8, 16, m))).astype(np.int64)
    def few(m): return np.exp2(8 * rng.random((N, 8, 16, m))).astype(np.int64) - rng.integers(0, 2, (N, 8, 16, m))
    X, z = col(W), col(Q)
    return pack(X, few(ND), few(Q), few(Q), z, rng.choice(np.array([1, 1, 1, 2, 3, 4]), (N, 8, Q)), few(1), few(1), limits(rng, X, [1, 10, 40, 120, 300], [200, 400, 460, 490, 508]))
def ends(rng, m):
    k = rng.integers(0, 3, (N, 8, 1, m))
    return np.where(k == 2, 255 * rng.integers(0, 2, (N, 8, 16, m)), 255 * k)
def setup_inputs_ends(rng):
    X, DL, L, R, z = ends(rng, W), ends(rng, ND), ends(rng, Q), ends(rng, Q), ends(rng, Q)
    n = 1 + 3 * rng.integers(0, 2, (N, 8, Q)); kp = 255 * rng.integers(0, 2, (N, 8, 16, 1)); w = 255 * rng.integers(0, 2, (N, 8, 16, 1))
    kp[:, :, 3] = 0; kp[:, :, 15] = 255; w[:, :, 2] = 0; w[:, :, 5] = 255; w[:, 4] = 255
    n[:, :, 0] = 4; n[:, :, 1] = 1; n[:, :, Q - 2] = 1; n[:, :, Q - 1] = 4
    for g in (0, 6):
        w[:, g, 14] = 1; w[:, g, 15] = 16
        for i in (0, 3, Q - 1): z[:, g, :, i] = 0; z[:, g, 14, i] = 15; z[:, g, 15, i] = 255
    for i in (2, 5, Q - 1): z[:, 7, :, i] = 0; z[:, 5, :, i] = 0
    X[:, 7, :, 0] = 255; X[:, 5, :, 0] = 0
    for i in (1, 4, Q - 1): z[:, 4, :, i] = 255
    lm = 4080 * rng.integers(0, 2, (N, 8, 2))
    lm[:, 2, 0] = 0; lm[:, 3, 0] = 4080; lm[:, 0, 1] = 0; lm[:, 1, 1] = 4080; lm[:, 7, 1] = 4080; lm[N - 1, :, 0] = 4080
    return pack(X, DL, L, R, z, n, kp, w, lm)
def far(d):
    return np.minimum(np.maximum(d - 255 * np.arange(16), 0), 255)
def setup_inputs_corners(rng):
    X, DL, L, R, z, n, kp, w, lm = parts(rng); o = KS * np.arange(16); k = np.arange(16)[:, None]
    for q in range(N):
        for g in range(8):
            j = (g // 2 + q) % 4
            if g % 2 == 1 and j == 3: continue
            w[q, g] = 0; DL[q, g, :, 0] = 0
            if g % 2 == 0:
                b = (2, 5, 15, 16)[j]; s = int(rng.integers(20, 100)); v = int(rng.integers(20, 100))
                y = np.full((16, 16), 100); y[0, b:] += s
            else:
                b = 7; s, v = ((4080, 4079), (2049, 2048), (1, 0))[j]
                y = np.zeros((16, 16), np.int64); y[:, b:] = far(s)[:, None]
            for e in range(3):
                X[q, g][:, o + e] = y + far((0, v, v + 1)[e])[:, None] * np.where(y >= 128, -1, 1)
            sb = s if q == 1 else s - 1
            lm[q, g, 0] = v; lm[q, g, 1] = sb
            m = n[q, g]; f = np.where((b > m) & (sb < s), b, 16)
            c = rng.integers(0, 6, Q); p = np.choose(c, [m - 1, m, f - 1, f, 15 + 0 * m, 16 + 0 * m])
            late = np.where((c == 0) | (c == 3), 2, rng.integers(1, 3, (16, Q)))
            R[q, g] = np.where(k == p, 1, np.where(k < p, 2, late))
    return pack(X, DL, L, R, z, n, kp, w, lm)
def setup_inputs_crowd(rng):
    X, DL, L, R, z, n, kp, w, lm = parts(rng); o = KS * np.arange(16)
    lm[:, :, 0] = 4080; lm[4:, :, 0] = rng.choice(np.array([0, 4080]), (N - 4, 8))
    s = (3 - S) % N
    for v in (DL, L, R): v[s] = np.minimum(v[s], 253)
    def plant(q, g, who):
        w[q, g] = 0; DL[q, g, :, 0] = 0; X[q, g][:, o] = 0; X[q, g][:, o + 1] = 255
        R[q, g] = np.where(who, 0, 1); lm[q, g, 0] = rng.choice(np.array([0, 4079])); lm[q, g, 1] = rng.choice(np.array([0, 4080]))
    i = np.arange(Q)
    plant(0, 7, i >= 0); plant(1, 0, i < Q - 1)
    for g in range(8):
        plant(2, g, i < 0); plant(3, g, (i == 0) & (g == 7))
    DL[3, :, :, 1] = 255 - (np.arange(16) & 1); lm[3, :, 0] = 0; lm[3, ::2, 1] = 0
    return pack(X, DL, L, R, z, n, kp, w, lm)
def setup_inputs_ties(rng):
    X, DL, L, R, z, n, kp, w, lm = parts(rng)
    pal = np.repeat(rng.integers(0, 256, (1, 8, 16, 5)), N, axis=0)
    X = pick(pal, rng.integers(0, 5, (N, 8, W))); z = pick(pal, rng.integers(0, 5, (N, 8, Q)))
    kp = rng.choice(np.array([0, 1, 7, 128, 255]), kp.shape); few = np.array([0, 1, 3, 100, 254, 255])
    DL[:, ::2] = rng.choice(few, (N, 4, 16, ND)); R[:, 1::2] = rng.choice(few, (N, 4, 16, Q))
    return pack(X, DL, L, R, z, n, kp, w, limits(rng, X, [10, 51, 150, 256], [150, 256, 400, 480]))
def check_inputs(d):
    bad = []
    for k, lo, hi in (("stock", 0, 255), ("donor", 0, 255), ("lend", 0, 255), ("rend", 0, 255), ("zed", 0, 255), ("cnt", 1, 4), ("kap", 0, 255), ("wt", 0, 255), ("lim", 0, 4080)):
        v = np.asarray(d[k]).astype(np.float64)
        if not np.all((v >= lo) & (v <= hi)): bad.append("range of " + k)
        elif not np.all(v == np.floor(v)): bad.append("whole numbers of " + k)
    return bad
def reference(stock, donor, lend, rend, zed, cnt, kap, wt, lim):
    def whole(a, m): return np.asarray(a).astype(np.float32).astype(np.int64).reshape(N, 8, 16, m)
    X, DL, L, R, z = whole(stock, W), whole(donor, ND), whole(lend, Q), whole(rend, Q), whole(zed, Q)
    n = cnt.astype(np.int64); kp, w = whole(kap, 1), whole(wt, 1)
    th = lim[:, :, 0].astype(np.int64)[:, :, None, None]; sb = lim[:, :, 1].astype(np.int64)[:, :, None, None]
    k = np.arange(16)[:, None]; lane = np.arange(Q); A = np.zeros((N, 1, 1, 1), np.int64)
    for t in range(T):
        if t > 0: L, R, z, n = [np.roll(v, S, axis=0) for v in (L, R, z, n)]
        u = np.add.reduce(w * z, axis=2) & 4095
        ub = u[:, :, None]; nb = n[:, :, None]
        c = ((ub * ub >> SH) + kp * ub + A) & (W - 1)
        m = np.argmin(np.add.reduce(np.abs(pick(X, c) - z[:, :, :, None]), axis=2), axis=2)
        c = np.take_along_axis(c, m[:, :, None], 2)[:, :, 0]
        xc = pick(X, c); D = pick(DL, c & (ND - 1))
        y = pick(X, ((D * ub >> SH) + D + KS * k) & (W - 1))
        h = pick(X, ((R * ub >> SH) + R + KS * k) & (W - 1))
        jump = np.add.reduce(np.abs(y[:, :, :, 1:] - y[:, :, :, :-1]), axis=2)
        f = np.min(np.where((jump > sb) & (k[1:] > nb), k[1:], 16), axis=2); fb = f[:, :, None]
        meet = (np.add.reduce(np.abs(y - h), axis=2) <= th) & (k >= nb) & (k < fb)
        a = np.min(np.where(meet, k, 16), axis=2); ab = a[:, :, None]
        found = a < 16; e = np.where(found, a, f - 1)
        ye = np.take_along_axis(y, e[:, :, None, None], 3)[:, :, :, 0]
        L = np.where((k >= nb) & (k < fb), D, L); L = np.where(k >= ab, R, L)
        done = found | (f == 16)
        R = np.where(done[:, :, None], L, R); n = np.where(done, 1 + (u & 3), f)
        z = (z + ye) >> 1
        ix = np.broadcast_to((WM * lane + (u & (WM - 1)))[:, :, None], (N, 8, 16, Q)); np.put_along_axis(X, ix, (xc + ye) >> 1, 3)
        ix = np.broadcast_to((DM * lane + (u & (DM - 1)))[:, :, None], (N, 8, 16, Q))
        np.put_along_axis(DL, ix, np.where(done[:, :, None], L, np.take_along_axis(DL, ix, 3)), 3)
        A = np.add.reduce(found.astype(np.int64).reshape(N, -1), axis=1).reshape(N, 1, 1, 1)
    return {"yl": bf(L.reshape(N, 128, Q)), "yr": bf(R.reshape(N, 128, Q)), "yd": bf(DL.reshape(N, 128, ND)), "yx": bf(X.reshape(N, 128, W)), "yz": bf(z.reshape(N, 128, Q)), "yn": n.astype(np.float32)}

@@ -1,0 +1,720 @@
+from concourse.mybir import AluOpType as ALU, ActivationFunctionType as ACT
+
+NV, W, ND = 5, 4096, 1024
+NP, QL, NA = 2, 128, 8
+POS = 16 * QL
+XW = 4672
+MAGIC = 25165824.0
+SLOT = 1088
+CFG = {
+    "c_path": ["VVSS", "VVSS"], "h_abs": ["SVSV", "SVSV"], "j_abs": ["SS", "SS"],
+    "ych": [[512] * 4, [512] * 4], "fz": "S", "fx": "P", "plan": False, "tile": True, "ext": True, "DB": 0.8,
+    "same_war": True, "SLACK": 300.0, "TOL": 60.0,
+    "G": 1.55, "F": 1.25, "PE": 0.42, "TT": 1.0, "LAT": 80.0, "OV": 50.0, "REM": 3200.0, "SC": 3.5,
+}
+PRIO = {}
+FIRST = {'xbY': 3400, 'wS': 16700, 'mbS': -13700, 'caS': 6700, 'xaV': 3700, 'uaV': 2600, 'cbV': -1000, 'ybS': -1300, 'cbS': 2500, 'yaS': 1700, 'uaP': 13600, 'eaS': 300, 'wV': 3600, 'ebS': -19300, 'mbV': -1300, 'caV': 900, 'oV': -7100, 'wP': -46300, 'maS': -12100, 'caP': 10700, 'ebP': 17400, 'ebV': -1800, 'eaP': 1000, 'ybV': -8000, 'cbP': 16600, 'yaP': -1700, 'haV': -300, 'wA': 5300, 'xaY': -32000, 'wG': 8000, 'eaG': -3700, 'hbV': -1600, 'uaY': -7700, 'wY': -1000, 'ubY': -18000, 'ybP': -1500, 'xbV': 3100, 'ubV': -6000, 'ebG': -4400, 'ubP': -5300, 'eaV': -1000}
+WHEN = {
+    "ua": [(0, -5, .1)], "ca": [(0, 1, 0), (1, -3, .1), (3, -1, .25)], "ub": [(0, 1, .1)], "cb": [(0, 2.5, .1), (4, 4, .3)],
+    "ma": [(0, 4.5, .1)], "ha": [(0, 7, .1)], "o": [(0, 7.5, .1)], "ya": [(0, 10, .18)], "mb": [(0, 9.5, .1)], "hb": [(0, 13, .1)],
+    "ea": [(0, 15, .1)], "yb": [(0, 16, .18)], "xa": [(0, 21, .1)], "eb": [(0, 22, .1)], "xb": [(0, 23, .1)],
+    "w": [(0, 22.5, .1), (4, 30.5, .15)],
+}
+
+SCRATCH = {
+    "XS": ("sbuf", [128, W + POS], "bfloat16"), "DL": ("sbuf", [128, 2 * ND], "bfloat16"),
+    "ST": ("sbuf", [128, NV * SLOT], "bfloat16"),
+    "AB": ("sbuf", [128, 46000], "bfloat16"), "AF": ("sbuf", [128, 7000], "float32"),
+    "AI": ("sbuf", [128, 4000], "int32"), "AU": ("sbuf", [128, 1500], "uint16"),
+    "PJH": ("psum", [128, 1024], "float32"), "PD0": ("psum", [128, 512], "float32"),
+    "PD1": ("psum", [128, 512], "float32"), "PK": ("psum", [128, 512], "float32"),
+    "PU": ("psum", [128, 512], "float32"), "PW": ("psum", [128, 512], "float32"),
+    "PL": ("psum", [128, 512], "float32"),
+}
+SEMAPHORES = ["cV", "cS", "cP", "cG", "ls"] + ["d%d" % i for i in range(70)] + ["r%d" % i for i in range(16)]
+BYTES = {"XS": 2, "DL": 2, "ST": 2, "AB": 2, "AF": 4, "AI": 4, "AU": 2}
+
+
+def A(name, c0, c1, step=1, p0=0, p1=128):
+    return (name, c0, c1, step, p0, p1)
+
+
+def sl(a, i, j, step=1, p0=None, p1=None):
+    return (a[0], a[1] + i, a[1] + j, step, a[4] if p0 is None else p0, a[5] if p1 is None else p1)
+
+
+def width(a):
+    return (a[2] - a[1] + a[3] - 1) // a[3]
+
+
+def isap(a):
+    return isinstance(a, tuple)
+
+
+def build():
+    ops = []
+    top = {"AB": 0, "AF": 0, "AI": 0, "AU": 0}
+    F, G = CFG["F"], CFG["G"]
+
+    def al(name, n):
+        c = top[name]
+        top[name] = c + (n + 15) // 16 * 16
+        assert top[name] <= SCRATCH[name][1][1], name
+        return A(name, c, c + n)
+
+    def op(eng, cost, call, rd, wr, **kw):
+        o = {"eng": eng, "cost": cost, "call": call, "rd": [r for r in rd if isap(r)], "wr": wr, "id": len(ops)}
+        o.update(kw)
+        ops.append(o)
+        return o
+
+    def two(*aps):
+        return all(BYTES.get(a[0], 4) == 2 for a in aps if isap(a))
+
+    def vc(n, c):
+        return CFG["OV"] + max(64, n * c) * 0.83 * F
+
+    def gc_(n):
+        return 50 + n * G * 0.83 * F
+
+    def copy(out, in_, ind=None, sc=None):
+        if ind is not None:
+            return op("V", gc_(width(out)), ("copy", out, in_, ind, None), [in_, ind], [out])
+        if sc is not None:
+            return op("V", 50 + width(in_) * CFG["SC"] * 0.83 * F, ("copy", out, in_, None, sc), [in_, sc], [out])
+        return op("V", vc(width(out), 0.5 if two(out, in_) else 1), ("copy", out, in_, None, None), [in_], [out])
+
+    def tt(out, a, b, o, ind=None):
+        if ind is not None:
+            c = gc_(width(out))
+        elif a[0][0] == "P" or b[0][0] == "P":
+            c = vc(width(out), 1)
+        else:
+            c = vc(width(out), CFG["TT"] if two(out, a, b) else 2)
+        return op("V", c, ("tt", out, a, b, o, ind), [a, b, ind], [out])
+
+    def ts(out, a, s1, s2, o0, o1=None, ind=None):
+        c = gc_(width(out)) if ind is not None else vc(width(out), 0.5 if two(out, a) else 1)
+        return op("V", c, ("ts", out, a, s1, s2, o0, o1, ind), [a, s1, s2, ind], [out])
+
+    def act(out, a, f, bias=None, scale=None, ind=None, acc=None):
+        c = (65 + width(out) * G * 0.83 * F) if ind is not None else vc(width(out), 1)
+        return op("S", c, ("act", out, a, f, bias, scale, ind, acc), [a, bias, scale, ind], [out] + ([acc] if acc else []))
+
+    def mm(lst, **kw):
+        c = sum(max(min(64, width(m[1])), width(m[2])) * (4 if m[1][0] == "AF" else 1) for m in lst) * CFG["PE"] * F + 30
+        return op("P", c, ("mm", lst), [m[1] for m in lst] + [m[2] for m in lst], [m[0] for m in lst], **kw)
+
+    def iota(out, pat, base=0, cm=0):
+        return op("G", 130 + 2 * width(out) * 0.83 * F, ("iota", out, pat, base, cm), [], [out])
+
+    def memset(out, v):
+        return op("V", vc(width(out), 0.5), ("memset", out, v), [], [out])
+
+    def dma(q, out, in_, nbytes):
+        rd = [in_] if in_[0] in SCRATCH else []
+        wr = [out] if out[0] in SCRATCH else []
+        return op(q, 60, ("dma", out, in_), rd, wr, lat=2000 + nbytes / 250.0, dma=True)
+
+    add, sub, mul, mx, mn = ALU.add, ALU.subtract, ALU.mult, ALU.max, ALU.min
+    band, shr = ALU.bitwise_and, ALU.logical_shift_right
+    ID = ACT.Identity
+
+    def slot(t):
+        return A("ST", t * SLOT, (t + 1) * SLOT)
+
+    def part(a, p, n=QL):
+        return sl(a, n * p, n * p + n)
+
+    ZL = [al("AB", NP * QL) for t in range(NV)]
+    ZN = [al("AB", NP * QL) for t in range(NV)]
+
+    wti, kpi, lmi, cni = al("AI", 1), al("AI", 1), al("AI", 2), al("AI", 256)
+    dma("Y", wti, A("wt", 0, 1), 0)
+    dma("Y", ZL[0], A("zed", 0, 256), 65536)
+    dma("A", kpi, A("kap", 0, 1), 0)
+    dma("Y", A("XS", 0, W), A("stock", 0, W), 1 << 20)
+    dma("A", sl(lmi, 0, 2, 1, 0, 8), A("lim", 0, 2, 1, 0, 8), 0)
+    dma("A", sl(cni, 0, 256, 1, 0, 8), A("cnt", 0, 256, 1, 0, 8), 0)
+    dma("Y", A("DL", 0, ND), A("donor", 0, ND), 1 << 20)
+    dma("Y", A("XS", W, XW), A("stock", 0, XW - W), 1 << 20)
+    dma("Y", sl(slot(0), 304, 560), A("rend", 0, 256), 1 << 20)
+    dma("Y", sl(slot(0), 48, 304), A("lend", 0, 256), 1 << 20)
+
+    PI, t1, t2, t3, t4 = [al("AI", 1) for _ in range(5)]
+    XI, X16, X8 = al("AF", 144), al("AF", 128), al("AF", 128)
+    iota(PI, [[0, 1]], 0, 1)
+    iota(XI, [[1, 144]])
+    iota(X16, [[16, 8], [0, 16]])
+    iota(X8, [[256, 16], [0, 8]])
+    G16, PM, Pf, wf, kf, P7, P3 = [al("AF", 1) for _ in range(7)]
+    ts(t1, PI, 112, None, band); copy(G16, t1)
+    ts(t2, PI, 15, None, band); copy(PM, t2)
+    ts(t3, PI, 7, None, band); copy(P7, t3)
+    ts(t4, PI, 3, 1, shr, band); copy(P3, t4)
+    copy(Pf, PI); copy(wf, wti); copy(kf, kpi)
+    BO, WBO, I1, NI, HI, BIGI, ON = [al("AB", 128) for _ in range(7)]
+    M1, MW, MP, MN, M2P, M2N = [al("AB", 144) for _ in range(6)]
+    ts(M1, XI, G16, 15.0, sub, ALU.is_equal)
+    ts(MW, M1, wf, None, mul)
+    ts(WBO, X16, G16, wf, ALU.is_equal, mul)
+    ts(BO, X16, G16, None, ALU.is_equal)
+    ts(I1, sl(XI, 0, 128), Pf, None, ALU.is_equal)
+    act(NI, I1, ID, scale=-1.0)
+    act(MP, M1, ID, scale=4096.0); act(MN, M1, ID, scale=-4096.0)
+    act(M2P, M1, ID, scale=8192.0); act(M2N, M1, ID, scale=-8192.0)
+    act(HI, I1, ID, scale=0.5); act(BIGI, I1, ID, scale=-33554432.0)
+    memset(ON, 1.0 / 256)
+
+    def win(M, b):
+        return sl(M, 15 - b, 143 - b)
+
+    PM256, B128, K37, R8, TC, P16, PL2, CM, CH, CN = [al("AF", 1) for _ in range(10)]
+    ts(PM256, PM, 256.0, None, mul); ts(B128, PM, 128.0, None, mul); ts(K37, PM, 37.0, None, mul)
+    ts(R8, PM, -8.0, -6.5, mul, add); ts(TC, P7, 16.0, P3, mul, add); ts(P16, Pf, 16.0, None, mul)
+    ts(PL2, PM, 2.0, None, ALU.is_lt)
+    memset(CM, MAGIC); memset(CH, -0.5); memset(CN, -MAGIC / 2)
+    kx, km, KAP = al("AB", 128), al("AB", 128), al("AF", 128)
+    ts(kx, X8, PM256, kf, ALU.is_equal, mul)
+    ts(km, X8, PM256, PM256, ALU.is_equal, mul)
+    mm([(A("PK", 0, 128), BO, kx, True, True)])
+    act(KAP, A("PK", 0, 128), ID)
+    REP8, REPA, TAU = al("AU", 8), al("AU", 16), al("AU", 8)
+    ts(REP8, sl(XI, 0, 8), 0.0, P7, mul, add)
+    ts(TAU, sl(XI, 0, 8), 2.0, TC, mul, add)
+    copy(REPA, sl(XI, 0, 16))
+    K12, C12, CE, SK = al("AF", 256), al("AF", 256), al("AF", 8), al("AF", 8)
+    iota(K12, [[0, 16], [8, 16]])
+    iota(C12, [[-6, 2], [128, 8], [-8, 16]], 134)
+    RC, K0 = al("AB", 256), al("AB", 128)
+    ts(K0, sl(K12, 0, 128), 0.0, None, ALU.is_equal)
+    ts(part(RC, 0), K0, PL2, None, mx); memset(part(RC, 1), 0.0)
+    memset(sl(K12, 0, 256, 16), 999.0)
+    ts(sl(C12, 0, 128, 16), sl(C12, 0, 128, 16), -127.0, None, add)
+    ts(CE, sl(XI, 0, 8), 256.0, 128.0, mul, add); ts(SK, sl(XI, 0, 8), 128.0, 134.0, mul, add)
+    PB, BB = al("AF", 16), al("AB", 2048)
+    ts(PB, sl(XI, 0, 16), PM, None, ALU.is_equal)
+    for b in range(16):
+        act(sl(BB, 128 * b, 128 * b + 128), BO, ID, scale=sl(PB, b, b + 1))
+    BASE, FL, CXD = al("AF", 64), al("AB", 48), al("AF", 32)
+    LANE = sl(BASE, 32, 48)
+    ts(LANE, sl(XI, 0, 16), 16.0, PM, mul, add)
+    ts(sl(BASE, 48, 64), sl(XI, 0, 16), 16.0, PM, mul, add)
+    ts(sl(CXD, 0, 8), sl(LANE, 0, 8), 16.0, None, mul); ts(sl(CXD, 8, 16), sl(LANE, 0, 8), 16.0, None, mul)
+    ts(sl(CXD, 16, 32), LANE, 4.0, None, mul)
+    lmf, E8, M8, n8r = al("AF", 2), al("AF", 128), al("AB", 144), al("AB", 256)
+    r8 = lambda a: sl(a, 0, width(a), 1, 0, 8)
+    copy(r8(lmf), r8(lmi))
+    ts(r8(E8), r8(X16), r8(P16), None, ALU.is_equal)
+    ts(r8(M8), r8(XI), r8(P16), 15.0, sub, ALU.is_equal)
+    ts(r8(n8r), r8(cni), 8.0, None, mul)
+    mm([(A("PL", 0, 2), r8(E8), r8(lmf), True, True)])
+    li, lh, ll = al("AI", 2), al("AI", 2), al("AI", 2)
+    ts(sl(li, 0, 1), A("PL", 0, 1), 1.0, None, add); copy(sl(li, 1, 2), A("PL", 1, 2))
+    ts(lh, li, 8128, None, band); ts(ll, li, 63, None, band)
+    s0, s1, s2, sv = al("AF", 2), al("AF", 2), al("AF", 1), al("AF", 2)
+    ts(s0, lh, sl(PB, 0, 1), None, mul); ts(s1, ll, sl(PB, 1, 2), None, mul); tt(sv, s0, s1, add)
+    ts(s2, sl(PB, 2, 3), -8192.0, sl(sv, 1, 2), mul, add)
+    LJ, LH = al("AB", 128), al("AB", 128)
+    ts(LJ, BO, s2, -4096.0, mul, mul); ts(LH, BO, sl(sv, 0, 1), 4096.0, mul, mul)
+    mm([(A("PL", 16, 32), r8(win(M8, b)), sl(r8(n8r), b, 256, 16), b == 0, b == 15) for b in range(16)])
+    act(sl(slot(0), 32, 48), A("PL", 16, 32), ID)
+
+    B = []
+    for p in range(NP):
+        d = {k: al("AB", POS) for k in ("cd", "ca", "hd", "ha", "ja")}
+        d["y"], d["zt"] = al("AB", POS + 16), al("AB", 512)
+        memset(sl(d["y"], 0, 16), 0.0)
+        for k, n in (("uu", 8), ("base", 8), ("cp", 128), ("cq", 128), ("km", 8), ("kap", 8),
+                     ("c", 8), ("cc", 16), ("hp", 128), ("hq", 128), ("yp", 128), ("yq", 128)):
+            d[k] = al("AI", n)
+        for k, n in (("u32", 128), ("bA", 8), ("ku", 128), ("k1", 64), ("k2", 64), ("k3", 32), ("k4", 16), ("cu", 8), ("a12", 256),
+                     ("sc", 128), ("zx", 256), ("s", 256), ("sm", 256)):
+            d[k] = al("AF", n)
+        for k, n in (("co", 128), ("cco", 16), ("ho", 128), ("yo", 128), ("eo", 8)):
+            d[k] = al("AU", n)
+        d["xn"], d["xc"], d["ye"], d["zx2"] = al("AB", QL), al("AB", QL), al("AB", QL), al("AB", 2 * QL)
+        B.append(d)
+    UR, U, UM, KI, TK = al("AI", 272), al("AI", 272), al("AI", 32), al("AI", 16), al("AI", 16)
+    AC, junk, O48, N2, NF = al("AF", 1), al("AF", 16), al("AF", 48), al("AF", 32), al("AF", 256)
+    XO, OO = al("AU", 16), al("AU", 48)
+    INV, DD, ALT, SG, TM = al("AB", 272), al("AB", 256), al("AB", 256), al("AB", 512), al("AB", 512)
+    memset(sl(INV, 256, 272), 0.0)
+    HALF = al("AB", 2 * QL)
+    memset(HALF, 0.5)
+    XC, XE = A("XS", 0, W), A("XS", 0, XW)
+    ulp = [sl(U, 128, 136), sl(U, 136, 144)]
+    unl = [sl(U, 0, 128), sl(U, 144, 272)]
+    rot = [0]
+
+    def bank():
+        rot[0] ^= 1
+        return A("PD%d" % rot[0], 0, 512)
+
+    def stage_u(t, p):
+        d, z = B[p], part(ZL[t], p)
+        pu = A("PU", 136 * p, 136 * p + 136)
+        a, b_ = (128, 0) if p == 0 else (0, 8)
+        mm([(sl(pu, a, a + 8), win(MW, b), sl(z, b, QL, 16), b == 0, b == 15) for b in range(16)] + [(sl(pu, b_, b_ + 128), WBO, z, True, True)])
+        for m in range(4 if CFG["tile"] else 0):
+            dma("Y", part(d["zt"], m), z if t else A("zed", QL * p, QL * p + QL), 32768)
+        copy(part(UR, p, 136), pu)
+        ts(part(U, p, 136), part(UR, p, 136), 4095, None, band)
+        u = ulp[p]
+        tt(d["uu"], u, u, mul)
+        ts(d["base"], d["uu"], 5, 4095, shr, band)
+        tt(d["ku"], u, KAP, mul, ind=REP8)
+        ts(d["u32"], unl[p], 32.0, None, add)
+        if CFG["fz"] == "S" and CFG["fx"] != "P":
+            act(sl(d["zx"], 0, QL), z, ID, bias=CH)
+
+    def stage_o(t):
+        u = sl(U, 128, 144)
+        ts(sl(UM, 0, 16), u, 15, None, band); ts(sl(UM, 16, 32), u, 3, None, band)
+        tt(sl(BASE, 0, 32), UM, CXD, add)
+        copy(XO, sl(BASE, 0, 16))
+        ts(sl(slot(t), 0, 16), sl(UM, 16, 32), 8.0, 8.0, mul, add)
+        tt(sl(INV, 0, 256), sl(slot(t), 32, 48), K12, ALU.is_ge, ind=REPA)
+
+    def stage_c(t, p):
+        d, z = B[p], part(ZL[t], p)
+        ts(d["bA"], d["base"], AC if t else 0.0, None, add)
+        XC = A("XS", 0, W + POS if t and CFG["ext"] else W)
+        tt(d["cp"], d["base" if CFG["ext"] else "bA"], d["ku"], add, ind=REP8)
+        ts(d["cq"], d["cp"], 4095, None, band)
+        if CFG["ext"] and t:
+            ts(d["co"], d["cq"], AC, None, add)
+        else:
+            copy(d["co"], d["cq"])
+        path = CFG["c_path"][p]
+        for c in range(4):
+            lo = 512 * c
+            cd, ca = sl(d["cd"], lo, lo + 512), sl(d["ca"], lo, lo + 512)
+            if path[c] in "VR":
+                if CFG["tile"]:
+                    tt(cd, XC, d["zt"], sub, ind=part(d["co"], c, 32))
+                for m in range(0 if CFG["tile"] else 4):
+                    tt(part(cd, m), XC, z, sub, ind=sl(d["co"], 32 * c + 8 * m, 32 * c + 8 * m + 8))
+                if path[c] == "V":
+                    act(ca, cd, ACT.Abs)
+                else:
+                    ts(ca, cd, 0.0, None, mx)
+            else:
+                if path[c] == "S":
+                    act(cd, XC, ID, ind=part(d["co"], c, 32))
+                else:
+                    copy(cd, XC, ind=part(d["co"], c, 32))
+                pd = bank()
+                lst = []
+                for m in range(4):
+                    lst += [(part(pd, m), I1, part(cd, m), True, False), (part(pd, m), NI, z, False, True)]
+                mm(lst)
+                act(ca, pd, ACT.Abs)
+            if c & 1:
+                h = c >> 1
+                pk = A("PK", QL * p + 64 * h, QL * p + 64 * h + 64)
+                lst = [(pk, BO, part(kx, h, 64), True, False), (pk, BO, part(km, h, 64), False, False)]
+                ra, rb = path[c - 1] == "R", path[c] == "R"
+                for (x0, x1, r) in (((0, 2, ra),) if ra == rb else ((0, 1, ra), (1, 2, rb))):
+                    o = sl(pk, 32 * x0, 32 * x1)
+                    for (M, src) in (((MN, "cd"), (M2P, "ca")) if r else ((MP, "ca"),)):
+                        lst += [(o, win(M, b), sl(d[src], 1024 * h + 512 * x0 + b, 1024 * h + 512 * x1, 16), False, False) for b in range(16)]
+                lst[-1] = lst[-1][:4] + (True,)
+                mm(lst)
+                if h == 0:
+                    act(d["k1"], pk, ID)
+                else:
+                    tt(d["k2"], pk, d["k1"], mn)
+
+    def stage_m(t, p):
+        d = B[p]
+        for a, b, n in (("k2", "k3", 32), ("k3", "k4", 16), ("k4", "km", 8)):
+            tt(d[b], sl(d[a], 0, n), sl(d[a], n, 2 * n), mn)
+        ts(d["kap"], d["km"], 255, None, band)
+        tt(d["cu"], d["kap"], ulp[p], mul)
+        tt(d["c"], d["cu"], d["bA"], add)
+        ts(sl(d["cc"], 0, 8), d["c"], 1023, None, band); ts(sl(d["cc"], 8, 16), d["c"], 4095, None, band)
+        copy(d["cco"], d["cc"])
+        tt(d["yp"], A("DL", 0, ND), d["u32"], mul, ind=sl(d["cco"], 0, 8))
+        ts(d["yq"], d["yp"], 5, 4095, shr, band)
+        ts(d["yo"], d["yq"], K37, None, add, ind=TAU)
+        act(part(DD, p), A("DL", 0, ND), ID, ind=sl(d["cco"], 0, 8))
+        if CFG["fx"] == "P":
+            act(d["xc"], XC, ID, ind=sl(d["cco"], 8, 16))
+        else:
+            act(sl(d["zx"], QL, 2 * QL), XC, ID, bias=CH if CFG["fx"] != "V" else None, ind=sl(d["cco"], 8, 16))
+
+    def stage_h(t, p):
+        d = B[p]
+        tt(d["hp"], part(sl(slot(t), 304, 560), p), d["u32"], mul)
+        ts(d["hq"], d["hp"], 5, 4095, shr, band)
+        ts(d["ho"], d["hq"], K37, None, add, ind=TAU)
+
+    def stage_y(t, p):
+        d = B[p]
+        pjh = A("PJH", 512 * p, 512 * p + 256)
+        pj, ph = part(pjh, 0), part(pjh, 1)
+        first = mm([(pjh, LJ, RC, True, False), (ph, LH, part(RC, 0), False, False)])
+        last = [first, first]
+        lo = 0
+        for ch in CFG["ych"][p]:
+            y = sl(d["y"], 16 + lo, 16 + lo + ch)
+            act(y, XE, ID, ind=sl(d["yo"], lo // 16, (lo + ch) // 16))
+            hd, ha = sl(d["hd"], lo, lo + ch), sl(d["ha"], lo, lo + ch)
+            tt(hd, XE, y, sub, ind=sl(d["ho"], lo // 16, (lo + ch) // 16))
+            bs = range(lo // QL, (lo + ch) // QL)
+            if CFG["j_abs"][p][lo * 2 // POS] == "S":
+                for l2 in range(lo, lo + ch, 512):
+                    n2 = min(512, lo + ch - l2)
+                    pd = sl(bank(), 0, n2)
+                    mm([(pd, I1, sl(d["y"], 16 + l2, 16 + l2 + n2), True, False), (pd, NI, sl(d["y"], 15 + l2, 15 + l2 + n2), False, True)])
+                    act(sl(d["ja"], l2, l2 + n2), pd, ACT.Abs)
+                    last[0] = mm([(pj, win(MP, b), part(d["ja"], b), False, False) for b in range(l2 // QL, (l2 + n2) // QL)], after=[last[0]])
+            else:
+                last[0] = mm([(pj, win(MN, b), sl(d["y"], e + QL * b, e + QL * b + QL), False, False) for b in bs for e in (15, 16)], after=[last[0]])
+                tt(sl(d["ja"], lo, lo + ch), y, sl(d["y"], 15 + lo, 15 + lo + ch), mx)
+                last[0] = mm([(pj, win(M2P, b), part(d["ja"], b), False, False) for b in bs], after=[last[0]])
+            if CFG["h_abs"][p][lo * 4 // POS] == "S":
+                act(ha, hd, ACT.Abs)
+                last[1] = mm([(ph, win(MN, b), part(d["ha"], b), False, False) for b in bs], after=[last[1]])
+            else:
+                last[1] = mm([(ph, win(MP, b), part(d["hd"], b), False, False) for b in bs], after=[last[1]])
+                ts(ha, hd, 0.0, None, mx)
+                last[1] = mm([(ph, win(M2N, b), part(d["ha"], b), False, False) for b in bs], after=[last[1]])
+            lo += ch
+        mm([(pj, BIGI, sl(INV, QL * p, QL * p + QL), False, False), (ph, BIGI, sl(INV, QL * p + 1, QL * p + QL + 1), False, True)], after=last)
+        tt(d["a12"], pjh, C12, mn)
+
+    nrem = [0]
+
+    def send(src, dst):
+        k = nrem[0]
+        nrem[0] += 1
+        op("G", 900, ("rem", dst, src, k), [src], [dst], lat=CFG["REM"] + width(src), rem=k)
+
+    def stage_e(t, p):
+        d, z = B[p], part(ZL[t], p)
+        op("V", vc(128, 1), ("scan", d["sc"], sl(d["a12"], 0, 128), sl(d["a12"], 128, 256)), [d["a12"]], [d["sc"]])
+        sc = sl(d["sc"], 15, 128, 16)
+        tt(part(KI, p, 8), CE, sc, sub)
+        ts(d["eo"], part(KI, p, 8), 0.125, B128, mul, add)
+        yw = sl(d["y"], 16, 16 + POS)
+        if CFG["fx"] == "P":
+            ps = A("PJH", 512 * p + 256, 512 * p + 512)
+            pz, px = part(ps, 0), part(ps, 1)
+            pre = mm([(ps, NI, HALF, True, False), (pz, I1, z, False, False), (px, I1, d["xc"], False, False)])
+            act(d["ye"], yw, ID, ind=d["eo"])
+            mm([(px, I1, d["ye"], False, False), (pz, I1, d["ye"], False, True)], after=[pre])
+            ts(d["zx2"], ps, MAGIC, MAGIC, add, sub)
+            act(part(ZN[t], p), part(d["zx2"], 0), ID, scale=0.5)
+            if t + 1 < NV:
+                send(part(ZN[t], p), part(ZL[t + 1], p))
+        for h in range(2 if CFG["fx"] != "P" else 0):
+            s_, sm = part(d["s"], h), part(d["sm"], h)
+            if h and CFG["fx"] == "M":
+                tt(s_, yw, part(d["zx"], h), add, ind=d["eo"])
+                ts(d["xn"], s_, MAGIC, MAGIC, add, sub)
+                continue
+            if CFG["fx" if h else "fz"] == "S":
+                tt(s_, yw, part(d["zx"], h), add, ind=d["eo"])
+                act(sm, s_, ID, bias=CM)
+            else:
+                tt(s_, yw, part(d["zx"], h) if h else z, add, ind=d["eo"])
+                ts(sm, s_, -0.5, MAGIC, add, add)
+            act(d["xn"] if h else part(ZN[t], p), sm, ID, bias=CN, scale=0.5)
+            if h == 0 and t + 1 < NV:
+                send(part(ZN[t], p), part(ZL[t + 1], p))
+        tt(sl(slot(t), 16 + 8 * p, 24 + 8 * p), SK, sc, sub)
+
+    def stage_x(t, p):
+        lo = POS * p
+        if CFG["fx"] in "MP":
+            o, i, x = A("XS", lo, lo + POS), B[p]["xn"] if CFG["fx"] == "M" else part(B[p]["zx2"], 1), part(XO, p, 8)
+            op("V", 50 + QL * CFG["SC"] * 0.83 * F, ("tts", o, i, part(HALF, 0), mul, x), [i, HALF, x], [o])
+        else:
+            copy(A("XS", lo, lo + POS), B[p]["xn"], sc=part(XO, p, 8))
+        if t + 1 == NV:
+            dma("Y", A("yx", lo, lo + POS), A("XS", lo, lo + POS), 1 << 19)
+        elif p == 0:
+            n = POS if CFG["ext"] else XW - W
+            dma("Y", A("XS", W, W + n), A("XS", 0, n), 256 * n * CFG["DB"])
+
+    def stage_w(t):
+        s = slot(t)
+        L, nn, Ln, Rn = sl(s, 48, 304), sl(s, 560, 576), sl(s, 576, 832), sl(s, 832, 1088)
+        ts(TK, KI, 3, None, band)
+        ts(sl(FL, 32, 48), TK, 1.0, 256.0, ALU.is_lt, mul)
+        if t + 1 < NV:
+            mm([(A("PL", 0, 16), ON, sl(FL, 32, 48), True, True)])
+            act(junk, A("PL", 0, 16), ID, acc=AC)
+        ts(sl(FL, 16, 32), TK, 2.0, 272.0, ALU.is_lt, mul)
+        ts(sl(FL, 0, 16), TK, 2.0, 1024.0, ALU.is_ge, mul)
+        tt(O48, FL, sl(BASE, 16, 64), add)
+        copy(OO, O48)
+        tt(N2, sl(s, 0, 32), sl(FL, 0, 32), add)
+        tt(nn, sl(N2, 0, 16), sl(N2, 16, 32), mn)
+        mm([(A("PW", b, 512, 16), part(BB, b), sl(s, 16, 48), True, True) for b in range(16)])
+        act(ALT, sl(s, 48, 560), ID, ind=sl(OO, 32, 48))
+        act(SG, A("PW", 0, 512), ACT.Sign, bias=R8)
+        pd = A("PW", 0, 512)
+        pa, pb = part(pd, 0, 256), part(pd, 1, 256)
+        mm([(pb, I1, L, True, False), (pb, NI, DD, False, True), (pa, I1, DD, True, False), (pa, NI, ALT, False, True)])
+        tt(TM, pd, SG, mul)
+        pl = A("PL", 256, 512)
+        mm([(pl, HI, r, i == 0, i == 3) for i, r in enumerate((L, ALT, part(TM, 0, 256), part(TM, 1, 256)))])
+        act(Ln, pl, ID)
+        act(Rn, sl(s, 304, 832), ID, ind=sl(OO, 16, 32))
+        copy(A("DL", 0, 2 * ND), Ln, sc=sl(OO, 0, 16))
+        if t + 1 < NV:
+            send(sl(s, 560, 1088), sl(slot(t + 1), 32, 560))
+        else:
+            dma("A", A("yz", 0, 256), ZN[t], 65536)
+            dma("A", A("yl", 0, 256), Ln, 65536)
+            dma("A", A("yr", 0, 256), Rn, 65536)
+            pn = A("PU", 0, 256, 1, 0, 8)
+            mm([(sl(pn, b, 256, 16), sl(BB, 128 * b, 128 * b + 128, 16), nn, True, True) for b in range(16)])
+            act(r8(NF), pn, ID, scale=0.125)
+            dma("A", A("yn", 0, 256, 1, 0, 8), r8(NF), 0)
+            dma("Y", A("yd", 0, ND), A("DL", 0, ND), 1 << 18)
+
+    def run(name, st, *a):
+        k = len(ops)
+        st(*a)
+        for o in ops[k:]:
+            o["stage"], o["k"], o["t"] = name + ("ab"[a[1]] if len(a) > 1 else ""), o["id"] - k, a[0]
+            o["key"] = "%s%s%d" % (name.upper() if a[0] + 1 == NV else name, "ab"[a[1]] if len(a) > 1 else "", o["id"] - k)
+
+    for t in range(NV):
+        for name, st in (("u", stage_u), ("c", stage_c), ("m", stage_m), ("h", stage_h)):
+            for p in range(NP):
+                run(name, st, t, p)
+        run("o", stage_o, t)
+        for p in range(NP):
+            run("y", stage_y, t, p)
+            run("e", stage_e, t, p)
+        for p in range(NP):
+            run("x", stage_x, t, p)
+        run("w", stage_w, t)
+    return ops
+
+
+def depend(ops):
+    hist = {}
+    banks = {}
+    for o in ops:
+        hard, soft = set(), set()
+        e = o["eng"]
+        for a in o["rd"]:
+            for (c0, c1, w, j) in hist.get(a[0], []):
+                if w and c0 < a[2] and a[1] < c1:
+                    hard.add(j)
+        for a in o["wr"]:
+            for (c0, c1, w, j) in hist.get(a[0], []):
+                if c0 < a[2] and a[1] < c1:
+                    x = ops[j]
+                    same = x["eng"] == e and "lat" not in x and "lat" not in o and (e == "P" or not (w or CFG["same_war"]))
+                    (soft if same else hard).add(j)
+        for a in o["rd"] + o["wr"]:
+            if a[0][0] == "P":
+                for k in range(a[1] // 512, (a[2] - 1) // 512 + 1):
+                    cur = banks.setdefault((a[0], k), [e, [], []])
+                    if cur[0] != e:
+                        cur[0], cur[1], cur[2] = e, [], cur[1]
+                    hard.update(cur[2])
+                    cur[1].append(o["id"])
+        if "after" in o:
+            soft.update(x["id"] for x in o["after"])
+        for a in o["wr"]:
+            h = hist.setdefault(a[0], [])
+            if a[3] == 1 and a[4] == 0 and a[5] == 128:
+                h[:] = [x for x in h if not (a[1] <= x[0] and x[1] <= a[2])]
+            h.append((a[1], a[2], True, o["id"]))
+        for a in o["rd"]:
+            hist.setdefault(a[0], []).append((a[1], a[2], False, o["id"]))
+        hard.discard(o["id"]); soft.discard(o["id"])
+        o["hard"], o["soft"] = hard, soft - hard
+
+
+def queue(o):
+    return "S" if o["eng"] == "A" else o["eng"]
+
+
+def order(ops):
+    n = len(ops)
+    succ = [[] for _ in ops]
+    for o in ops:
+        for j in o["hard"] | o["soft"]:
+            succ[j].append(o["id"])
+    lat = CFG["LAT"]
+    bl = [0.0] * n
+    for o in reversed(ops):
+        bl[o["id"]] = o["cost"] + o.get("lat", 0) + max([bl[k] + lat for k in succ[o["id"]]] + [0])
+    if CFG["plan"]:
+        top = max(bl)
+        for o in ops:
+            if "key" in o:
+                name, k = o["stage"], o["k"]
+                for (k0, t0, dt) in WHEN[name]:
+                    if k >= k0:
+                        bl[o["id"]] = top - 6000 - 30000 * o["t"] - 1000 * (t0 + dt * (k - k0))
+    for o in ops:
+        bl[o["id"]] += PRIO.get(o.get("key"), 0) + FIRST.get(o.get("stage", "") + o["eng"], 0)
+    left = [len(o["hard"] | o["soft"]) for o in ops]
+    ready = {q: [] for q in "VSPGY"}
+    est = [0.0] * n
+    for o in ops:
+        if left[o["id"]] == 0:
+            ready[queue(o)].append(o["id"])
+    free = {q: 0.0 for q in ready}
+    seq = []
+    while len(seq) < n:
+        best = None
+        for q, r in ready.items():
+            if r:
+                t0 = max(free[q], min(est[i] for i in r))
+                if best is None or t0 < best[0]:
+                    best = (t0, q)
+        t0, q = best
+        i = max((i for i in ready[q] if est[i] <= t0 + CFG["SLACK"]), key=lambda i: bl[i])
+        if est[i] > t0:
+            fit = [k for k in ready[q] if est[k] <= t0 and t0 + ops[k]["cost"] <= est[i] + CFG["TOL"]]
+            if fit:
+                i = max(fit, key=lambda k: bl[k])
+        ready[q].remove(i)
+        o = ops[i]
+        o["t0"] = max(free[q], est[i])
+        free[q] = o["t0"] + o["cost"]
+        o["t1"] = free[q] + o.get("lat", 0)
+        seq.append(i)
+        for k in succ[i]:
+            est[k] = max(est[k], o["t1"] + lat if i in ops[k]["hard"] else o["t0"])
+            left[k] -= 1
+            if left[k] == 0:
+                ready[queue(ops[k])].append(k)
+    return seq
+
+
+def plan():
+    ops = build()
+    depend(ops)
+    seq = order(ops)
+    pos = {q: 0 for q in "VSPG"}
+    known = {q: ({}, set()) for q in "VSPGY"}
+    for i in seq:
+        o = ops[i]
+        q = queue(o)
+        cnt, one = known[q]
+        waits = []
+        for j in sorted(o["hard"], key=lambda j: -ops[j]["t1"]):
+            x = ops[j]
+            if "lat" in x:
+                if j in one:
+                    continue
+                one.add(j)
+            else:
+                if cnt.get(x["eng"], -1) >= x["pos"]:
+                    continue
+                cnt[x["eng"]] = x["pos"]
+            waits.append(j)
+            x["need"] = True
+            if "rem" not in x:
+                for k, v in x["clock"][0].items():
+                    cnt[k] = max(cnt.get(k, -1), v)
+                one.update(x["clock"][1])
+        o["waits"] = waits
+        o["clock"] = (dict(cnt), set(one))
+        if "lat" not in o:
+            o["pos"] = pos[q]
+            pos[q] += 1
+    num = {q: 0 for q in "VSPG"}
+    nd = 0
+    for i in seq:
+        o = ops[i]
+        if "dma" in o:
+            o["sem"], o["val"] = "d%d" % nd, 16
+            nd += 1
+        elif "rem" in o:
+            o["sem"] = "r%d" % o["rem"]
+        elif o.get("need"):
+            num[o["eng"]] += 1
+            o["sem"], o["val"] = "c" + o["eng"], num[o["eng"]]
+    return ops, seq, num
+
+
+PLAN = []
+
+
+def rank_program(g, core, T, topo):
+    rank = T.rank_of(core)
+    if rank is None:
+        return
+    if not PLAN:
+        PLAN.append(plan())
+    ops, seq, num = PLAN[0]
+    n = len(T.cores)
+    nxt, prv = T.cores[(rank + 1) % n], T.cores[(rank - 1) % n]
+    rid, pid, _se = topo.addr(nxt)
+    mask = topo.mask(core, nxt)
+    out_n, in_n = len(topo.engines(core, nxt)), len(topo.engines(prv, core))
+    Q = {"V": g.vector, "S": g.scalar, "P": g.tensor, "G": g, "Y": g.sync}
+
+    def ap(a, ind=None):
+        if not isap(a):
+            return a
+        v = T[a[0]][a[4]:a[5], a[1]:a[2]:a[3]] if a[3] != 1 else T[a[0]][a[4]:a[5], a[1]:a[2]]
+        return v if ind is None else v.indirect(ap(ind))
+
+    sent = 0
+    for i in seq:
+        o = ops[i]
+        q = Q[queue(o)]
+        for j in o["waits"]:
+            x = ops[j]
+            q.wait_ge(T.sem[x["sem"]], in_n if "rem" in x else x["val"])
+        c = o["call"]
+        k = c[0]
+        if k == "copy":
+            r = q.tensor_copy(ap(c[1], c[4]), ap(c[2], c[3]))
+        elif k == "tt":
+            r = q.tensor_tensor(ap(c[1]), ap(c[2], c[5]), ap(c[3]), c[4])
+        elif k == "tts":
+            r = q.tensor_tensor(ap(c[1], c[5]), ap(c[2]), ap(c[3]), c[4])
+        elif k == "ts":
+            if c[6] is None:
+                r = q.tensor_scalar(ap(c[1]), ap(c[2], c[7]), ap(c[3]), None, c[5])
+            else:
+                r = q.tensor_scalar(ap(c[1]), ap(c[2], c[7]), ap(c[3]), ap(c[4]), c[5], c[6])
+        elif k == "scan":
+            r = q.tensor_tensor_scan(ap(c[1]), ap(c[2]), ap(c[3]), 0.0, ALU.max, ALU.max)
+        elif k == "memset":
+            r = q.memset(ap(c[1]), c[2])
+        elif k == "act":
+            kw = {}
+            if c[4] is not None:
+                kw["bias"] = ap(c[4])
+            if c[5] is not None:
+                kw["scale"] = ap(c[5])
+            if c[7] is not None:
+                kw["accum_out"] = ap(c[7])
+            r = q.activation(ap(c[1]), ap(c[2], c[6]), c[3], **kw)
+        elif k == "mm":
+            for m in c[1]:
+                r = q.matmul(ap(m[0]), ap(m[1]), ap(m[2]), m[3], m[4])
+        elif k == "iota":
+            if c[1][0] == "AI":
+                r = q.iota(ap(c[1]), c[2], c[3], c[4])
+            else:
+                r = q.iota(ap(c[1]), c[2], c[3], c[4], allow_small_or_imprecise_dtypes=True)
+        elif k == "dma":
+            whole = lambda a: T[a[0]][:] if a[0] in ("wt", "kap", "lim", "cnt") else ap(a)
+            r = q.dma_start(whole(c[1]), whole(c[2]))
+        else:
+            q.remote_dma(ap(c[1]), ap(c[2]), T.sem[o["sem"]], T.sem.ls, pid, rid, mask)
+            sent += out_n
+            continue
+        if "sem" in o:
+            r.then_inc(T.sem[o["sem"]], 16 if k == "dma" else 1)
+    g.wait_ge(T.sem.ls, sent)
+    for o in ops:
+        if "dma" in o and not o.get("need"):
+            g.wait_ge(T.sem[o["sem"]], 16)

@@ -1,38 +1,77 @@
+import numpy as np
 from concourse.mybir import AluOpType as ALU, ActivationFunctionType as ACT
 
 NV, W, ND = 5, 4096, 1024
 NP, QL, NA = 2, 128, 8
 POS = 16 * QL
 XW = 4672
-MAGIC = 25165824.0
+ROUND1 = 12582912.0
+ROUND4096 = 51539607552.0
 SLOT = 1088
 CFG = {
-    "c_path": ["VVSS", "VVSS"], "h_abs": ["SVSV", "SVSV"], "j_abs": ["SS", "SS"],
-    "ych": [[512] * 4, [512] * 4], "fz": "S", "fx": "P", "plan": False, "tile": True, "ext": True, "DB": 0.8,
-    "same_war": True, "SLACK": 300.0, "TOL": 60.0,
-    "G": 1.55, "F": 1.25, "PE": 0.42, "TT": 1.0, "LAT": 80.0, "OV": 50.0, "REM": 3200.0, "SC": 3.5,
+    "c": ["VVSS", "SSVV"], "h": ["RVRR", "RVRV"], "ych": [[512] * 4, [512] * 4], "hch": [[512] * 4, [512] * 4],
+    "split": [0, 1], "wrap": "D", "inv": "V", "last": ("a", "p", "w", "s", "rb", "xb", "eb"), "fuse": [0, 0], "tile": "SD", "SLACK": 200.0, "TOL": 60.0, "T": 25,
 }
-PRIO = {}
-FIRST = {'xbY': 3400, 'wS': 16700, 'mbS': -13700, 'caS': 6700, 'xaV': 3700, 'uaV': 2600, 'cbV': -1000, 'ybS': -1300, 'cbS': 2500, 'yaS': 1700, 'uaP': 13600, 'eaS': 300, 'wV': 3600, 'ebS': -19300, 'mbV': -1300, 'caV': 900, 'oV': -7100, 'wP': -46300, 'maS': -12100, 'caP': 10700, 'ebP': 17400, 'ebV': -1800, 'eaP': 1000, 'ybV': -8000, 'cbP': 16600, 'yaP': -1700, 'haV': -300, 'wA': 5300, 'xaY': -32000, 'wG': 8000, 'eaG': -3700, 'hbV': -1600, 'uaY': -7700, 'wY': -1000, 'ubY': -18000, 'ybP': -1500, 'xbV': 3100, 'ubV': -6000, 'ebG': -4400, 'ubP': -5300, 'eaV': -1000}
+MODELS = [
+    {"F": 1.1, "G": 1.55, "SC": 3.5, "OV": 0.0, "LAT": 150.0, "PE": 0.42, "TT": 1.0, "REM": 3400.0, "BW": 250.0, "W": 145},
+    {"F": 1.45, "G": 2.0, "SC": 4.5, "OV": 0.0, "LAT": 60.0, "PE": 0.42, "TT": 1.0, "REM": 3400.0, "BW": 200.0, "W": 185},
+    {"F": 1.05, "G": 1.1, "SC": 2.5, "OV": 0.0, "LAT": 200.0, "PE": 0.42, "TT": 1.0, "REM": 4200.0, "BW": 300.0, "W": 142},
+    {"F": 1.3, "G": 1.1, "SC": 4.0, "OV": 0.0, "LAT": 80.0, "PE": 0.5, "TT": 1.0, "REM": 4000.0, "BW": 200.0, "W": 120},
+]
 WHEN = {
-    "ua": [(0, -5, .1)], "ca": [(0, 1, 0), (1, -3, .1), (3, -1, .25)], "ub": [(0, 1, .1)], "cb": [(0, 2.5, .1), (4, 4, .3)],
-    "ma": [(0, 4.5, .1)], "ha": [(0, 7, .1)], "o": [(0, 7.5, .1)], "ya": [(0, 10, .18)], "mb": [(0, 9.5, .1)], "hb": [(0, 13, .1)],
-    "ea": [(0, 15, .1)], "yb": [(0, 16, .18)], "xa": [(0, 21, .1)], "eb": [(0, 22, .1)], "xb": [(0, 23, .1)],
-    "w": [(0, 22.5, .1), (4, 30.5, .15)],
+    "ua": -8, "na": 1, "ka": -1, "ca0": 0, "ca1": 0.8, "ca2": 0, "ca3": 0.8, "ma": -2, "ga": 12, "ha": 5,
+    "ub": 0.5, "nb": 4, "kb": 0.6, "cb0": 4, "cb1": 5, "cb2": 5.5, "cb3": 6.5, "mb": 5.2, "gb": 18, "hb": 9,
+    "o": 10, "i": 8, "fa": 6, "fb": 12,
+    "ya0": 6, "ya1": 7, "ya2": 8, "ya3": 9, "ja0": 7.5, "ja1": 8.5, "ja2": 9.5, "ja3": 10.5,
+    "da0": 7.2, "da1": 8.2, "da2": 9.2, "da3": 10.2, "ea": 8,
+    "yb0": 12, "yb1": 13, "yb2": 14, "yb3": 15, "jb0": 13.5, "jb1": 14.5, "jb2": 15.5, "jb3": 16.5,
+    "db0": 13.2, "db1": 14.2, "db2": 15.2, "db3": 16.2, "eb": 14,
+    "xa": 21, "xb": 20, "a": 20.5, "w": 25.5, "s": 28, "za": 22, "zb": 22, "va": 20, "vb": 23,
 }
+WHEN.update({'ua': -6.3, 'na': 6.0, 'ka': -0.4, 'ca0': -2.1, 'ca1': -0.5, 'ca2': -3.9, 'ca3': 6.5, 'ma': -2.1, 'ga': -1.0, 'ha': 6.2, 'ub': 0.9, 'nb': 6.8, 'kb': -6.6, 'cb0': 8.1, 'cb1': 0.4, 'cb2': 3.7, 'cb3': 6.3, 'mb': 4.0, 'gb': 36.6, 'hb': 10.6, 'o': 11.4, 'i': 11.2, 'fa': 7.9, 'fb': 15.9, 'ya0': 6.6, 'ya1': -6.8, 'ya2': 4.9, 'ya3': 16.2, 'ja0': 11.6, 'ja1': 7.0, 'ja2': 4.4, 'ja3': 18.8, 'da0': 14.0, 'da1': 8.7, 'da2': 6.1, 'da3': 13.9, 'ea': -0.1, 'yb0': 17.2, 'yb1': 7.1, 'yb2': 16.5, 'yb3': 17.3, 'jb0': 19.5, 'jb1': 2.9, 'jb2': 21.1, 'jb3': 19.7, 'db0': 8.2, 'db1': 16.6, 'db2': -7.2, 'db3': 22.0, 'eb': 12.5, 'xa': 36.6, 'xb': 2.0, 'a': 23.3, 'w': 24.3, 's': 27.9, 'da0.1': 6.8, 'ca3.4': -6.2, 'ca3.2': -2.9, 'xa.1': -2.3, 'da1.0': -1.1, 'ub.8': -1.5, 'da0.0': -3.7, 'mb.2': -4.0, 'da0.3': 3.7, 'fb.0': 1.4, 'mb.11': 5.3, 'w.1': 2.9, 'w.7': -0.2, 'yb3.0': 1.8, 'ya1.0': 2.8, 'w.3': -1.0, 'ma.3': 1.2, 'ca1.0': -6.9, 'da1.3': 5.2, 'i.0': -3.8, 'ja1.0': 2.8, 's.5': -2.1, 'mb.13': -4.3, 'cb2.0': 1.0, 'mb.3': 0.7, 'ca3.1': -6.5, 'db3.2': 0.1, 'ua.7': 7.4, 'fb.1': -1.5, 'ma.1': 3.5, 'jb3.0': 2.7, 'mb.7': 4.7, 'hb.2': -5.0, 'mb.5': 2.5, 'w.8': -6.4, 'ma.2': 4.1, 'ua.4': -3.9, 'ja2.2': 10.2, 'ea.6': -5.7, 'db3.3': 7.4, 'xb.1': 5.0, 'o.1': 1.7, 'ca3.3': 0.0, 'jb1.1': 0.3, 'na.2': 1.7, 'db1.1': 6.6, 'ma.7': -4.0, 'ma.11': -1.9, 'ja0.0': 2.6, 'w.9': 2.8, 'ca2.1': 2.2, 'ha.0': -4.3, 'w.0': -2.4, 'cb3.0': -4.2, 'ca1.2': 6.9, 'ma.6': 0.0, 'da2.2': -0.1, 'da0.2': -0.2, 'ja2.0': 0.5, 'da3.0': -2.8, 'da1.1': -3.1, 'w.5': 2.0, 'da2.1': -4.8, 'eb.2': -6.6, 'jb0.0': 3.9, 'ca1.4': -8.3, 'w.6': 6.5, 'fa.1': -6.3, 'da1.2': 1.8, 'db2.1': -7.0, 'a.2': 1.0, 'cb3.3': -3.2, 'na.0': 3.9, 'o.2': 4.5, 'yb0.0': -2.1, 'ub.6': 3.6, 'fa.0': 0.3, 'ka.0': -0.8, 'da2.0': -1.1, 'ma.8': -1.9, 'ca2.0': -0.3, 'cb1.1': -1.2, 'nb.1': 2.5, 'ha.2': 0.5, 'ma.4': -5.0, 'ja2.1': -1.3, 'ea.4': -0.1, 'a.0': 2.9, 'ua.0': 1.9, 'mb.6': 4.7, 'ca0.1': -2.5, 'ca2.2': 0.9, 'jb0.2': 3.9, 'ea.2': 1.9, 'ca1.3': 0.3, 'db1.2': -1.9, 'cb0.1': -3.3, 'ja0.2': -2.9, 'w.13': -2.6, 'ma.12': -4.4, 'eb.4': -3.6, 'ja3.1': -1.6, 'ua.5': 0.4, 'w.10': -5.4, 'db0.3': -2.1, 'na.1': -1.1, 'ja0.1': 0.3, 'ua.1': 3.9, 'cb3.2': -1.6, 'ua.6': -1.5, 'db1.3': 3.1, 'eb.3': -3.1, 'ea.7': 6.5, 'jb2.2': 4.8, 'eb.5': -1.7, 'ca1.1': 0.1, 'ub.5': -4.8, 'jb0.1': 0.8, 'ub.0': -3.1, 'ub.3': 3.3, 'eb.0': -2.7, 'ea.1': 1.3, 'w.14': 0.6, 'db3.1': 6.4, 'xa.0': 1.3, 'ya2.0': -4.6, 'ea.9': 1.8, 'ea.5': -2.5, 'ma.9': -1.0, 'ub.2': 7.5, 'mb.0': 2.0, 'eb.6': 0.7, 'db3.0': 3.0, 'ya3.0': -0.6, 'nb.2': 1.0, 'ea.8': 1.5, 'ja3.0': -4.9, 's.6': 2.2, 'cb1.3': 3.8, 'xb.0': -1.1, 'mb.1': -1.5, 'ga.0': 0.1, 'ea.0': 3.7, 'kb.0': 0.9, 'ub.7': 0.7, 'db2.2': 0.4, 'w.4': 4.2, 'jb1.0': 0.5, 'ma.0': 3.5, 'o.0': -0.7, 'ma.13': 4.2, 'ja3.2': -1.2, 'a.1': 0.4, 'hb.0': -1.3, 'eb.1': 2.9, 's.1': -3.6, 'cb0.0': -5.2, 'ca0.0': 0.0, 'ca3.0': -2.5, 'ub.1': -0.7, 's.4': -6.1, 'ua.8': 1.1, 'ha.1': -1.2, 'a.3': -2.1, 'da2.3': -1.7, 'db1.0': -0.5, 'ub.4': 0.6, 'yb1.0': 1.6, 's.0': -0.8, 'cb3.1': -2.2, 'cb3.4': 1.2, 'da3.2': 1.0, 'ya0.0': 2.7, 'mb.10': -2.5, 'ea.3': -3.2, 'jb2.0': 1.2, 'ja1.1': 0.3, 'jb2.1': 0.1, 'ma.5': -3.3, 's.3': -0.1, 'mb.4': 1.0, 'ua.3': 1.1, 'eb.7': 1.8, 'db2.0': -0.7, 's.2': 2.8, 'db0.0': -0.6, 'jb1.2': -1.6, 'o.3': 1.6, 'gb.0': -1.9, 'cb2.1': -1.2})
 
+ORDER = """
+V ua.2 rb.0- ma.0 ua.3 w.4- ua.4 rb.1- ua.5 xb.0- ka.0 w.5- w.10- ca0.0 ca1.0 ca0.2 ca1.2 s.0- ub.1 ub.2 na.1 ub.3 ub.4 qa1.2 ub.5 ma.2 kb.0 ma.3 ma.4 ma.1 ma.5 ma.6 ma.7 nb.1 ma.9 ma.8 cb2.0 ma.10 cb3.0 ma.12 ha.0 ma.13 mb.0 ma.14 ha.1 cb3.2 ha.2 i.0 mb.1 da0.0 qb1.2 mb.2 mb.3 o.1 mb.4 mb.5 da1.0 mb.6 da0.2 mb.7 hb.0 mb.8 mb.9 hb.1 mb.10 da2.0 mb.12 o.0 mb.13 mb.14 da3.0 da2.2 hb.2 da3.2 db0.0 ea.0 o.2 ea.1 ea.2 o.3 ea.3 db1.0 ra.0 db2.0 db0.2 o.4 db2.2 db3.0 ea.7 xa.0 eb.0 eb.1 eb.2 a.0 eb.3 a.1 w.1 w.0 eb.7 w.2 ua.1+ w.3
+S cb1.2 cb2.2 ya0.0 qb0.2 ya1.0 ya2.0 ja0.1 ya3.0 ja2.1 ja1.1 mb.11 da1.2 ja3.1 yb0.0 yb1.0 yb2.0 ga.0 jb0.1 ea.5 jb1.1 yb3.0 gb.0 db1.2 jb2.1 jb3.1 db3.2 eb.5 a.3 w.7 w.8 ca2.0+ ca3.0+ w.12 w.13 ca2.2+ ca3.2+ qa0.2+ cb0.0+ cb1.0+ cb0.2+ ma.11+
+P fb.0 qb1.0 qb0.1 qb1.1 ja0.0 nb.2 da0.1 ja2.0 ja1.0 fa.1 ja0.2 ja3.0 ja2.2 ja1.2 da0.3 da1.3 da2.1 ja3.2 da3.1 da2.3 da3.3 jb0.0 jb1.0 ea.4 fb.1 ea.6 jb0.2 db0.1 jb1.2 jb2.0 jb3.0 db2.1 db1.3 db0.3 db2.3 jb2.2 jb3.2 db3.3 eb.4 ua.0+ a.2 eb.6 w.6 na.0+ w.9 w.11 ca2.1+ ca3.1+ qa0.0+ ub.0+ qa0.1+ qa1.1+ fa.0+ na.2+ nb.0+ cb0.1+ cb1.1+
+G w.14- ra.2 rb.2
+Y tb.2 tb.0 tb.1 xa.1 ta.2+ ta.1+ ta.0+
+"""
+ORDER = """
+V ca1.0 ca0.0 ca1.2 ca0.2 s.0- ub.1 na.1 ub.2 ma.0 ub.3 ub.4 qa1.2 ub.5 ma.2 kb.0 ma.3 ma.4 nb.1 ma.5 ma.1 ma.6 cb2.0 ma.7 mb.0 ma.9 ma.8 ma.10 cb3.0 ma.12 ha.0 ma.13 o.1 ma.14 ha.1 cb3.2 ha.2 i.0 da0.0 qb1.2 mb.1 mb.2 mb.3 hb.0 mb.4 da0.2 mb.5 mb.6 da1.0 mb.7 hb.1 mb.9 mb.8 hb.2 mb.10 da2.0 mb.12 mb.13 mb.14 da3.0 da2.2 da3.2 db0.0 o.0 ea.0 ea.1 ea.2 ea.3 o.2 db1.0 ra.0 db0.2 db2.0 db3.0 o.3 db2.2 o.4 xa.0 ea.7 eb.0 eb.1 eb.2 eb.3 a.0 eb.7 w.1 w.0 a.1 w.4 ua.1+ w.2 rb.0 ua.2+ w.3 ua.3+ rb.1 ua.4+ w.5 ua.5+ xb.0 ka.0+ w.10
+S qb0.2 ya1.0 ya2.0 ja0.1 ya3.0 ja2.1 ja1.1 mb.11 da1.2 ga.0 ja3.1 yb0.0 yb2.0 yb1.0 jb0.1 ea.5 jb1.1 yb3.0 db1.2 jb2.1 gb.0 jb3.1 db3.2 eb.5 w.7 a.3 w.8 ca2.0+ ca3.0+ w.12 w.13 ca3.2+ ca2.2+ qa0.2+ cb0.0+ cb1.0+ cb0.2+ ma.11+ cb1.2+ cb2.2+ ya0.0+
+P cb1.1 fa.0 qb1.0 qb0.1 qb1.1 fa.1 ja0.0 da0.1 ja2.0 ja1.0 ja0.2 da0.3 ja2.2 ja3.0 da2.1 da1.3 ja1.2 ja3.2 da3.1 da2.3 da3.3 jb0.0 ea.4 jb1.0 fb.1 ea.6 jb2.0 db0.1 db0.3 jb0.2 jb3.0 db2.1 db1.3 jb2.2 jb1.2 db2.3 jb3.2 db3.3 eb.4 ua.0+ eb.6 w.6 a.2 w.9 na.0+ w.11 ca2.1+ ca3.1+ qa0.0+ ub.0+ qa0.1+ qa1.1+ nb.0+ na.2+ fb.0+ nb.2+ cb0.1+
+G ra.2 rb.2 w.14
+Y xa.1- ta.0 ta.1 ta.2 tb.2 tb.1 tb.0
+"""
+ORDER = """
+V ub.1 na.1 ub.2 ma.0 ub.3 ma.1 ub.4 qa1.2 ub.5 ma.2 kb.0 ma.3 ma.4 nb.1 ma.5 cb2.0 ma.6 ma.7 ma.9 ma.8 ma.10 cb3.0 ma.12 mb.0 ma.13 cb3.2 ma.14 ha.0 o.1 i.0 ha.1 hb.0 ha.2 qb1.2 mb.1 mb.2 da0.0 mb.3 mb.4 o.0 mb.5 da0.2 mb.6 o.2 mb.7 mb.9 mb.8 da1.0 mb.10 da2.0 mb.12 da2.2 mb.13 hb.1 mb.14 da3.0 hb.2 da3.2 db0.0 ea.0 ea.1 db1.0 o.3 ra.0 db0.2 db2.0 db3.0 db2.2 xa.0 o.4 eb.0 eb.1 a.0 a.1 w.1 w.0 a.2 w.2 rb.1 rb.0 w.3 p.0 xb.0 ua.1+ ua.2+ w.4 ua.3+ ua.4+ w.5 ua.5+ ka.0+ w.10 ca0.0+ ca1.0+ ca0.2+ ca1.2+ s.0
+S eb.3 a.4 w.7 w.8 ca2.0+ ca3.0+ w.12 w.13 ca2.2+ ca3.2+ qa0.2+ cb0.0+ cb1.0+ cb0.2+ ma.11+ cb1.2+ ga.0+ cb2.2+ ya0.0+ qb0.2+ ya1.0+ ja0.1+ ya2.0+ ja1.1+ ya3.0+ mb.11+ da1.2+ ja2.1+ ja3.1+ yb0.0+ yb1.0+ yb2.0+ jb0.1+ ea.3+ jb1.1+ yb3.0+ jb2.1+ gb.0+ db1.2+ jb3.1+ db3.2+
+P fa.0 qb1.0 qb0.1 qb1.1 fa.1 ja0.0 ja1.0 da0.3 ja2.0 da0.1 ja0.2 ja1.2 ja3.0 da2.1 da2.3 da1.3 ja2.2 fb.1 ja3.2 da3.1 da3.3 jb0.0 jb1.0 ea.2 jb0.2 ea.4 jb2.0 jb1.2 db0.1 jb3.0 db2.1 db0.3 jb2.2 db1.3 db2.3 jb3.2 db3.3 eb.2 eb.4 ua.0+ a.3 w.6 w.9 na.0+ w.11 ca2.1+ ca3.1+ qa0.0+ ub.0+ qa0.1+ qa1.1+ nb.0+ fb.0+ na.2+ nb.2+ cb0.1+ cb1.1+
+G w.14- ra.2 rb.2
+Y tb.0 tb.2 tb.1 xa.1 ta.0+ ta.2+ ta.1+
+"""
+ORDER = """
+V ub.5 kb.0 qa1.2 ma.2 ma.3 ma.4 ma.5 ma.6 nb.1 ma.7 mb.0 ma.8 ma.9 ma.10 cb3.0 cb2.0 ma.12 hb.0 ma.13 ha.0 ma.14 ha.1 i.0 qb1.2 ha.2 mb.2 o.1 mb.1 mb.3 da0.0 mb.4 mb.5 o.0 o.4 mb.6 da0.2 mb.7 da1.0 mb.8 mb.9 hb.1 mb.10 da2.0 mb.12 o.2 mb.13 da2.2 mb.14 da3.0 hb.2 da3.2 db0.0 ea.0 o.3 ea.1 db0.2 db2.0 ra.0 db1.0 db2.2 db3.0 xa.0 eb.0 eb.1 a.0 a.1 a.2 w.0 w.1 p.0 w.2 rb.0 rb.1 w.3 xb.0 ua.1+ ua.2+ ua.3+ ua.4+ ua.5+ ma.0+ ka.0+ w.10 ca0.0+ na.1+ w.4 ca1.0+ w.5 s.0 ub.1+ ma.1+ ub.2+ ub.3+ ub.4+
+S eb.3 ta.0+ w.7 a.4 w.8 ta.1+ ca2.0+ ca3.0+ w.12 ca0.2+ w.13 ca1.2+ ca3.2+ ca2.2+ qa0.2+ cb0.0+ cb1.0+ cb0.2+ ma.11+ cb1.2+ cb3.2+ cb2.2+ qb0.2+ ya0.0+ ya1.0+ ya2.0+ ja0.1+ ya3.0+ ja2.1+ mb.11+ ja1.1+ da1.2+ ja3.1+ yb0.0+ yb1.0+ yb2.0+ ga.0+ ea.3+ jb1.1+ jb0.1+ yb3.0+ gb.0+ db1.2+ jb2.1+ jb3.1+ db3.2+
+P qa1.1 cb0.1 cb1.1 nb.2 na.2 fa.0 fb.0 qb0.1 qb1.1 fb.1 ja0.0 ja1.0 fa.1 da0.1 ja2.0 da0.3 ja0.2 ja3.0 da2.1 ja1.2 ja2.2 da2.3 da1.3 ja3.2 da3.1 da3.3 jb1.0 jb0.0 ea.2 ea.4 db0.3 jb1.2 db2.1 jb2.0 jb3.0 db0.1 db2.3 jb0.2 jb2.2 db1.3 jb3.2 db3.3 eb.2 eb.4 ua.0+ a.3 w.6 w.9 na.0+ w.11 ca2.1+ ca3.1+ ub.0+ qa0.1+ nb.0+
+G ra.2 rb.2 w.14
+Y tb.1- xa.1- tb.2 tb.0
+"""
 SCRATCH = {
     "XS": ("sbuf", [128, W + POS], "bfloat16"), "DL": ("sbuf", [128, 2 * ND], "bfloat16"),
     "ST": ("sbuf", [128, NV * SLOT], "bfloat16"),
-    "AB": ("sbuf", [128, 46000], "bfloat16"), "AF": ("sbuf", [128, 7000], "float32"),
+    "AB": ("sbuf", [128, 50000], "bfloat16"), "AF": ("sbuf", [128, 5000], "float32"),
     "AI": ("sbuf", [128, 4000], "int32"), "AU": ("sbuf", [128, 1500], "uint16"),
-    "PJH": ("psum", [128, 1024], "float32"), "PD0": ("psum", [128, 512], "float32"),
-    "PD1": ("psum", [128, 512], "float32"), "PK": ("psum", [128, 512], "float32"),
+    "AK": ("sbuf", [128, 2 * QL, 16], "bfloat16"),
+    "PJH": ("psum", [128, 1024], "float32"), "PD0": ("psum", [128, 32, 16], "float32"),
+    "PD1": ("psum", [128, 32, 16], "float32"), "PK0": ("psum", [128, 512], "float32"),
     "PU": ("psum", [128, 512], "float32"), "PW": ("psum", [128, 512], "float32"),
-    "PL": ("psum", [128, 512], "float32"),
+    "PK1": ("psum", [128, 512], "float32"),
 }
+AB = "ab"
 SEMAPHORES = ["cV", "cS", "cP", "cG", "ls"] + ["d%d" % i for i in range(70)] + ["r%d" % i for i in range(16)]
-BYTES = {"XS": 2, "DL": 2, "ST": 2, "AB": 2, "AF": 4, "AI": 4, "AU": 2}
+BYTES = {"AK": 2, "XS": 2, "DL": 2, "ST": 2, "AB": 2, "AF": 4, "AI": 4, "AU": 2}
 
 
 def A(name, c0, c1, step=1, p0=0, p1=128):
@@ -43,18 +82,42 @@ def sl(a, i, j, step=1, p0=None, p1=None):
     return (a[0], a[1] + i, a[1] + j, step, a[4] if p0 is None else p0, a[5] if p1 is None else p1)
 
 
+def rows(a, k0, k1):
+    return a[:6] + ((k0, k1),)
+
+
 def width(a):
-    return (a[2] - a[1] + a[3] - 1) // a[3]
+    n = (a[2] - a[1] + a[3] - 1) // a[3]
+    return n if len(a) == 6 else n // 16 * (a[6][1] - a[6][0])
 
 
 def isap(a):
     return isinstance(a, tuple)
 
 
+def price(o, m):
+    k, n = o["size"]
+    c = 0.83 * m["F"]
+    if k == "v":
+        return m["OV"] + max(64, n) * c, 0
+    if k == "t":
+        return m["OV"] + max(64, n * m["TT"]) * c, 0
+    if k == "g":
+        return (50 if o["eng"] == "V" else 65) + n * m["G"] * c, 0
+    if k == "s":
+        return 50 + n * m["SC"] * c, 0
+    if k == "p":
+        return 30 + n * m["PE"] * m["F"], 0
+    if k == "i":
+        return 130 + 2 * n * c, 0
+    if k == "d":
+        return 60, 2000 + n / m["BW"]
+    return 900, m["REM"] + n
+
+
 def build():
-    ops = []
+    ops, now = [], ["init", 0]
     top = {"AB": 0, "AF": 0, "AI": 0, "AU": 0}
-    F, G = CFG["F"], CFG["G"]
 
     def al(name, n):
         c = top[name]
@@ -62,62 +125,61 @@ def build():
         assert top[name] <= SCRATCH[name][1][1], name
         return A(name, c, c + n)
 
-    def op(eng, cost, call, rd, wr, **kw):
-        o = {"eng": eng, "cost": cost, "call": call, "rd": [r for r in rd if isap(r)], "wr": wr, "id": len(ops)}
+    def op(eng, size, call, rd, wr, **kw):
+        o = {"eng": eng, "size": size, "call": call, "rd": [r for r in rd if isap(r)], "wr": wr, "id": len(ops)}
         o.update(kw)
+        o["tag"], o["nth"] = now[0], now[1]
+        now[1] += 1
         ops.append(o)
         return o
+
+    def at(tag):
+        now[0], now[1] = tag, 0
 
     def two(*aps):
         return all(BYTES.get(a[0], 4) == 2 for a in aps if isap(a))
 
-    def vc(n, c):
-        return CFG["OV"] + max(64, n * c) * 0.83 * F
-
-    def gc_(n):
-        return 50 + n * G * 0.83 * F
-
     def copy(out, in_, ind=None, sc=None):
         if ind is not None:
-            return op("V", gc_(width(out)), ("copy", out, in_, ind, None), [in_, ind], [out])
+            return op("V", ("g", width(out)), ("copy", out, in_, ind, None), [in_, ind], [out])
         if sc is not None:
-            return op("V", 50 + width(in_) * CFG["SC"] * 0.83 * F, ("copy", out, in_, None, sc), [in_, sc], [out])
-        return op("V", vc(width(out), 0.5 if two(out, in_) else 1), ("copy", out, in_, None, None), [in_], [out])
+            return op("V", ("s", width(in_)), ("copy", out, in_, None, sc), [in_, sc], [out])
+        return op("V", ("v", width(out) * (0.5 if two(out, in_) else 1)), ("copy", out, in_, None, None), [in_], [out])
 
     def tt(out, a, b, o, ind=None):
         if ind is not None:
-            c = gc_(width(out))
+            c = ("g", width(out))
         elif a[0][0] == "P" or b[0][0] == "P":
-            c = vc(width(out), 1)
+            c = ("v", width(out))
         else:
-            c = vc(width(out), CFG["TT"] if two(out, a, b) else 2)
+            c = ("t", width(out)) if two(out, a, b) else ("v", 2 * width(out))
         return op("V", c, ("tt", out, a, b, o, ind), [a, b, ind], [out])
 
     def ts(out, a, s1, s2, o0, o1=None, ind=None):
-        c = gc_(width(out)) if ind is not None else vc(width(out), 0.5 if two(out, a) else 1)
+        c = ("g", width(out)) if ind is not None else ("v", width(out) * (0.5 if two(out, a) else 1))
         return op("V", c, ("ts", out, a, s1, s2, o0, o1, ind), [a, s1, s2, ind], [out])
 
     def act(out, a, f, bias=None, scale=None, ind=None, acc=None):
-        c = (65 + width(out) * G * 0.83 * F) if ind is not None else vc(width(out), 1)
+        c = ("g" if ind is not None else "v", width(out))
         return op("S", c, ("act", out, a, f, bias, scale, ind, acc), [a, bias, scale, ind], [out] + ([acc] if acc else []))
 
     def mm(lst, **kw):
-        c = sum(max(min(64, width(m[1])), width(m[2])) * (4 if m[1][0] == "AF" else 1) for m in lst) * CFG["PE"] * F + 30
-        return op("P", c, ("mm", lst), [m[1] for m in lst] + [m[2] for m in lst], [m[0] for m in lst], **kw)
+        c = sum(max(min(64, width(m[1])), width(m[2])) * (4 if m[1][0] == "AF" else 1) for m in lst)
+        return op("P", ("p", c), ("mm", lst), [m[1] for m in lst] + [m[2] for m in lst], [m[0] for m in lst], **kw)
 
     def iota(out, pat, base=0, cm=0):
-        return op("G", 130 + 2 * width(out) * 0.83 * F, ("iota", out, pat, base, cm), [], [out])
+        return op("G", ("i", width(out)), ("iota", out, pat, base, cm), [], [out])
 
     def memset(out, v):
-        return op("V", vc(width(out), 0.5), ("memset", out, v), [], [out])
+        return op("V", ("v", width(out) * 0.5), ("memset", out, v), [], [out])
 
     def dma(q, out, in_, nbytes):
         rd = [in_] if in_[0] in SCRATCH else []
         wr = [out] if out[0] in SCRATCH else []
-        return op(q, 60, ("dma", out, in_), rd, wr, lat=2000 + nbytes / 250.0, dma=True)
+        return op(q, ("d", nbytes), ("dma", out, in_), rd, wr, dma=True, far=True)
 
     add, sub, mul, mx, mn = ALU.add, ALU.subtract, ALU.mult, ALU.max, ALU.min
-    band, shr = ALU.bitwise_and, ALU.logical_shift_right
+    band, shr, eq = ALU.bitwise_and, ALU.logical_shift_right, ALU.is_equal
     ID = ACT.Identity
 
     def slot(t):
@@ -126,20 +188,21 @@ def build():
     def part(a, p, n=QL):
         return sl(a, n * p, n * p + n)
 
-    ZL = [al("AB", NP * QL) for t in range(NV)]
-    ZN = [al("AB", NP * QL) for t in range(NV)]
+    ZT = [[al("AB", 4 * QL) for p in range(NP)] for t in range(NV)]
+    ZX = [[al("AB", 2 * QL) for p in range(NP)] for t in range(NV)]
 
     wti, kpi, lmi, cni = al("AI", 1), al("AI", 1), al("AI", 2), al("AI", 256)
     dma("Y", wti, A("wt", 0, 1), 0)
-    dma("Y", ZL[0], A("zed", 0, 256), 65536)
+    dma("A", part(ZT[0][0], 0), A("zed", 0, QL), 32768)
     dma("A", kpi, A("kap", 0, 1), 0)
     dma("Y", A("XS", 0, W), A("stock", 0, W), 1 << 20)
-    dma("A", sl(lmi, 0, 2, 1, 0, 8), A("lim", 0, 2, 1, 0, 8), 0)
-    dma("A", sl(cni, 0, 256, 1, 0, 8), A("cnt", 0, 256, 1, 0, 8), 0)
-    dma("Y", A("DL", 0, ND), A("donor", 0, ND), 1 << 20)
-    dma("Y", A("XS", W, XW), A("stock", 0, XW - W), 1 << 20)
-    dma("Y", sl(slot(0), 304, 560), A("rend", 0, 256), 1 << 20)
-    dma("Y", sl(slot(0), 48, 304), A("lend", 0, 256), 1 << 20)
+    dma("A", part(ZT[0][1], 0), A("zed", QL, 2 * QL), 1 << 20)
+    dma("A", sl(lmi, 0, 2, 1, 0, 8), A("lim", 0, 2, 1, 0, 8), 1 << 20)
+    dma("A", sl(cni, 0, 256, 1, 0, 8), A("cnt", 0, 256, 1, 0, 8), 1 << 20)
+    dma("Y", A("DL", 0, ND), A("donor", 0, ND), 5 << 18)
+    dma("Y", A("XS", W, XW), A("stock", 0, XW - W), 6 << 18)
+    dma("Y", sl(slot(0), 304, 560), A("rend", 0, 256), 6 << 18)
+    dma("Y", sl(slot(0), 48, 304), A("lend", 0, 256), 6 << 18)
 
     PI, t1, t2, t3, t4 = [al("AI", 1) for _ in range(5)]
     XI, X16, X8 = al("AF", 144), al("AF", 128), al("AF", 128)
@@ -155,11 +218,11 @@ def build():
     copy(Pf, PI); copy(wf, wti); copy(kf, kpi)
     BO, WBO, I1, NI, HI, BIGI, ON = [al("AB", 128) for _ in range(7)]
     M1, MW, MP, MN, M2P, M2N = [al("AB", 144) for _ in range(6)]
-    ts(M1, XI, G16, 15.0, sub, ALU.is_equal)
+    ts(M1, XI, G16, 15.0, sub, eq)
     ts(MW, M1, wf, None, mul)
-    ts(WBO, X16, G16, wf, ALU.is_equal, mul)
-    ts(BO, X16, G16, None, ALU.is_equal)
-    ts(I1, sl(XI, 0, 128), Pf, None, ALU.is_equal)
+    ts(WBO, X16, G16, wf, eq, mul)
+    ts(BO, X16, G16, None, eq)
+    ts(I1, sl(XI, 0, 128), Pf, None, eq)
     act(NI, I1, ID, scale=-1.0)
     act(MP, M1, ID, scale=4096.0); act(MN, M1, ID, scale=-4096.0)
     act(M2P, M1, ID, scale=8192.0); act(M2N, M1, ID, scale=-8192.0)
@@ -169,33 +232,45 @@ def build():
     def win(M, b):
         return sl(M, 15 - b, 143 - b)
 
-    PM256, B128, K37, R8, TC, P16, PL2, CM, CH, CN = [al("AF", 1) for _ in range(10)]
-    ts(PM256, PM, 256.0, None, mul); ts(B128, PM, 128.0, None, mul); ts(K37, PM, 37.0, None, mul)
+    PM256, B128, K37, R8, TC, P16, PL2, NK0, PN256 = [al("AF", 1) for _ in range(9)]
+    ts(PM256, PM, 256.0, None, mul); ts(B128, PM, 128.0, 256.0, mul, add); ts(K37, PM, 37.0, None, mul)
     ts(R8, PM, -8.0, -6.5, mul, add); ts(TC, P7, 16.0, P3, mul, add); ts(P16, Pf, 16.0, None, mul)
     ts(PL2, PM, 2.0, None, ALU.is_lt)
-    memset(CM, MAGIC); memset(CH, -0.5); memset(CN, -MAGIC / 2)
-    kx, km, KAP = al("AB", 128), al("AB", 128), al("AF", 128)
-    ts(kx, X8, PM256, kf, ALU.is_equal, mul)
-    ts(km, X8, PM256, PM256, ALU.is_equal, mul)
-    mm([(A("PK", 0, 128), BO, kx, True, True)])
-    act(KAP, A("PK", 0, 128), ID)
+    ts(PN256, PM, 256.0, -256.0, mul, add)
+    kx, km, kw, KM, K32 = al("AB", 128), al("AB", 128), al("AB", 128), al("AB", 128), al("AF", 128)
+    ts(kx, X8, PM256, kf, eq, mul)
+    mm([(A("PK1", 0, 128), BO, kx, True, True)])
+    act(K32, A("PK1", 0, 128), ID, scale=32.0)
+    act(NK0, A("PK1", 0, 1), ID, scale=-1.0)
     REP8, REPA, TAU = al("AU", 8), al("AU", 16), al("AU", 8)
     ts(REP8, sl(XI, 0, 8), 0.0, P7, mul, add)
     ts(TAU, sl(XI, 0, 8), 2.0, TC, mul, add)
     copy(REPA, sl(XI, 0, 16))
-    K12, C12, CE, SK = al("AF", 256), al("AF", 256), al("AF", 8), al("AF", 8)
+    K12, CODE, SK, SC = al("AF", 256), al("AF", 256), al("AF", 16), al("AF", 512)
     iota(K12, [[0, 16], [8, 16]])
-    iota(C12, [[-6, 2], [128, 8], [-8, 16]], 134)
-    RC, K0 = al("AB", 256), al("AB", 128)
-    ts(K0, sl(K12, 0, 128), 0.0, None, ALU.is_equal)
-    ts(part(RC, 0), K0, PL2, None, mx); memset(part(RC, 1), 0.0)
-    memset(sl(K12, 0, 256, 16), 999.0)
-    ts(sl(C12, 0, 128, 16), sl(C12, 0, 128, 16), -127.0, None, add)
-    ts(CE, sl(XI, 0, 8), 256.0, 128.0, mul, add); ts(SK, sl(XI, 0, 8), 128.0, 134.0, mul, add)
+    iota(CODE, [[-8, 128], [-6, 2]], 2054)
+    iota(SK, [[0, 2], [-128, 8]], 2054)
+    RC, K0, P2, P34 = al("AB", 256), al("AB", 128), al("AF", 1), al("AF", 1)
+    ts(P2, PM, 2.0, None, eq); ts(P34, PM, 3.0, None, ALU.is_ge)
+    ts(K0, sl(K12, 0, 128), 0.0, P2, eq, mul)
+    ts(sl(RC, 1, 256, 2), K0, 0.0, P34, mul, add)
+    ts(sl(RC, 0, 256, 2), K0, PL2, None, mx)
+    memset(sl(K12, 0, 256, 16), 260.0)
+    KR = al("AB", 256)
+    act(KR, K12, ID, bias=4.0, scale=-1.0)
+    ts(sl(CODE, 0, 256, 32), sl(CODE, 0, 256, 32), 1.0, None, add)
     PB, BB = al("AF", 16), al("AB", 2048)
-    ts(PB, sl(XI, 0, 16), PM, None, ALU.is_equal)
+    ts(PB, sl(XI, 0, 16), PM, None, eq)
     for b in range(16):
         act(sl(BB, 128 * b, 128 * b + 128), BO, ID, scale=sl(PB, b, b + 1))
+    P0K = al("AF", 1)
+    ts(km, X8, PN256, PN256, eq, mul)
+    ts(P0K, sl(PB, 0, 1), 3840.0, None, mul)
+    ts(kw, X8, 3840.0, P0K, eq, mul)
+    tt(KM, kx, km, add); tt(KM, KM, kw, add)
+    c0, c1, CQ = al("AF", 1), al("AF", 1), al("AB", 128)
+    ts(c0, sl(PB, 0, 1), -2048.0, None, mul); ts(c1, sl(PB, 1, 2), 32.0, c0, mul, add)
+    ts(c0, sl(PB, 2, 3), -31.5, c1, mul, add); ts(CQ, X16, 0.0, c0, mul, add)
     BASE, FL, CXD = al("AF", 64), al("AB", 48), al("AF", 32)
     LANE = sl(BASE, 32, 48)
     ts(LANE, sl(XI, 0, 16), 16.0, PM, mul, add)
@@ -205,250 +280,278 @@ def build():
     lmf, E8, M8, n8r = al("AF", 2), al("AF", 128), al("AB", 144), al("AB", 256)
     r8 = lambda a: sl(a, 0, width(a), 1, 0, 8)
     copy(r8(lmf), r8(lmi))
-    ts(r8(E8), r8(X16), r8(P16), None, ALU.is_equal)
-    ts(r8(M8), r8(XI), r8(P16), 15.0, sub, ALU.is_equal)
+    ts(r8(E8), r8(X16), r8(P16), None, eq)
+    ts(r8(M8), r8(XI), r8(P16), 15.0, sub, eq)
     ts(r8(n8r), r8(cni), 8.0, None, mul)
-    mm([(A("PL", 0, 2), r8(E8), r8(lmf), True, True)])
-    li, lh, ll = al("AI", 2), al("AI", 2), al("AI", 2)
-    ts(sl(li, 0, 1), A("PL", 0, 1), 1.0, None, add); copy(sl(li, 1, 2), A("PL", 1, 2))
-    ts(lh, li, 8128, None, band); ts(ll, li, 63, None, band)
+    mm([(A("PW", 0, 2), r8(E8), r8(lmf), True, True)])
+    li, lhi, lli, lh, ll = al("AI", 2), al("AI", 2), al("AI", 2), al("AF", 2), al("AF", 2)
+    ts(sl(li, 0, 1), A("PW", 0, 1), 1.0, None, add); copy(sl(li, 1, 2), A("PW", 1, 2))
+    ts(lhi, li, 8128, None, band); ts(lli, li, 63, None, band); copy(lh, lhi); copy(ll, lli)
     s0, s1, s2, sv = al("AF", 2), al("AF", 2), al("AF", 1), al("AF", 2)
-    ts(s0, lh, sl(PB, 0, 1), None, mul); ts(s1, ll, sl(PB, 1, 2), None, mul); tt(sv, s0, s1, add)
-    ts(s2, sl(PB, 2, 3), -8192.0, sl(sv, 1, 2), mul, add)
-    LJ, LH = al("AB", 128), al("AB", 128)
-    ts(LJ, BO, s2, -4096.0, mul, mul); ts(LH, BO, sl(sv, 0, 1), 4096.0, mul, mul)
-    mm([(A("PL", 16, 32), r8(win(M8, b)), sl(r8(n8r), b, 256, 16), b == 0, b == 15) for b in range(16)])
-    act(sl(slot(0), 32, 48), A("PL", 16, 32), ID)
+    ts(s0, sl(PB, 0, 4, 3), sl(lh, 1, 2), None, mul); ts(s1, sl(PB, 1, 5, 3), sl(ll, 1, 2), None, mul)
+    ts(sl(s0, 1, 2), sl(PB, 3, 4), sl(lh, 0, 1), -1.0, mul, mul); ts(sl(s1, 1, 2), sl(PB, 4, 5), sl(ll, 0, 1), -1.0, mul, mul)
+    tt(sv, s0, s1, add); tt(s2, sl(sv, 0, 1), sl(sv, 1, 2), add)
+    ts(s2, sl(PB, 2, 3), -8192.0, s2, mul, add)
+    LJ = al("AB", 128)
+    ts(LJ, BO, s2, -4096.0, mul, mul)
+    mm([(A("PW", 16, 32), r8(win(M8, b)), sl(r8(n8r), b, 256, 16), b == 0, b == 15) for b in range(16)])
+    act(sl(slot(0), 32, 48), A("PW", 16, 32), ID)
 
     B = []
     for p in range(NP):
-        d = {k: al("AB", POS) for k in ("cd", "ca", "hd", "ha", "ja")}
-        d["y"], d["zt"] = al("AB", POS + 16), al("AB", 512)
-        memset(sl(d["y"], 0, 16), 0.0)
-        for k, n in (("uu", 8), ("base", 8), ("cp", 128), ("cq", 128), ("km", 8), ("kap", 8),
-                     ("c", 8), ("cc", 16), ("hp", 128), ("hq", 128), ("yp", 128), ("yq", 128)):
+        d = {k: al("AB", POS) for k in ("cd", "ca", "hd", "ha")}
+        d["ja"] = A("AK", POS * p, POS * (p + 1))
+        memset(rows(d["ja"], 0, 2), 0.0)
+        d["y0"] = al("AB", POS + 16)
+        d["y"] = sl(d["y0"], 16, POS + 16)
+        memset(sl(d["y0"], 0, 16), 0.0)
+        for k, n in (("ur", 8), ("cp", 128), ("cq", 128), ("km", 8), ("kap", 8), ("c", 8), ("cc", 16),
+                     ("hp", 128), ("hq", 128), ("yp", 128), ("yq", 128)):
             d[k] = al("AI", n)
-        for k, n in (("u32", 128), ("bA", 8), ("ku", 128), ("k1", 64), ("k2", 64), ("k3", 32), ("k4", 16), ("cu", 8), ("a12", 256),
-                     ("sc", 128), ("zx", 256), ("s", 256), ("sm", 256)):
+        for k, n in (("b0", 8), ("bA", 8), ("v", 128), ("k1", 64), ("k2", 64), ("k3", 32), ("k4", 16), ("cu", 8),
+                     ("u32", 128)):
             d[k] = al("AF", n)
         for k, n in (("co", 128), ("cco", 16), ("ho", 128), ("yo", 128), ("eo", 8)):
             d[k] = al("AU", n)
-        d["xn"], d["xc"], d["ye"], d["zx2"] = al("AB", QL), al("AB", QL), al("AB", QL), al("AB", 2 * QL)
+        for k in ("q", "xc", "ye"):
+            d[k] = al("AB", QL)
         B.append(d)
-    UR, U, UM, KI, TK = al("AI", 272), al("AI", 272), al("AI", 32), al("AI", 16), al("AI", 16)
+    U, UM, KI, TK = al("AI", 16), al("AI", 32), al("AI", 16), al("AI", 16)
     AC, junk, O48, N2, NF = al("AF", 1), al("AF", 16), al("AF", 48), al("AF", 32), al("AF", 256)
     XO, OO = al("AU", 16), al("AU", 48)
     INV, DD, ALT, SG, TM = al("AB", 272), al("AB", 256), al("AB", 256), al("AB", 512), al("AB", 512)
     memset(sl(INV, 256, 272), 0.0)
-    HALF = al("AB", 2 * QL)
-    memset(HALF, 0.5)
-    XC, XE = A("XS", 0, W), A("XS", 0, XW)
-    ulp = [sl(U, 128, 136), sl(U, 136, 144)]
-    unl = [sl(U, 0, 128), sl(U, 144, 272)]
+    QUART = al("AB", 2 * QL)
+    memset(QUART, 0.25)
+    XE = A("XS", 0, XW)
+    dma("Y", A("XS", XW, W + POS), A("stock", XW - W, POS), 2 << 20)
     rot = [0]
 
     def bank():
-        rot[0] ^= 1
-        return A("PD%d" % rot[0], 0, 512)
+        rot[0] += 1
+        return A("PD#%d" % rot[0], 0, 512)
+
+    def u32(p):
+        return A("PU", QL * p, QL * p + QL)
 
     def stage_u(t, p):
-        d, z = B[p], part(ZL[t], p)
-        pu = A("PU", 136 * p, 136 * p + 136)
-        a, b_ = (128, 0) if p == 0 else (0, 8)
-        mm([(sl(pu, a, a + 8), win(MW, b), sl(z, b, QL, 16), b == 0, b == 15) for b in range(16)] + [(sl(pu, b_, b_ + 128), WBO, z, True, True)])
-        for m in range(4 if CFG["tile"] else 0):
-            dma("Y", part(d["zt"], m), z if t else A("zed", QL * p, QL * p + QL), 32768)
-        copy(part(UR, p, 136), pu)
-        ts(part(U, p, 136), part(UR, p, 136), 4095, None, band)
-        u = ulp[p]
-        tt(d["uu"], u, u, mul)
-        ts(d["base"], d["uu"], 5, 4095, shr, band)
-        tt(d["ku"], u, KAP, mul, ind=REP8)
-        ts(d["u32"], unl[p], 32.0, None, add)
-        if CFG["fz"] == "S" and CFG["fx"] != "P":
-            act(sl(d["zx"], 0, QL), z, ID, bias=CH)
+        d, z = B[p], part(ZT[t][p], 0)
+        lp, rw, u = A("PU", 256 + 8 * p, 264 + 8 * p), A("PU", 272, 400), part(U, p, 8)
+        at("u" + AB[p])
+        mm([(lp, win(MW, b), sl(z, b, QL, 16), b == 0, b == 15) for b in range(16)])
+        copy(d["ur"], lp)
+        ts(u, d["ur"], 4095, None, band)
+        tt(d["v"], u, K32, add, ind=REP8)
+        tt(d["cp"], u, d["v"], mul, ind=REP8)
+        ts(d["cq"], d["cp"], 5, 4095, shr, band)
+        at("t" + AB[p])
+        if CFG["tile"][p] == "D":
+            for m in range(1, 4):
+                dma("Y", part(ZT[t][p], m), z if t else A("zed", QL * p, QL * p + QL), 32768 if t else 1 << 20)
+        else:
+            for n in (QL, 2 * QL):
+                if CFG["tile"][p] == "S":
+                    act(sl(ZT[t][p], n, 2 * n), sl(ZT[t][p], 0, n), ID)
+                else:
+                    copy(sl(ZT[t][p], n, 2 * n), sl(ZT[t][p], 0, n))
+        at("n" + AB[p])
+        mm([(rw, WBO, z, True, False), (rw, BO, CQ, False, True)])
+        ts(d["q"], rw, ROUND4096, ROUND4096, add, sub)
+        mm([(u32(p), WBO, z, True, False), (u32(p), part(BB, 1), CQ, False, False), (u32(p), NI, d["q"], False, True)])
+        if CFG["fuse"][p]:
+            act(d["u32"], u32(p), ID)
 
     def stage_o(t):
-        u = sl(U, 128, 144)
-        ts(sl(UM, 0, 16), u, 15, None, band); ts(sl(UM, 16, 32), u, 3, None, band)
+        at("o")
+        ts(sl(UM, 0, 16), U, 15, None, band); ts(sl(UM, 16, 32), U, 3, None, band)
         tt(sl(BASE, 0, 32), UM, CXD, add)
         copy(XO, sl(BASE, 0, 16))
         ts(sl(slot(t), 0, 16), sl(UM, 16, 32), 8.0, 8.0, mul, add)
-        tt(sl(INV, 0, 256), sl(slot(t), 32, 48), K12, ALU.is_ge, ind=REPA)
+        at("i")
+        if CFG["inv"] == "V":
+            tt(sl(INV, 0, 256), sl(slot(t), 32, 48), K12, ALU.is_ge, ind=REPA)
+        else:
+            pi = A("PW", 0, 256)
+            mm([(pi, part(BB, 0), KR, True, False)] + [(sl(pi, k, 256, 16), I1, sl(slot(t), 32, 48), False, k == 15) for k in range(16)])
+            act(sl(INV, 0, 256), pi, ACT.Relu)
 
     def stage_c(t, p):
-        d, z = B[p], part(ZL[t], p)
-        ts(d["bA"], d["base"], AC if t else 0.0, None, add)
-        XC = A("XS", 0, W + POS if t and CFG["ext"] else W)
-        tt(d["cp"], d["base" if CFG["ext"] else "bA"], d["ku"], add, ind=REP8)
-        ts(d["cq"], d["cp"], 4095, None, band)
-        if CFG["ext"] and t:
-            ts(d["co"], d["cq"], AC, None, add)
-        else:
-            copy(d["co"], d["cq"])
-        path = CFG["c_path"][p]
+        d, zt = B[p], ZT[t][p]
+        z = part(zt, 0)
+        XC = A("XS", 0, W + POS if t else W)
+        at("k" + AB[p])
+        ts(d["co"], d["cq"], AC if t else 0.0, None, add)
+        path = CFG["c"][p]
         for c in range(4):
+            at("c%s%d" % (AB[p], c))
             lo = 512 * c
             cd, ca = sl(d["cd"], lo, lo + 512), sl(d["ca"], lo, lo + 512)
-            if path[c] in "VR":
-                if CFG["tile"]:
-                    tt(cd, XC, d["zt"], sub, ind=part(d["co"], c, 32))
-                for m in range(0 if CFG["tile"] else 4):
-                    tt(part(cd, m), XC, z, sub, ind=sl(d["co"], 32 * c + 8 * m, 32 * c + 8 * m + 8))
+            if path[c] in "RV":
+                tt(cd, XC, zt, sub, ind=part(d["co"], c, 32))
+                now[1] = 2
                 if path[c] == "V":
-                    act(ca, cd, ACT.Abs)
+                    act(ca, cd, ACT.Abs, scale=0.5)
                 else:
                     ts(ca, cd, 0.0, None, mx)
             else:
-                if path[c] == "S":
-                    act(cd, XC, ID, ind=part(d["co"], c, 32))
-                else:
-                    copy(cd, XC, ind=part(d["co"], c, 32))
+                act(cd, XC, ID, ind=part(d["co"], c, 32))
                 pd = bank()
                 lst = []
                 for m in range(4):
                     lst += [(part(pd, m), I1, part(cd, m), True, False), (part(pd, m), NI, z, False, True)]
                 mm(lst)
-                act(ca, pd, ACT.Abs)
+                act(ca, pd, ACT.Abs, scale=0.5)
             if c & 1:
                 h = c >> 1
-                pk = A("PK", QL * p + 64 * h, QL * p + 64 * h + 64)
-                lst = [(pk, BO, part(kx, h, 64), True, False), (pk, BO, part(km, h, 64), False, False)]
-                ra, rb = path[c - 1] == "R", path[c] == "R"
-                for (x0, x1, r) in (((0, 2, ra),) if ra == rb else ((0, 1, ra), (1, 2, rb))):
-                    o = sl(pk, 32 * x0, 32 * x1)
-                    for (M, src) in (((MN, "cd"), (M2P, "ca")) if r else ((MP, "ca"),)):
-                        lst += [(o, win(M, b), sl(d[src], 1024 * h + 512 * x0 + b, 1024 * h + 512 * x1, 16), False, False) for b in range(16)]
-                lst[-1] = lst[-1][:4] + (True,)
-                mm(lst)
+                at("q%s%d" % (AB[p], h))
+                pk = A("PK%d" % h, 0, 64)
+                lst = [(pk, BO, part(KM, h, 64), True, False)]
+                r = [x for x in (0, 1) if path[c - 1 + x] == "R"]
+                if r:
+                    x0, x1 = r[0], r[-1] + 1
+                    lst += [(sl(pk, 32 * x0, 32 * x1), win(MN, b), sl(d["cd"], 1024 * h + 512 * x0 + b, 1024 * h + 512 * x1, 16), False, False) for b in range(16)]
+                    mm(lst)
+                    lst = []
+                now[1] = 1
+                mm(lst + [(pk, win(M2P, b), sl(d["ca"], 1024 * h + b, 1024 * h + 1024, 16), False, b == 15) for b in range(16)])
                 if h == 0:
                     act(d["k1"], pk, ID)
                 else:
                     tt(d["k2"], pk, d["k1"], mn)
 
     def stage_m(t, p):
-        d = B[p]
+        d, u = B[p], part(U, p, 8)
+        at("m" + AB[p])
+        ts(d["b0"], u, NK0, AC if t else 0.0, mul, add)
+        tt(d["bA"], d["b0"], sl(d["cq"], 0, 8), add)
         for a, b, n in (("k2", "k3", 32), ("k3", "k4", 16), ("k4", "km", 8)):
             tt(d[b], sl(d[a], 0, n), sl(d[a], n, 2 * n), mn)
         ts(d["kap"], d["km"], 255, None, band)
-        tt(d["cu"], d["kap"], ulp[p], mul)
+        tt(d["cu"], d["kap"], u, mul)
         tt(d["c"], d["cu"], d["bA"], add)
         ts(sl(d["cc"], 0, 8), d["c"], 1023, None, band); ts(sl(d["cc"], 8, 16), d["c"], 4095, None, band)
         copy(d["cco"], d["cc"])
-        tt(d["yp"], A("DL", 0, ND), d["u32"], mul, ind=sl(d["cco"], 0, 8))
+        act(part(DD, p), A("DL", 0, ND), ID, ind=sl(d["cco"], 0, 8))
+        if CFG["fuse"][p]:
+            tt(d["yp"], A("DL", 0, ND), d["u32"], mul, ind=sl(d["cco"], 0, 8))
+        else:
+            tt(d["yp"], u32(p), part(DD, p), mul)
         ts(d["yq"], d["yp"], 5, 4095, shr, band)
         ts(d["yo"], d["yq"], K37, None, add, ind=TAU)
-        act(part(DD, p), A("DL", 0, ND), ID, ind=sl(d["cco"], 0, 8))
-        if CFG["fx"] == "P":
-            act(d["xc"], XC, ID, ind=sl(d["cco"], 8, 16))
-        else:
-            act(sl(d["zx"], QL, 2 * QL), XC, ID, bias=CH if CFG["fx"] != "V" else None, ind=sl(d["cco"], 8, 16))
+        at("g" + AB[p])
+        act(d["xc"], A("XS", 0, W), ID, ind=sl(d["cco"], 8, 16))
 
     def stage_h(t, p):
         d = B[p]
-        tt(d["hp"], part(sl(slot(t), 304, 560), p), d["u32"], mul)
+        at("h" + AB[p])
+        tt(d["hp"], u32(p), part(sl(slot(t), 304, 560), p), mul)
         ts(d["hq"], d["hp"], 5, 4095, shr, band)
         ts(d["ho"], d["hq"], K37, None, add, ind=TAU)
 
     def stage_y(t, p):
         d = B[p]
         pjh = A("PJH", 512 * p, 512 * p + 256)
-        pj, ph = part(pjh, 0), part(pjh, 1)
-        first = mm([(pjh, LJ, RC, True, False), (ph, LH, part(RC, 0), False, False)])
-        last = [first, first]
+        pj, ph = sl(pjh, 0, 256, 2), sl(pjh, 1, 256, 2)
+        at("f" + AB[p])
+        first = mm([(pjh, LJ, RC, True, False)])
+        first["wr"] = [A("PJH", 512 * p, 512 * p + 512)]
+        upto = mm([(pj, BIGI, sl(INV, QL * p, QL * p + QL), False, False), (ph, BIGI, sl(INV, QL * p + 1, QL * p + QL + 1), False, False)], after=[first])
+        sums = [upto]
         lo = 0
-        for ch in CFG["ych"][p]:
-            y = sl(d["y"], 16 + lo, 16 + lo + ch)
-            act(y, XE, ID, ind=sl(d["yo"], lo // 16, (lo + ch) // 16))
-            hd, ha = sl(d["hd"], lo, lo + ch), sl(d["ha"], lo, lo + ch)
-            tt(hd, XE, y, sub, ind=sl(d["ho"], lo // 16, (lo + ch) // 16))
-            bs = range(lo // QL, (lo + ch) // QL)
-            if CFG["j_abs"][p][lo * 2 // POS] == "S":
-                for l2 in range(lo, lo + ch, 512):
-                    n2 = min(512, lo + ch - l2)
-                    pd = sl(bank(), 0, n2)
-                    mm([(pd, I1, sl(d["y"], 16 + l2, 16 + l2 + n2), True, False), (pd, NI, sl(d["y"], 15 + l2, 15 + l2 + n2), False, True)])
-                    act(sl(d["ja"], l2, l2 + n2), pd, ACT.Abs)
-                    last[0] = mm([(pj, win(MP, b), part(d["ja"], b), False, False) for b in range(l2 // QL, (l2 + n2) // QL)], after=[last[0]])
-            else:
-                last[0] = mm([(pj, win(MN, b), sl(d["y"], e + QL * b, e + QL * b + QL), False, False) for b in bs for e in (15, 16)], after=[last[0]])
-                tt(sl(d["ja"], lo, lo + ch), y, sl(d["y"], 15 + lo, 15 + lo + ch), mx)
-                last[0] = mm([(pj, win(M2P, b), part(d["ja"], b), False, False) for b in bs], after=[last[0]])
-            if CFG["h_abs"][p][lo * 4 // POS] == "S":
-                act(ha, hd, ACT.Abs)
-                last[1] = mm([(ph, win(MN, b), part(d["ha"], b), False, False) for b in bs], after=[last[1]])
-            else:
-                last[1] = mm([(ph, win(MP, b), part(d["hd"], b), False, False) for b in bs], after=[last[1]])
-                ts(ha, hd, 0.0, None, mx)
-                last[1] = mm([(ph, win(M2N, b), part(d["ha"], b), False, False) for b in bs], after=[last[1]])
+        for c, ch in enumerate(CFG["ych"][p]):
+            at("y%s%d" % (AB[p], c))
+            act(sl(d["y"], lo, lo + ch), XE, ID, ind=sl(d["yo"], lo // 16, (lo + ch) // 16))
             lo += ch
-        mm([(pj, BIGI, sl(INV, QL * p, QL * p + QL), False, False), (ph, BIGI, sl(INV, QL * p + 1, QL * p + QL + 1), False, True)], after=last)
-        tt(d["a12"], pjh, C12, mn)
+        for c in range(4):
+            pd, lo = bank(), 512 * c
+            at("j%s%d" % (AB[p], c))
+            mm([(pd, I1, part(d["y"], c, 512), True, False), (pd, NI, sl(d["y0"], 15 + lo, 527 + lo), False, True)])
+            act(rows(part(d["ja"], c, 512), 2, 16), rows(pd, 2, 16), ACT.Abs)
+            sums.append(mm([(pj, win(MP, b), part(d["ja"], b), False, False) for b in range(4 * c, 4 * c + 4)], after=[first]))
+        lo = 0
+        for c, ch in enumerate(CFG["hch"][p]):
+            end = lo + ch == POS
+            y = sl(d["y"], lo, lo + ch)
+            hd, ha = sl(d["hd"], lo, lo + ch), sl(d["ha"], lo, lo + ch)
+            ho = sl(d["ho"], lo // 16, (lo + ch) // 16)
+            bs = range(lo // QL, (lo + ch) // QL)
+            path = CFG["h"][p][c]
+            at("d%s%d" % (AB[p], c))
+            if path == "S":
+                act(hd, XE, ID, ind=ho)
+                pd = sl(bank(), 0, ch)
+                mm([(pd, I1, hd, True, False), (pd, NI, y, False, True)])
+                act(ha, pd, ACT.Abs, scale=0.5)
+            else:
+                tt(hd, XE, y, sub, ind=ho)
+                if path == "V":
+                    now[1] = 2
+                    act(ha, hd, ACT.Abs, scale=0.5)
+                else:
+                    sums.append(mm([(ph, win(MP, b), part(d["hd"], b), False, False) for b in bs], after=[first]))
+                    ts(ha, hd, 0.0, None, mx)
+            sums.append(mm([(ph, win(M2N, b), part(d["ha"], b), False, end and b == bs[-1]) for b in bs], after=sums[:] if end else [first]))
+            lo += ch
 
     nrem = [0]
 
     def send(src, dst):
         k = nrem[0]
         nrem[0] += 1
-        op("G", 900, ("rem", dst, src, k), [src], [dst], lat=CFG["REM"] + width(src), rem=k)
+        op("G", ("r", width(src)), ("rem", dst, src, k), [src], [dst], rem=k, far=True)
 
     def stage_e(t, p):
-        d, z = B[p], part(ZL[t], p)
-        op("V", vc(128, 1), ("scan", d["sc"], sl(d["a12"], 0, 128), sl(d["a12"], 128, 256)), [d["a12"]], [d["sc"]])
-        sc = sl(d["sc"], 15, 128, 16)
-        tt(part(KI, p, 8), CE, sc, sub)
-        ts(d["eo"], part(KI, p, 8), 0.125, B128, mul, add)
-        yw = sl(d["y"], 16, 16 + POS)
-        if CFG["fx"] == "P":
-            ps = A("PJH", 512 * p + 256, 512 * p + 512)
-            pz, px = part(ps, 0), part(ps, 1)
-            pre = mm([(ps, NI, HALF, True, False), (pz, I1, z, False, False), (px, I1, d["xc"], False, False)])
-            act(d["ye"], yw, ID, ind=d["eo"])
-            mm([(px, I1, d["ye"], False, False), (pz, I1, d["ye"], False, True)], after=[pre])
-            ts(d["zx2"], ps, MAGIC, MAGIC, add, sub)
-            act(part(ZN[t], p), part(d["zx2"], 0), ID, scale=0.5)
-            if t + 1 < NV:
-                send(part(ZN[t], p), part(ZL[t + 1], p))
-        for h in range(2 if CFG["fx"] != "P" else 0):
-            s_, sm = part(d["s"], h), part(d["sm"], h)
-            if h and CFG["fx"] == "M":
-                tt(s_, yw, part(d["zx"], h), add, ind=d["eo"])
-                ts(d["xn"], s_, MAGIC, MAGIC, add, sub)
-                continue
-            if CFG["fx" if h else "fz"] == "S":
-                tt(s_, yw, part(d["zx"], h), add, ind=d["eo"])
-                act(sm, s_, ID, bias=CM)
-            else:
-                tt(s_, yw, part(d["zx"], h) if h else z, add, ind=d["eo"])
-                ts(sm, s_, -0.5, MAGIC, add, add)
-            act(d["xn"] if h else part(ZN[t], p), sm, ID, bias=CN, scale=0.5)
-            if h == 0 and t + 1 < NV:
-                send(part(ZN[t], p), part(ZL[t + 1], p))
-        tt(sl(slot(t), 16 + 8 * p, 24 + 8 * p), SK, sc, sub)
+        d, z = B[p], part(ZT[t][p], 0)
+        at("e" + AB[p])
+        pjh, sc = A("PJH", 512 * p, 512 * p + 256), part(SC, p, 256)
+        op("V", ("v", 256), ("scan", sc, pjh, CODE, 2048.0 - 1017.0), [pjh, CODE], [sc])
+        ts(d["eo"], sl(sc, 2, 256, 32), -0.125, B128, mul, add)
+        ps = A("PJH", 512 * p + 256, 512 * p + 512)
+        pz, px = part(ps, 0), part(ps, 1)
+        pre = mm([(ps, HI, sl(ZT[t][p], 0, 2 * QL), True, False), (pz, NI, QUART, False, False), (px, HI, d["xc"], False, False)] if 0 else
+                 [(ps, NI, QUART, True, False), (pz, HI, z, False, False), (px, HI, d["xc"], False, False)], rdx=[sc])
+        act(d["ye"], d["y"], ID, ind=d["eo"])
+        mm([(px, HI, d["ye"], False, False), (pz, HI, d["ye"], False, True)], after=[pre])
+        at("r" + AB[p])
+        if CFG["split"][p]:
+            ts(part(ZX[t][p], 0), pz, ROUND1, ROUND1, add, sub)
+            ts(part(ZX[t][p], 1), px, ROUND1, ROUND1, add, sub)
+        else:
+            ts(ZX[t][p], ps, ROUND1, ROUND1, add, sub)
+        now[1] = 2
+        if t + 1 < NV:
+            send(part(ZX[t][p], 0), part(ZT[t + 1][p], 0))
+        else:
+            at("v" + AB[p])
+            dma("Y", A("yz", QL * p, QL * p + QL), part(ZX[t][p], 0), 32768)
 
     def stage_x(t, p):
         lo = POS * p
-        if CFG["fx"] in "MP":
-            o, i, x = A("XS", lo, lo + POS), B[p]["xn"] if CFG["fx"] == "M" else part(B[p]["zx2"], 1), part(XO, p, 8)
-            op("V", 50 + QL * CFG["SC"] * 0.83 * F, ("tts", o, i, part(HALF, 0), mul, x), [i, HALF, x], [o])
-        else:
-            copy(A("XS", lo, lo + POS), B[p]["xn"], sc=part(XO, p, 8))
+        at("x" + AB[p])
+        copy(A("XS", lo, lo + POS), part(ZX[t][p], 1), sc=part(XO, p, 8))
         if t + 1 == NV:
+            at("z" + AB[p])
             dma("Y", A("yx", lo, lo + POS), A("XS", lo, lo + POS), 1 << 19)
+        elif p == 0 and CFG["wrap"] == "D":
+            dma("Y", A("XS", W, W + POS), A("XS", 0, POS), 1 << 19)
         elif p == 0:
-            n = POS if CFG["ext"] else XW - W
-            dma("Y", A("XS", W, W + n), A("XS", 0, n), 256 * n * CFG["DB"])
+            copy(A("XS", W, W + POS), part(ZX[t][p], 1), sc=part(XO, p, 8))
 
     def stage_w(t):
         s = slot(t)
         L, nn, Ln, Rn = sl(s, 48, 304), sl(s, 560, 576), sl(s, 576, 832), sl(s, 832, 1088)
+        at("a")
+        copy(KI, sl(SC, 2, 512, 32))
         ts(TK, KI, 3, None, band)
         ts(sl(FL, 32, 48), TK, 1.0, 256.0, ALU.is_lt, mul)
         if t + 1 < NV:
-            mm([(A("PL", 0, 16), ON, sl(FL, 32, 48), True, True)])
-            act(junk, A("PL", 0, 16), ID, acc=AC)
-        ts(sl(FL, 16, 32), TK, 2.0, 272.0, ALU.is_lt, mul)
-        ts(sl(FL, 0, 16), TK, 2.0, 1024.0, ALU.is_ge, mul)
+            mm([(A("PK0", 64, 80), ON, sl(FL, 32, 48), True, True)])
+            act(junk, A("PK0", 64, 80), ID, acc=AC)
+        at("p")
+        tt(sl(s, 16, 32), SK, sl(SC, 2, 512, 32), sub)
+        at("w")
+        ts(sl(FL, 16, 32), TK, 2.0, 272.0, ALU.not_equal, mul)
+        ts(sl(FL, 0, 16), TK, 2.0, 1024.0, eq, mul)
         tt(O48, FL, sl(BASE, 16, 64), add)
         copy(OO, O48)
         tt(N2, sl(s, 0, 32), sl(FL, 0, 32), add)
@@ -456,19 +559,23 @@ def build():
         mm([(A("PW", b, 512, 16), part(BB, b), sl(s, 16, 48), True, True) for b in range(16)])
         act(ALT, sl(s, 48, 560), ID, ind=sl(OO, 32, 48))
         act(SG, A("PW", 0, 512), ACT.Sign, bias=R8)
-        pd = A("PW", 0, 512)
+        pd = A("PJH", 0, 512)
         pa, pb = part(pd, 0, 256), part(pd, 1, 256)
         mm([(pb, I1, L, True, False), (pb, NI, DD, False, True), (pa, I1, DD, True, False), (pa, NI, ALT, False, True)])
         tt(TM, pd, SG, mul)
-        pl = A("PL", 256, 512)
-        mm([(pl, HI, r, i == 0, i == 3) for i, r in enumerate((L, ALT, part(TM, 0, 256), part(TM, 1, 256)))])
-        act(Ln, pl, ID)
+        pa = A("PW", 0, 256)
+        mm([(pa, HI, r, i == 0, i == 3) for i, r in enumerate((L, ALT, part(TM, 0, 256), part(TM, 1, 256)))])
+        act(Ln, pa, ID)
         act(Rn, sl(s, 304, 832), ID, ind=sl(OO, 16, 32))
-        copy(A("DL", 0, 2 * ND), Ln, sc=sl(OO, 0, 16))
-        if t + 1 < NV:
+        if t + 1 < NV and CFG["inv"] == "V":
             send(sl(s, 560, 1088), sl(slot(t + 1), 32, 560))
-        else:
-            dma("A", A("yz", 0, 256), ZN[t], 65536)
+        elif t + 1 < NV:
+            send(sl(s, 576, 1088), sl(slot(t + 1), 48, 560))
+            send(nn, sl(slot(t + 1), 32, 48))
+        at("s")
+        copy(A("DL", 0, 2 * ND), Ln, sc=sl(OO, 0, 16))
+        if t + 1 == NV:
+            at("l")
             dma("A", A("yl", 0, 256), Ln, 65536)
             dma("A", A("yr", 0, 256), Rn, 65536)
             pn = A("PU", 0, 256, 1, 0, 8)
@@ -481,8 +588,8 @@ def build():
         k = len(ops)
         st(*a)
         for o in ops[k:]:
-            o["stage"], o["k"], o["t"] = name + ("ab"[a[1]] if len(a) > 1 else ""), o["id"] - k, a[0]
-            o["key"] = "%s%s%d" % (name.upper() if a[0] + 1 == NV else name, "ab"[a[1]] if len(a) > 1 else "", o["id"] - k)
+            o["t"] = a[0]
+            o["key"] = "%s.%d" % (o["tag"], o["nth"])
 
     for t in range(NV):
         for name, st in (("u", stage_u), ("c", stage_c), ("m", stage_m), ("h", stage_h)):
@@ -500,11 +607,11 @@ def build():
 
 def depend(ops):
     hist = {}
-    banks = {}
     for o in ops:
         hard, soft = set(), set()
         e = o["eng"]
-        for a in o["rd"]:
+        reads = o["rd"] + o.get("rdx", [])
+        for a in reads:
             for (c0, c1, w, j) in hist.get(a[0], []):
                 if w and c0 < a[2] and a[1] < c1:
                     hard.add(j)
@@ -512,102 +619,209 @@ def depend(ops):
             for (c0, c1, w, j) in hist.get(a[0], []):
                 if c0 < a[2] and a[1] < c1:
                     x = ops[j]
-                    same = x["eng"] == e and "lat" not in x and "lat" not in o and (e == "P" or not (w or CFG["same_war"]))
-                    (soft if same else hard).add(j)
-        for a in o["rd"] + o["wr"]:
-            if a[0][0] == "P":
-                for k in range(a[1] // 512, (a[2] - 1) // 512 + 1):
-                    cur = banks.setdefault((a[0], k), [e, [], []])
-                    if cur[0] != e:
-                        cur[0], cur[1], cur[2] = e, [], cur[1]
-                    hard.update(cur[2])
-                    cur[1].append(o["id"])
+                    if x["eng"] == e == "P":
+                        if "after" not in o:
+                            soft.add(j)
+                    else:
+                        hard.add(j)
         if "after" in o:
             soft.update(x["id"] for x in o["after"])
         for a in o["wr"]:
             h = hist.setdefault(a[0], [])
-            if a[3] == 1 and a[4] == 0 and a[5] == 128:
+            if a[3] == 1 and a[4] == 0 and a[5] == 128 and "after" not in o:
                 h[:] = [x for x in h if not (a[1] <= x[0] and x[1] <= a[2])]
             h.append((a[1], a[2], True, o["id"]))
-        for a in o["rd"]:
+        for a in reads:
             hist.setdefault(a[0], []).append((a[1], a[2], False, o["id"]))
         hard.discard(o["id"]); soft.discard(o["id"])
-        o["hard"], o["soft"] = hard, soft - hard
+        o["hard"], o["soft"] = sorted(hard), sorted(soft - hard)
+        o["q"] = "S" if e == "A" else e
+        o["banks"] = sorted({(a[0], k) for a in o["rd"] + o["wr"] if a[0][0] == "P" and "#" not in a[0] for k in range(a[1] // 512, (a[2] - 1) // 512 + 1)})
+        o["take"] = [a[0] for a in o["wr"] if "#" in a[0]][:1]
+        o["give"] = [a[0] for a in o["rd"] if "#" in a[0]][:1]
+    for o in ops:
+        o["succ"] = []
+    for o in ops:
+        for j in o["hard"]:
+            ops[j]["succ"].append((o["id"], True))
+        for j in o["soft"]:
+            ops[j]["succ"].append((o["id"], False))
 
 
-def queue(o):
-    return "S" if o["eng"] == "A" else o["eng"]
-
-
-def order(ops):
+def order(ops, cost, lat, when):
     n = len(ops)
-    succ = [[] for _ in ops]
-    for o in ops:
-        for j in o["hard"] | o["soft"]:
-            succ[j].append(o["id"])
-    lat = CFG["LAT"]
-    bl = [0.0] * n
+    pr = [0.0] * n
     for o in reversed(ops):
-        bl[o["id"]] = o["cost"] + o.get("lat", 0) + max([bl[k] + lat for k in succ[o["id"]]] + [0])
-    if CFG["plan"]:
-        top = max(bl)
-        for o in ops:
-            if "key" in o:
-                name, k = o["stage"], o["k"]
-                for (k0, t0, dt) in WHEN[name]:
-                    if k >= k0:
-                        bl[o["id"]] = top - 6000 - 30000 * o["t"] - 1000 * (t0 + dt * (k - k0))
-    for o in ops:
-        bl[o["id"]] += PRIO.get(o.get("key"), 0) + FIRST.get(o.get("stage", "") + o["eng"], 0)
-    left = [len(o["hard"] | o["soft"]) for o in ops]
+        i = o["id"]
+        if "t" in o:
+            pr[i] = -1000 * (CFG["T"] * o["t"] + when[o["tag"]] + when.get(o["key"], 0) + 0.02 * o["nth"])
+        else:
+            pr[i] = sum(cost[i]) + lat + max([pr[k] for k, _h in o["succ"]] + [-1e9])
+    lent, name = [-1, -1], {}
+    left = [len(o["hard"]) + len(o["soft"]) for o in ops]
     ready = {q: [] for q in "VSPGY"}
-    est = [0.0] * n
+    est, t1 = [0.0] * n, [0.0] * n
     for o in ops:
         if left[o["id"]] == 0:
-            ready[queue(o)].append(o["id"])
+            ready[o["q"]].append(o["id"])
     free = {q: 0.0 for q in ready}
-    seq = []
+    held = {}
+    seq, hand = [], [()] * n
+
+    def start(i):
+        s = est[i]
+        for k in ops[i]["banks"]:
+            h = held.get(k)
+            if h and h[0] != ops[i]["q"] and t1[h[1]] + lat > s:
+                s = t1[h[1]] + lat
+        if ops[i]["take"]:
+            s = max(s, min(1e18 if j is None else t1[j] + lat if j >= 0 else 0 for j in lent))
+        return s
+
     while len(seq) < n:
         best = None
         for q, r in ready.items():
             if r:
-                t0 = max(free[q], min(est[i] for i in r))
+                t0 = max(free[q], min(map(start, r)))
                 if best is None or t0 < best[0]:
                     best = (t0, q)
         t0, q = best
-        i = max((i for i in ready[q] if est[i] <= t0 + CFG["SLACK"]), key=lambda i: bl[i])
-        if est[i] > t0:
-            fit = [k for k in ready[q] if est[k] <= t0 and t0 + ops[k]["cost"] <= est[i] + CFG["TOL"]]
+        st = {k: start(k) for k in ready[q]}
+        i = max((k for k in st if st[k] <= t0 + CFG["SLACK"]), key=lambda k: pr[k])
+        if st[i] > t0:
+            fit = [k for k in st if st[k] <= t0 and t0 + cost[k][0] <= st[i] + CFG["TOL"]]
             if fit:
-                i = max(fit, key=lambda k: bl[k])
+                i = max(fit, key=lambda k: pr[k])
         ready[q].remove(i)
         o = ops[i]
-        o["t0"] = max(free[q], est[i])
-        free[q] = o["t0"] + o["cost"]
-        o["t1"] = free[q] + o.get("lat", 0)
+        s = max(free[q], st[i])
+        free[q] = s + cost[i][0]
+        t1[i] = free[q] + cost[i][1]
+        hand[i] = tuple(held[k][1] for k in o["banks"] if k in held and held[k][0] != q)
+        for k in o["banks"]:
+            held[k] = (q, i)
+        if o["take"]:
+            k = min((k for k in (0, 1) if lent[k] is not None), key=lambda k: t1[lent[k]] if lent[k] >= 0 else 0)
+            hand[i] += (lent[k],) if lent[k] >= 0 else ()
+            lent[k], name[o["take"][0]] = None, k
+        if o["give"]:
+            lent[name[o["give"][0]]] = i
         seq.append(i)
-        for k in succ[i]:
-            est[k] = max(est[k], o["t1"] + lat if i in ops[k]["hard"] else o["t0"])
+        for k, hard in o["succ"]:
+            e = t1[i] + lat if hard else s
+            if e > est[k]:
+                est[k] = e
             left[k] -= 1
             if left[k] == 0:
-                ready[queue(ops[k])].append(k)
-    return seq
+                ready[ops[k]["q"]].append(k)
+    return seq, hand, name
+
+
+def rename(x, name):
+    if isinstance(x, (tuple, list)):
+        y = [rename(v, name) for v in x]
+        return tuple(y) if isinstance(x, tuple) else y
+    return "PD%d" % name[x] if isinstance(x, str) and x in name else x
+
+
+def replay(ops, seq, hand, cost, lat):
+    free = {q: 0.0 for q in "VSPGY"}
+    t1 = [0.0] * len(ops)
+    for i in seq:
+        o = ops[i]
+        s = free[o["q"]]
+        for j in o["hard"]:
+            if t1[j] + lat > s:
+                s = t1[j] + lat
+        for j in hand[i]:
+            if t1[j] + lat > s:
+                s = t1[j] + lat
+        free[o["q"]] = s + cost[i][0]
+        t1[i] = s + cost[i][0] + cost[i][1]
+    return t1
+
+
+def merge(ops, rows, cost, lat, pr):
+    n = len(ops)
+    left = [len(o["hard"]) + len(o["soft"]) for o in ops]
+    est, t1, hand, seq = [0.0] * n, [0.0] * n, [()] * n, []
+    listed = {i for q in rows for i in rows[q]}
+    loose = {q: sorted((o["id"] for o in ops if o["q"] == q and o["id"] not in listed), key=lambda i: pr[i]) for q in rows}
+    at, free = {q: 0 for q in rows}, {q: 0.0 for q in rows}
+    held, lent, name = {}, [-1, -1], {}
+    while len(seq) < n:
+        best = None
+        for q in rows:
+            pick = None
+            for i in loose[q] + rows[q][at[q]:at[q] + 1]:
+                if left[i]:
+                    continue
+                s = max([est[i], free[q]] + [t1[held[k][1]] + lat for k in ops[i]["banks"] if k in held and held[k][0] != q])
+                if ops[i]["take"]:
+                    back = [t1[j] + lat if j >= 0 else 0 for j in lent if j is not None]
+                    if not back:
+                        continue
+                    s = max(s, min(back))
+                if pick is None or (s - 60 < pick[0] if pr[i] < pr[pick[2]] else s + 60 < pick[0]):
+                    pick = (s, q, i)
+            if pick and (best is None or pick[0] < best[0]):
+                best = pick
+        s, q, i = best
+        o = ops[i]
+        if i in listed:
+            at[q] += 1
+        else:
+            loose[q].remove(i)
+        free[q] = s + cost[i][0]
+        t1[i] = free[q] + cost[i][1]
+        hand[i] = tuple(held[k][1] for k in o["banks"] if k in held and held[k][0] != q)
+        for k in o["banks"]:
+            held[k] = (q, i)
+        if o["take"]:
+            k = min((k for k in (0, 1) if lent[k] is not None), key=lambda k: t1[lent[k]] if lent[k] >= 0 else 0)
+            hand[i] += (lent[k],) if lent[k] >= 0 else ()
+            lent[k], name[o["take"][0]] = None, k
+        elif o["give"]:
+            lent[name[o["give"][0]]] = i
+        seq.append(i)
+        for k, hard in o["succ"]:
+            est[k] = max(est[k], t1[i] + lat if hard else s)
+            left[k] -= 1
+    return seq, hand, name, t1
 
 
 def plan():
     ops = build()
     depend(ops)
-    seq = order(ops)
+    lat = MODELS[0]["LAT"]
+    cost = [price(o, MODELS[0]) for o in ops]
+    by = {(o["key"], o["t"]): o["id"] for o in ops if "t" in o and not (o["t"] == NV - 1 and o["tag"] in CFG["last"])}
+    rows = {}
+    for line in ORDER.strip().splitlines():
+        q, *names = line.split()
+        turn = [(x.rstrip("+-"), x.count("+") - x.count("-")) for x in names]
+        rows[q] = [by[k, t + d] for t in range(-1, NV + 1) for k, d in turn if (k, t + d) in by]
+    listed = {i for q in rows for i in rows[q]}
+    pr = [0.0] * len(ops)
+    bare = [cost[o["id"]] if "t" in o else (0, 0) for o in ops]
+    t0 = merge(ops, rows, bare, lat, pr)[3]
+    for o in reversed(ops):
+        i = o["id"]
+        pr[i] = t0[i] - sum(bare[i]) if i in listed else min([pr[k] for k, _h in o["succ"]] + [max(t0) - 1500]) - sum(cost[i]) - lat
+    seq, hand, name, t1 = merge(ops, rows, cost, lat, pr)
+    CFG["end"] = max(t1)
+    for o in ops:
+        o["call"] = rename(o["call"], name)
     pos = {q: 0 for q in "VSPG"}
     known = {q: ({}, set()) for q in "VSPGY"}
     for i in seq:
         o = ops[i]
-        q = queue(o)
+        q = o["q"]
         cnt, one = known[q]
         waits = []
-        for j in sorted(o["hard"], key=lambda j: -ops[j]["t1"]):
+        for j in sorted(set(o["hard"]) | set(hand[i]), key=lambda j: -t1[j]):
             x = ops[j]
-            if "lat" in x:
+            if "far" in x:
                 if j in one:
                     continue
                 one.add(j)
@@ -623,7 +837,7 @@ def plan():
                 one.update(x["clock"][1])
         o["waits"] = waits
         o["clock"] = (dict(cnt), set(one))
-        if "lat" not in o:
+        if "far" not in o:
             o["pos"] = pos[q]
             pos[q] += 1
     num = {q: 0 for q in "VSPG"}
@@ -661,13 +875,17 @@ def rank_program(g, core, T, topo):
     def ap(a, ind=None):
         if not isap(a):
             return a
-        v = T[a[0]][a[4]:a[5], a[1]:a[2]:a[3]] if a[3] != 1 else T[a[0]][a[4]:a[5], a[1]:a[2]]
+        k0, k1 = a[6] if len(a) > 6 else (0, 16)
+        if len(SCRATCH.get(a[0], "--")[1]) == 3:
+            v = T[a[0]][:, a[1] // 16:a[2] // 16, k0:k1]
+        else:
+            v = T[a[0]][a[4]:a[5], a[1]:a[2]:a[3]] if a[3] != 1 else T[a[0]][a[4]:a[5], a[1]:a[2]]
         return v if ind is None else v.indirect(ap(ind))
 
     sent = 0
     for i in seq:
         o = ops[i]
-        q = Q[queue(o)]
+        q = Q[o["q"]]
         for j in o["waits"]:
             x = ops[j]
             q.wait_ge(T.sem[x["sem"]], in_n if "rem" in x else x["val"])
@@ -677,15 +895,14 @@ def rank_program(g, core, T, topo):
             r = q.tensor_copy(ap(c[1], c[4]), ap(c[2], c[3]))
         elif k == "tt":
             r = q.tensor_tensor(ap(c[1]), ap(c[2], c[5]), ap(c[3]), c[4])
-        elif k == "tts":
-            r = q.tensor_tensor(ap(c[1], c[5]), ap(c[2]), ap(c[3]), c[4])
         elif k == "ts":
             if c[6] is None:
                 r = q.tensor_scalar(ap(c[1]), ap(c[2], c[7]), ap(c[3]), None, c[5])
             else:
                 r = q.tensor_scalar(ap(c[1]), ap(c[2], c[7]), ap(c[3]), ap(c[4]), c[5], c[6])
         elif k == "scan":
-            r = q.tensor_tensor_scan(ap(c[1]), ap(c[2]), ap(c[3]), 0.0, ALU.max, ALU.max)
+            back = lambda a: T[a[0]][:, a[2] - 1:a[1] - 1:-1] if a[1] else T[a[0]][:, a[2] - 1::-1]
+            r = q.tensor_tensor_scan(back(c[1]), back(c[2]), back(c[3]), c[4], ALU.max, ALU.min)
         elif k == "memset":
             r = q.memset(ap(c[1]), c[2])
         elif k == "act":

import numpy as np
from concourse.mybir import AluOpType as ALU, ActivationFunctionType as ACT

NV, W, ND = 5, 4096, 1024
NP, QL, NA = 2, 128, 8
POS = 16 * QL
XW = 4672
ROUND1 = 12582912.0
ROUND4096 = 51539607552.0
SLOT = 1088
CFG = {
    "c": ["VVSS", "SSVV"], "h": ["RVRR", "RVRV"], "ych": [[512] * 4, [512] * 4], "hch": [[512] * 4, [512] * 4],
    "split": [0, 1], "wrap": "D", "inv": "V", "last": ("a", "p", "w", "s", "rb", "xb", "eb"), "fuse": [0, 0], "tile": "SD", "SLACK": 200.0, "TOL": 60.0, "T": 25,
}
MODELS = [
    {"F": 1.1, "G": 1.55, "SC": 3.5, "OV": 0.0, "LAT": 150.0, "PE": 0.42, "TT": 1.0, "REM": 3400.0, "BW": 250.0, "W": 145},
    {"F": 1.45, "G": 2.0, "SC": 4.5, "OV": 0.0, "LAT": 60.0, "PE": 0.42, "TT": 1.0, "REM": 3400.0, "BW": 200.0, "W": 185},
    {"F": 1.05, "G": 1.1, "SC": 2.5, "OV": 0.0, "LAT": 200.0, "PE": 0.42, "TT": 1.0, "REM": 4200.0, "BW": 300.0, "W": 142},
    {"F": 1.3, "G": 1.1, "SC": 4.0, "OV": 0.0, "LAT": 80.0, "PE": 0.5, "TT": 1.0, "REM": 4000.0, "BW": 200.0, "W": 120},
]
WHEN = {
    "ua": -8, "na": 1, "ka": -1, "ca0": 0, "ca1": 0.8, "ca2": 0, "ca3": 0.8, "ma": -2, "ga": 12, "ha": 5,
    "ub": 0.5, "nb": 4, "kb": 0.6, "cb0": 4, "cb1": 5, "cb2": 5.5, "cb3": 6.5, "mb": 5.2, "gb": 18, "hb": 9,
    "o": 10, "i": 8, "fa": 6, "fb": 12,
    "ya0": 6, "ya1": 7, "ya2": 8, "ya3": 9, "ja0": 7.5, "ja1": 8.5, "ja2": 9.5, "ja3": 10.5,
    "da0": 7.2, "da1": 8.2, "da2": 9.2, "da3": 10.2, "ea": 8,
    "yb0": 12, "yb1": 13, "yb2": 14, "yb3": 15, "jb0": 13.5, "jb1": 14.5, "jb2": 15.5, "jb3": 16.5,
    "db0": 13.2, "db1": 14.2, "db2": 15.2, "db3": 16.2, "eb": 14,
    "xa": 21, "xb": 20, "a": 20.5, "w": 25.5, "s": 28, "za": 22, "zb": 22, "va": 20, "vb": 23,
}
WHEN.update({'ua': -6.3, 'na': 6.0, 'ka': -0.4, 'ca0': -2.1, 'ca1': -0.5, 'ca2': -3.9, 'ca3': 6.5, 'ma': -2.1, 'ga': -1.0, 'ha': 6.2, 'ub': 0.9, 'nb': 6.8, 'kb': -6.6, 'cb0': 8.1, 'cb1': 0.4, 'cb2': 3.7, 'cb3': 6.3, 'mb': 4.0, 'gb': 36.6, 'hb': 10.6, 'o': 11.4, 'i': 11.2, 'fa': 7.9, 'fb': 15.9, 'ya0': 6.6, 'ya1': -6.8, 'ya2': 4.9, 'ya3': 16.2, 'ja0': 11.6, 'ja1': 7.0, 'ja2': 4.4, 'ja3': 18.8, 'da0': 14.0, 'da1': 8.7, 'da2': 6.1, 'da3': 13.9, 'ea': -0.1, 'yb0': 17.2, 'yb1': 7.1, 'yb2': 16.5, 'yb3': 17.3, 'jb0': 19.5, 'jb1': 2.9, 'jb2': 21.1, 'jb3': 19.7, 'db0': 8.2, 'db1': 16.6, 'db2': -7.2, 'db3': 22.0, 'eb': 12.5, 'xa': 36.6, 'xb': 2.0, 'a': 23.3, 'w': 24.3, 's': 27.9, 'da0.1': 6.8, 'ca3.4': -6.2, 'ca3.2': -2.9, 'xa.1': -2.3, 'da1.0': -1.1, 'ub.8': -1.5, 'da0.0': -3.7, 'mb.2': -4.0, 'da0.3': 3.7, 'fb.0': 1.4, 'mb.11': 5.3, 'w.1': 2.9, 'w.7': -0.2, 'yb3.0': 1.8, 'ya1.0': 2.8, 'w.3': -1.0, 'ma.3': 1.2, 'ca1.0': -6.9, 'da1.3': 5.2, 'i.0': -3.8, 'ja1.0': 2.8, 's.5': -2.1, 'mb.13': -4.3, 'cb2.0': 1.0, 'mb.3': 0.7, 'ca3.1': -6.5, 'db3.2': 0.1, 'ua.7': 7.4, 'fb.1': -1.5, 'ma.1': 3.5, 'jb3.0': 2.7, 'mb.7': 4.7, 'hb.2': -5.0, 'mb.5': 2.5, 'w.8': -6.4, 'ma.2': 4.1, 'ua.4': -3.9, 'ja2.2': 10.2, 'ea.6': -5.7, 'db3.3': 7.4, 'xb.1': 5.0, 'o.1': 1.7, 'ca3.3': 0.0, 'jb1.1': 0.3, 'na.2': 1.7, 'db1.1': 6.6, 'ma.7': -4.0, 'ma.11': -1.9, 'ja0.0': 2.6, 'w.9': 2.8, 'ca2.1': 2.2, 'ha.0': -4.3, 'w.0': -2.4, 'cb3.0': -4.2, 'ca1.2': 6.9, 'ma.6': 0.0, 'da2.2': -0.1, 'da0.2': -0.2, 'ja2.0': 0.5, 'da3.0': -2.8, 'da1.1': -3.1, 'w.5': 2.0, 'da2.1': -4.8, 'eb.2': -6.6, 'jb0.0': 3.9, 'ca1.4': -8.3, 'w.6': 6.5, 'fa.1': -6.3, 'da1.2': 1.8, 'db2.1': -7.0, 'a.2': 1.0, 'cb3.3': -3.2, 'na.0': 3.9, 'o.2': 4.5, 'yb0.0': -2.1, 'ub.6': 3.6, 'fa.0': 0.3, 'ka.0': -0.8, 'da2.0': -1.1, 'ma.8': -1.9, 'ca2.0': -0.3, 'cb1.1': -1.2, 'nb.1': 2.5, 'ha.2': 0.5, 'ma.4': -5.0, 'ja2.1': -1.3, 'ea.4': -0.1, 'a.0': 2.9, 'ua.0': 1.9, 'mb.6': 4.7, 'ca0.1': -2.5, 'ca2.2': 0.9, 'jb0.2': 3.9, 'ea.2': 1.9, 'ca1.3': 0.3, 'db1.2': -1.9, 'cb0.1': -3.3, 'ja0.2': -2.9, 'w.13': -2.6, 'ma.12': -4.4, 'eb.4': -3.6, 'ja3.1': -1.6, 'ua.5': 0.4, 'w.10': -5.4, 'db0.3': -2.1, 'na.1': -1.1, 'ja0.1': 0.3, 'ua.1': 3.9, 'cb3.2': -1.6, 'ua.6': -1.5, 'db1.3': 3.1, 'eb.3': -3.1, 'ea.7': 6.5, 'jb2.2': 4.8, 'eb.5': -1.7, 'ca1.1': 0.1, 'ub.5': -4.8, 'jb0.1': 0.8, 'ub.0': -3.1, 'ub.3': 3.3, 'eb.0': -2.7, 'ea.1': 1.3, 'w.14': 0.6, 'db3.1': 6.4, 'xa.0': 1.3, 'ya2.0': -4.6, 'ea.9': 1.8, 'ea.5': -2.5, 'ma.9': -1.0, 'ub.2': 7.5, 'mb.0': 2.0, 'eb.6': 0.7, 'db3.0': 3.0, 'ya3.0': -0.6, 'nb.2': 1.0, 'ea.8': 1.5, 'ja3.0': -4.9, 's.6': 2.2, 'cb1.3': 3.8, 'xb.0': -1.1, 'mb.1': -1.5, 'ga.0': 0.1, 'ea.0': 3.7, 'kb.0': 0.9, 'ub.7': 0.7, 'db2.2': 0.4, 'w.4': 4.2, 'jb1.0': 0.5, 'ma.0': 3.5, 'o.0': -0.7, 'ma.13': 4.2, 'ja3.2': -1.2, 'a.1': 0.4, 'hb.0': -1.3, 'eb.1': 2.9, 's.1': -3.6, 'cb0.0': -5.2, 'ca0.0': 0.0, 'ca3.0': -2.5, 'ub.1': -0.7, 's.4': -6.1, 'ua.8': 1.1, 'ha.1': -1.2, 'a.3': -2.1, 'da2.3': -1.7, 'db1.0': -0.5, 'ub.4': 0.6, 'yb1.0': 1.6, 's.0': -0.8, 'cb3.1': -2.2, 'cb3.4': 1.2, 'da3.2': 1.0, 'ya0.0': 2.7, 'mb.10': -2.5, 'ea.3': -3.2, 'jb2.0': 1.2, 'ja1.1': 0.3, 'jb2.1': 0.1, 'ma.5': -3.3, 's.3': -0.1, 'mb.4': 1.0, 'ua.3': 1.1, 'eb.7': 1.8, 'db2.0': -0.7, 's.2': 2.8, 'db0.0': -0.6, 'jb1.2': -1.6, 'o.3': 1.6, 'gb.0': -1.9, 'cb2.1': -1.2})

ORDER = """
V ua.2 rb.0- ma.0 ua.3 w.4- ua.4 rb.1- ua.5 xb.0- ka.0 w.5- w.10- ca0.0 ca1.0 ca0.2 ca1.2 s.0- ub.1 ub.2 na.1 ub.3 ub.4 qa1.2 ub.5 ma.2 kb.0 ma.3 ma.4 ma.1 ma.5 ma.6 ma.7 nb.1 ma.9 ma.8 cb2.0 ma.10 cb3.0 ma.12 ha.0 ma.13 mb.0 ma.14 ha.1 cb3.2 ha.2 i.0 mb.1 da0.0 qb1.2 mb.2 mb.3 o.1 mb.4 mb.5 da1.0 mb.6 da0.2 mb.7 hb.0 mb.8 mb.9 hb.1 mb.10 da2.0 mb.12 o.0 mb.13 mb.14 da3.0 da2.2 hb.2 da3.2 db0.0 ea.0 o.2 ea.1 ea.2 o.3 ea.3 db1.0 ra.0 db2.0 db0.2 o.4 db2.2 db3.0 ea.7 xa.0 eb.0 eb.1 eb.2 a.0 eb.3 a.1 w.1 w.0 eb.7 w.2 ua.1+ w.3
S cb1.2 cb2.2 ya0.0 qb0.2 ya1.0 ya2.0 ja0.1 ya3.0 ja2.1 ja1.1 mb.11 da1.2 ja3.1 yb0.0 yb1.0 yb2.0 ga.0 jb0.1 ea.5 jb1.1 yb3.0 gb.0 db1.2 jb2.1 jb3.1 db3.2 eb.5 a.3 w.7 w.8 ca2.0+ ca3.0+ w.12 w.13 ca2.2+ ca3.2+ qa0.2+ cb0.0+ cb1.0+ cb0.2+ ma.11+
P fb.0 qb1.0 qb0.1 qb1.1 ja0.0 nb.2 da0.1 ja2.0 ja1.0 fa.1 ja0.2 ja3.0 ja2.2 ja1.2 da0.3 da1.3 da2.1 ja3.2 da3.1 da2.3 da3.3 jb0.0 jb1.0 ea.4 fb.1 ea.6 jb0.2 db0.1 jb1.2 jb2.0 jb3.0 db2.1 db1.3 db0.3 db2.3 jb2.2 jb3.2 db3.3 eb.4 ua.0+ a.2 eb.6 w.6 na.0+ w.9 w.11 ca2.1+ ca3.1+ qa0.0+ ub.0+ qa0.1+ qa1.1+ fa.0+ na.2+ nb.0+ cb0.1+ cb1.1+
G w.14- ra.2 rb.2
Y tb.2 tb.0 tb.1 xa.1 ta.2+ ta.1+ ta.0+
"""
ORDER = """
V ca1.0 ca0.0 ca1.2 ca0.2 s.0- ub.1 na.1 ub.2 ma.0 ub.3 ub.4 qa1.2 ub.5 ma.2 kb.0 ma.3 ma.4 nb.1 ma.5 ma.1 ma.6 cb2.0 ma.7 mb.0 ma.9 ma.8 ma.10 cb3.0 ma.12 ha.0 ma.13 o.1 ma.14 ha.1 cb3.2 ha.2 i.0 da0.0 qb1.2 mb.1 mb.2 mb.3 hb.0 mb.4 da0.2 mb.5 mb.6 da1.0 mb.7 hb.1 mb.9 mb.8 hb.2 mb.10 da2.0 mb.12 mb.13 mb.14 da3.0 da2.2 da3.2 db0.0 o.0 ea.0 ea.1 ea.2 ea.3 o.2 db1.0 ra.0 db0.2 db2.0 db3.0 o.3 db2.2 o.4 xa.0 ea.7 eb.0 eb.1 eb.2 eb.3 a.0 eb.7 w.1 w.0 a.1 w.4 ua.1+ w.2 rb.0 ua.2+ w.3 ua.3+ rb.1 ua.4+ w.5 ua.5+ xb.0 ka.0+ w.10
S qb0.2 ya1.0 ya2.0 ja0.1 ya3.0 ja2.1 ja1.1 mb.11 da1.2 ga.0 ja3.1 yb0.0 yb2.0 yb1.0 jb0.1 ea.5 jb1.1 yb3.0 db1.2 jb2.1 gb.0 jb3.1 db3.2 eb.5 w.7 a.3 w.8 ca2.0+ ca3.0+ w.12 w.13 ca3.2+ ca2.2+ qa0.2+ cb0.0+ cb1.0+ cb0.2+ ma.11+ cb1.2+ cb2.2+ ya0.0+
P cb1.1 fa.0 qb1.0 qb0.1 qb1.1 fa.1 ja0.0 da0.1 ja2.0 ja1.0 ja0.2 da0.3 ja2.2 ja3.0 da2.1 da1.3 ja1.2 ja3.2 da3.1 da2.3 da3.3 jb0.0 ea.4 jb1.0 fb.1 ea.6 jb2.0 db0.1 db0.3 jb0.2 jb3.0 db2.1 db1.3 jb2.2 jb1.2 db2.3 jb3.2 db3.3 eb.4 ua.0+ eb.6 w.6 a.2 w.9 na.0+ w.11 ca2.1+ ca3.1+ qa0.0+ ub.0+ qa0.1+ qa1.1+ nb.0+ na.2+ fb.0+ nb.2+ cb0.1+
G ra.2 rb.2 w.14
Y xa.1- ta.0 ta.1 ta.2 tb.2 tb.1 tb.0
"""
ORDER = """
V ub.1 na.1 ub.2 ma.0 ub.3 ma.1 ub.4 qa1.2 ub.5 ma.2 kb.0 ma.3 ma.4 nb.1 ma.5 cb2.0 ma.6 ma.7 ma.9 ma.8 ma.10 cb3.0 ma.12 mb.0 ma.13 cb3.2 ma.14 ha.0 o.1 i.0 ha.1 hb.0 ha.2 qb1.2 mb.1 mb.2 da0.0 mb.3 mb.4 o.0 mb.5 da0.2 mb.6 o.2 mb.7 mb.9 mb.8 da1.0 mb.10 da2.0 mb.12 da2.2 mb.13 hb.1 mb.14 da3.0 hb.2 da3.2 db0.0 ea.0 ea.1 db1.0 o.3 ra.0 db0.2 db2.0 db3.0 db2.2 xa.0 o.4 eb.0 eb.1 a.0 a.1 w.1 w.0 a.2 w.2 rb.1 rb.0 w.3 p.0 xb.0 ua.1+ ua.2+ w.4 ua.3+ ua.4+ w.5 ua.5+ ka.0+ w.10 ca0.0+ ca1.0+ ca0.2+ ca1.2+ s.0
S eb.3 a.4 w.7 w.8 ca2.0+ ca3.0+ w.12 w.13 ca2.2+ ca3.2+ qa0.2+ cb0.0+ cb1.0+ cb0.2+ ma.11+ cb1.2+ ga.0+ cb2.2+ ya0.0+ qb0.2+ ya1.0+ ja0.1+ ya2.0+ ja1.1+ ya3.0+ mb.11+ da1.2+ ja2.1+ ja3.1+ yb0.0+ yb1.0+ yb2.0+ jb0.1+ ea.3+ jb1.1+ yb3.0+ jb2.1+ gb.0+ db1.2+ jb3.1+ db3.2+
P fa.0 qb1.0 qb0.1 qb1.1 fa.1 ja0.0 ja1.0 da0.3 ja2.0 da0.1 ja0.2 ja1.2 ja3.0 da2.1 da2.3 da1.3 ja2.2 fb.1 ja3.2 da3.1 da3.3 jb0.0 jb1.0 ea.2 jb0.2 ea.4 jb2.0 jb1.2 db0.1 jb3.0 db2.1 db0.3 jb2.2 db1.3 db2.3 jb3.2 db3.3 eb.2 eb.4 ua.0+ a.3 w.6 w.9 na.0+ w.11 ca2.1+ ca3.1+ qa0.0+ ub.0+ qa0.1+ qa1.1+ nb.0+ fb.0+ na.2+ nb.2+ cb0.1+ cb1.1+
G w.14- ra.2 rb.2
Y tb.0 tb.2 tb.1 xa.1 ta.0+ ta.2+ ta.1+
"""
ORDER = """
V ub.5 kb.0 qa1.2 ma.2 ma.3 ma.4 ma.5 ma.6 nb.1 ma.7 mb.0 ma.8 ma.9 ma.10 cb3.0 cb2.0 ma.12 hb.0 ma.13 ha.0 ma.14 ha.1 i.0 qb1.2 ha.2 mb.2 o.1 mb.1 mb.3 da0.0 mb.4 mb.5 o.0 o.4 mb.6 da0.2 mb.7 da1.0 mb.8 mb.9 hb.1 mb.10 da2.0 mb.12 o.2 mb.13 da2.2 mb.14 da3.0 hb.2 da3.2 db0.0 ea.0 o.3 ea.1 db0.2 db2.0 ra.0 db1.0 db2.2 db3.0 xa.0 eb.0 eb.1 a.0 a.1 a.2 w.0 w.1 p.0 w.2 rb.0 rb.1 w.3 xb.0 ua.1+ ua.2+ ua.3+ ua.4+ ua.5+ ma.0+ ka.0+ w.10 ca0.0+ na.1+ w.4 ca1.0+ w.5 s.0 ub.1+ ma.1+ ub.2+ ub.3+ ub.4+
S eb.3 ta.0+ w.7 a.4 w.8 ta.1+ ca2.0+ ca3.0+ w.12 ca0.2+ w.13 ca1.2+ ca3.2+ ca2.2+ qa0.2+ cb0.0+ cb1.0+ cb0.2+ ma.11+ cb1.2+ cb3.2+ cb2.2+ qb0.2+ ya0.0+ ya1.0+ ya2.0+ ja0.1+ ya3.0+ ja2.1+ mb.11+ ja1.1+ da1.2+ ja3.1+ yb0.0+ yb1.0+ yb2.0+ ga.0+ ea.3+ jb1.1+ jb0.1+ yb3.0+ gb.0+ db1.2+ jb2.1+ jb3.1+ db3.2+
P qa1.1 cb0.1 cb1.1 nb.2 na.2 fa.0 fb.0 qb0.1 qb1.1 fb.1 ja0.0 ja1.0 fa.1 da0.1 ja2.0 da0.3 ja0.2 ja3.0 da2.1 ja1.2 ja2.2 da2.3 da1.3 ja3.2 da3.1 da3.3 jb1.0 jb0.0 ea.2 ea.4 db0.3 jb1.2 db2.1 jb2.0 jb3.0 db0.1 db2.3 jb0.2 jb2.2 db1.3 jb3.2 db3.3 eb.2 eb.4 ua.0+ a.3 w.6 w.9 na.0+ w.11 ca2.1+ ca3.1+ ub.0+ qa0.1+ nb.0+
G ra.2 rb.2 w.14
Y tb.1- xa.1- tb.2 tb.0
"""
SCRATCH = {
    "XS": ("sbuf", [128, W + POS], "bfloat16"), "DL": ("sbuf", [128, 2 * ND], "bfloat16"),
    "ST": ("sbuf", [128, NV * SLOT], "bfloat16"),
    "AB": ("sbuf", [128, 50000], "bfloat16"), "AF": ("sbuf", [128, 5000], "float32"),
    "AI": ("sbuf", [128, 4000], "int32"), "AU": ("sbuf", [128, 1500], "uint16"),
    "AK": ("sbuf", [128, 2 * QL, 16], "bfloat16"),
    "PJH": ("psum", [128, 1024], "float32"), "PD0": ("psum", [128, 32, 16], "float32"),
    "PD1": ("psum", [128, 32, 16], "float32"), "PK0": ("psum", [128, 512], "float32"),
    "PU": ("psum", [128, 512], "float32"), "PW": ("psum", [128, 512], "float32"),
    "PK1": ("psum", [128, 512], "float32"),
}
AB = "ab"
SEMAPHORES = ["cV", "cS", "cP", "cG", "ls"] + ["d%d" % i for i in range(70)] + ["r%d" % i for i in range(16)]
BYTES = {"AK": 2, "XS": 2, "DL": 2, "ST": 2, "AB": 2, "AF": 4, "AI": 4, "AU": 2}


def A(name, c0, c1, step=1, p0=0, p1=128):
    return (name, c0, c1, step, p0, p1)


def sl(a, i, j, step=1, p0=None, p1=None):
    return (a[0], a[1] + i, a[1] + j, step, a[4] if p0 is None else p0, a[5] if p1 is None else p1)


def rows(a, k0, k1):
    return a[:6] + ((k0, k1),)


def width(a):
    n = (a[2] - a[1] + a[3] - 1) // a[3]
    return n if len(a) == 6 else n // 16 * (a[6][1] - a[6][0])


def isap(a):
    return isinstance(a, tuple)


def price(o, m):
    k, n = o["size"]
    c = 0.83 * m["F"]
    if k == "v":
        return m["OV"] + max(64, n) * c, 0
    if k == "t":
        return m["OV"] + max(64, n * m["TT"]) * c, 0
    if k == "g":
        return (50 if o["eng"] == "V" else 65) + n * m["G"] * c, 0
    if k == "s":
        return 50 + n * m["SC"] * c, 0
    if k == "p":
        return 30 + n * m["PE"] * m["F"], 0
    if k == "i":
        return 130 + 2 * n * c, 0
    if k == "d":
        return 60, 2000 + n / m["BW"]
    return 900, m["REM"] + n


def build():
    ops, now = [], ["init", 0]
    top = {"AB": 0, "AF": 0, "AI": 0, "AU": 0}

    def al(name, n):
        c = top[name]
        top[name] = c + (n + 15) // 16 * 16
        assert top[name] <= SCRATCH[name][1][1], name
        return A(name, c, c + n)

    def op(eng, size, call, rd, wr, **kw):
        o = {"eng": eng, "size": size, "call": call, "rd": [r for r in rd if isap(r)], "wr": wr, "id": len(ops)}
        o.update(kw)
        o["tag"], o["nth"] = now[0], now[1]
        now[1] += 1
        ops.append(o)
        return o

    def at(tag):
        now[0], now[1] = tag, 0

    def two(*aps):
        return all(BYTES.get(a[0], 4) == 2 for a in aps if isap(a))

    def copy(out, in_, ind=None, sc=None):
        if ind is not None:
            return op("V", ("g", width(out)), ("copy", out, in_, ind, None), [in_, ind], [out])
        if sc is not None:
            return op("V", ("s", width(in_)), ("copy", out, in_, None, sc), [in_, sc], [out])
        return op("V", ("v", width(out) * (0.5 if two(out, in_) else 1)), ("copy", out, in_, None, None), [in_], [out])

    def tt(out, a, b, o, ind=None):
        if ind is not None:
            c = ("g", width(out))
        elif a[0][0] == "P" or b[0][0] == "P":
            c = ("v", width(out))
        else:
            c = ("t", width(out)) if two(out, a, b) else ("v", 2 * width(out))
        return op("V", c, ("tt", out, a, b, o, ind), [a, b, ind], [out])

    def ts(out, a, s1, s2, o0, o1=None, ind=None):
        c = ("g", width(out)) if ind is not None else ("v", width(out) * (0.5 if two(out, a) else 1))
        return op("V", c, ("ts", out, a, s1, s2, o0, o1, ind), [a, s1, s2, ind], [out])

    def act(out, a, f, bias=None, scale=None, ind=None, acc=None):
        c = ("g" if ind is not None else "v", width(out))
        return op("S", c, ("act", out, a, f, bias, scale, ind, acc), [a, bias, scale, ind], [out] + ([acc] if acc else []))

    def mm(lst, **kw):
        c = sum(max(min(64, width(m[1])), width(m[2])) * (4 if m[1][0] == "AF" else 1) for m in lst)
        return op("P", ("p", c), ("mm", lst), [m[1] for m in lst] + [m[2] for m in lst], [m[0] for m in lst], **kw)

    def iota(out, pat, base=0, cm=0):
        return op("G", ("i", width(out)), ("iota", out, pat, base, cm), [], [out])

    def memset(out, v):
        return op("V", ("v", width(out) * 0.5), ("memset", out, v), [], [out])

    def dma(q, out, in_, nbytes):
        rd = [in_] if in_[0] in SCRATCH else []
        wr = [out] if out[0] in SCRATCH else []
        return op(q, ("d", nbytes), ("dma", out, in_), rd, wr, dma=True, far=True)

    add, sub, mul, mx, mn = ALU.add, ALU.subtract, ALU.mult, ALU.max, ALU.min
    band, shr, eq = ALU.bitwise_and, ALU.logical_shift_right, ALU.is_equal
    ID = ACT.Identity

    def slot(t):
        return A("ST", t * SLOT, (t + 1) * SLOT)

    def part(a, p, n=QL):
        return sl(a, n * p, n * p + n)

    ZT = [[al("AB", 4 * QL) for p in range(NP)] for t in range(NV)]
    ZX = [[al("AB", 2 * QL) for p in range(NP)] for t in range(NV)]

    wti, kpi, lmi, cni = al("AI", 1), al("AI", 1), al("AI", 2), al("AI", 256)
    dma("Y", wti, A("wt", 0, 1), 0)
    dma("A", part(ZT[0][0], 0), A("zed", 0, QL), 32768)
    dma("A", kpi, A("kap", 0, 1), 0)
    dma("Y", A("XS", 0, W), A("stock", 0, W), 1 << 20)
    dma("A", part(ZT[0][1], 0), A("zed", QL, 2 * QL), 1 << 20)
    dma("A", sl(lmi, 0, 2, 1, 0, 8), A("lim", 0, 2, 1, 0, 8), 1 << 20)
    dma("A", sl(cni, 0, 256, 1, 0, 8), A("cnt", 0, 256, 1, 0, 8), 1 << 20)
    dma("Y", A("DL", 0, ND), A("donor", 0, ND), 5 << 18)
    dma("Y", A("XS", W, XW), A("stock", 0, XW - W), 6 << 18)
    dma("Y", sl(slot(0), 304, 560), A("rend", 0, 256), 6 << 18)
    dma("Y", sl(slot(0), 48, 304), A("lend", 0, 256), 6 << 18)

    PI, t1, t2, t3, t4 = [al("AI", 1) for _ in range(5)]
    XI, X16, X8 = al("AF", 144), al("AF", 128), al("AF", 128)
    iota(PI, [[0, 1]], 0, 1)
    iota(XI, [[1, 144]])
    iota(X16, [[16, 8], [0, 16]])
    iota(X8, [[256, 16], [0, 8]])
    G16, PM, Pf, wf, kf, P7, P3 = [al("AF", 1) for _ in range(7)]
    ts(t1, PI, 112, None, band); copy(G16, t1)
    ts(t2, PI, 15, None, band); copy(PM, t2)
    ts(t3, PI, 7, None, band); copy(P7, t3)
    ts(t4, PI, 3, 1, shr, band); copy(P3, t4)
    copy(Pf, PI); copy(wf, wti); copy(kf, kpi)
    BO, WBO, I1, NI, HI, BIGI, ON = [al("AB", 128) for _ in range(7)]
    M1, MW, MP, MN, M2P, M2N = [al("AB", 144) for _ in range(6)]
    ts(M1, XI, G16, 15.0, sub, eq)
    ts(MW, M1, wf, None, mul)
    ts(WBO, X16, G16, wf, eq, mul)
    ts(BO, X16, G16, None, eq)
    ts(I1, sl(XI, 0, 128), Pf, None, eq)
    act(NI, I1, ID, scale=-1.0)
    act(MP, M1, ID, scale=4096.0); act(MN, M1, ID, scale=-4096.0)
    act(M2P, M1, ID, scale=8192.0); act(M2N, M1, ID, scale=-8192.0)
    act(HI, I1, ID, scale=0.5); act(BIGI, I1, ID, scale=-33554432.0)
    memset(ON, 1.0 / 256)

    def win(M, b):
        return sl(M, 15 - b, 143 - b)

    PM256, B128, K37, R8, TC, P16, PL2, NK0, PN256 = [al("AF", 1) for _ in range(9)]
    ts(PM256, PM, 256.0, None, mul); ts(B128, PM, 128.0, 256.0, mul, add); ts(K37, PM, 37.0, None, mul)
    ts(R8, PM, -8.0, -6.5, mul, add); ts(TC, P7, 16.0, P3, mul, add); ts(P16, Pf, 16.0, None, mul)
    ts(PL2, PM, 2.0, None, ALU.is_lt)
    ts(PN256, PM, 256.0, -256.0, mul, add)
    kx, km, kw, KM, K32 = al("AB", 128), al("AB", 128), al("AB", 128), al("AB", 128), al("AF", 128)
    ts(kx, X8, PM256, kf, eq, mul)
    mm([(A("PK1", 0, 128), BO, kx, True, True)])
    act(K32, A("PK1", 0, 128), ID, scale=32.0)
    act(NK0, A("PK1", 0, 1), ID, scale=-1.0)
    REP8, REPA, TAU = al("AU", 8), al("AU", 16), al("AU", 8)
    ts(REP8, sl(XI, 0, 8), 0.0, P7, mul, add)
    ts(TAU, sl(XI, 0, 8), 2.0, TC, mul, add)
    copy(REPA, sl(XI, 0, 16))
    K12, CODE, SK, SC = al("AF", 256), al("AF", 256), al("AF", 16), al("AF", 512)
    iota(K12, [[0, 16], [8, 16]])
    iota(CODE, [[-8, 128], [-6, 2]], 2054)
    iota(SK, [[0, 2], [-128, 8]], 2054)
    RC, K0, P2, P34 = al("AB", 256), al("AB", 128), al("AF", 1), al("AF", 1)
    ts(P2, PM, 2.0, None, eq); ts(P34, PM, 3.0, None, ALU.is_ge)
    ts(K0, sl(K12, 0, 128), 0.0, P2, eq, mul)
    ts(sl(RC, 1, 256, 2), K0, 0.0, P34, mul, add)
    ts(sl(RC, 0, 256, 2), K0, PL2, None, mx)
    memset(sl(K12, 0, 256, 16), 260.0)
    KR = al("AB", 256)
    act(KR, K12, ID, bias=4.0, scale=-1.0)
    ts(sl(CODE, 0, 256, 32), sl(CODE, 0, 256, 32), 1.0, None, add)
    PB, BB = al("AF", 16), al("AB", 2048)
    ts(PB, sl(XI, 0, 16), PM, None, eq)
    for b in range(16):
        act(sl(BB, 128 * b, 128 * b + 128), BO, ID, scale=sl(PB, b, b + 1))
    P0K = al("AF", 1)
    ts(km, X8, PN256, PN256, eq, mul)
    ts(P0K, sl(PB, 0, 1), 3840.0, None, mul)
    ts(kw, X8, 3840.0, P0K, eq, mul)
    tt(KM, kx, km, add); tt(KM, KM, kw, add)
    c0, c1, CQ = al("AF", 1), al("AF", 1), al("AB", 128)
    ts(c0, sl(PB, 0, 1), -2048.0, None, mul); ts(c1, sl(PB, 1, 2), 32.0, c0, mul, add)
    ts(c0, sl(PB, 2, 3), -31.5, c1, mul, add); ts(CQ, X16, 0.0, c0, mul, add)
    BASE, FL, CXD = al("AF", 64), al("AB", 48), al("AF", 32)
    LANE = sl(BASE, 32, 48)
    ts(LANE, sl(XI, 0, 16), 16.0, PM, mul, add)
    ts(sl(BASE, 48, 64), sl(XI, 0, 16), 16.0, PM, mul, add)
    ts(sl(CXD, 0, 8), sl(LANE, 0, 8), 16.0, None, mul); ts(sl(CXD, 8, 16), sl(LANE, 0, 8), 16.0, None, mul)
    ts(sl(CXD, 16, 32), LANE, 4.0, None, mul)
    lmf, E8, M8, n8r = al("AF", 2), al("AF", 128), al("AB", 144), al("AB", 256)
    r8 = lambda a: sl(a, 0, width(a), 1, 0, 8)
    copy(r8(lmf), r8(lmi))
    ts(r8(E8), r8(X16), r8(P16), None, eq)
    ts(r8(M8), r8(XI), r8(P16), 15.0, sub, eq)
    ts(r8(n8r), r8(cni), 8.0, None, mul)
    mm([(A("PW", 0, 2), r8(E8), r8(lmf), True, True)])
    li, lhi, lli, lh, ll = al("AI", 2), al("AI", 2), al("AI", 2), al("AF", 2), al("AF", 2)
    ts(sl(li, 0, 1), A("PW", 0, 1), 1.0, None, add); copy(sl(li, 1, 2), A("PW", 1, 2))
    ts(lhi, li, 8128, None, band); ts(lli, li, 63, None, band); copy(lh, lhi); copy(ll, lli)
    s0, s1, s2, sv = al("AF", 2), al("AF", 2), al("AF", 1), al("AF", 2)
    ts(s0, sl(PB, 0, 4, 3), sl(lh, 1, 2), None, mul); ts(s1, sl(PB, 1, 5, 3), sl(ll, 1, 2), None, mul)
    ts(sl(s0, 1, 2), sl(PB, 3, 4), sl(lh, 0, 1), -1.0, mul, mul); ts(sl(s1, 1, 2), sl(PB, 4, 5), sl(ll, 0, 1), -1.0, mul, mul)
    tt(sv, s0, s1, add); tt(s2, sl(sv, 0, 1), sl(sv, 1, 2), add)
    ts(s2, sl(PB, 2, 3), -8192.0, s2, mul, add)
    LJ = al("AB", 128)
    ts(LJ, BO, s2, -4096.0, mul, mul)
    mm([(A("PW", 16, 32), r8(win(M8, b)), sl(r8(n8r), b, 256, 16), b == 0, b == 15) for b in range(16)])
    act(sl(slot(0), 32, 48), A("PW", 16, 32), ID)

    B = []
    for p in range(NP):
        d = {k: al("AB", POS) for k in ("cd", "ca", "hd", "ha")}
        d["ja"] = A("AK", POS * p, POS * (p + 1))
        memset(rows(d["ja"], 0, 2), 0.0)
        d["y0"] = al("AB", POS + 16)
        d["y"] = sl(d["y0"], 16, POS + 16)
        memset(sl(d["y0"], 0, 16), 0.0)
        for k, n in (("ur", 8), ("cp", 128), ("cq", 128), ("km", 8), ("kap", 8), ("c", 8), ("cc", 16),
                     ("hp", 128), ("hq", 128), ("yp", 128), ("yq", 128)):
            d[k] = al("AI", n)
        for k, n in (("b0", 8), ("bA", 8), ("v", 128), ("k1", 64), ("k2", 64), ("k3", 32), ("k4", 16), ("cu", 8),
                     ("u32", 128)):
            d[k] = al("AF", n)
        for k, n in (("co", 128), ("cco", 16), ("ho", 128), ("yo", 128), ("eo", 8)):
            d[k] = al("AU", n)
        for k in ("q", "xc", "ye"):
            d[k] = al("AB", QL)
        B.append(d)
    U, UM, KI, TK = al("AI", 16), al("AI", 32), al("AI", 16), al("AI", 16)
    AC, junk, O48, N2, NF = al("AF", 1), al("AF", 16), al("AF", 48), al("AF", 32), al("AF", 256)
    XO, OO = al("AU", 16), al("AU", 48)
    INV, DD, ALT, SG, TM = al("AB", 272), al("AB", 256), al("AB", 256), al("AB", 512), al("AB", 512)
    memset(sl(INV, 256, 272), 0.0)
    QUART = al("AB", 2 * QL)
    memset(QUART, 0.25)
    XE = A("XS", 0, XW)
    dma("Y", A("XS", XW, W + POS), A("stock", XW - W, POS), 2 << 20)
    rot = [0]

    def bank():
        rot[0] += 1
        return A("PD#%d" % rot[0], 0, 512)

    def u32(p):
        return A("PU", QL * p, QL * p + QL)

    def stage_u(t, p):
        d, z = B[p], part(ZT[t][p], 0)
        lp, rw, u = A("PU", 256 + 8 * p, 264 + 8 * p), A("PU", 272, 400), part(U, p, 8)
        at("u" + AB[p])
        mm([(lp, win(MW, b), sl(z, b, QL, 16), b == 0, b == 15) for b in range(16)])
        copy(d["ur"], lp)
        ts(u, d["ur"], 4095, None, band)
        tt(d["v"], u, K32, add, ind=REP8)
        tt(d["cp"], u, d["v"], mul, ind=REP8)
        ts(d["cq"], d["cp"], 5, 4095, shr, band)
        at("t" + AB[p])
        if CFG["tile"][p] == "D":
            for m in range(1, 4):
                dma("Y", part(ZT[t][p], m), z if t else A("zed", QL * p, QL * p + QL), 32768 if t else 1 << 20)
        else:
            for n in (QL, 2 * QL):
                if CFG["tile"][p] == "S":
                    act(sl(ZT[t][p], n, 2 * n), sl(ZT[t][p], 0, n), ID)
                else:
                    copy(sl(ZT[t][p], n, 2 * n), sl(ZT[t][p], 0, n))
        at("n" + AB[p])
        mm([(rw, WBO, z, True, False), (rw, BO, CQ, False, True)])
        ts(d["q"], rw, ROUND4096, ROUND4096, add, sub)
        mm([(u32(p), WBO, z, True, False), (u32(p), part(BB, 1), CQ, False, False), (u32(p), NI, d["q"], False, True)])
        if CFG["fuse"][p]:
            act(d["u32"], u32(p), ID)

    def stage_o(t):
        at("o")
        ts(sl(UM, 0, 16), U, 15, None, band); ts(sl(UM, 16, 32), U, 3, None, band)
        tt(sl(BASE, 0, 32), UM, CXD, add)
        copy(XO, sl(BASE, 0, 16))
        ts(sl(slot(t), 0, 16), sl(UM, 16, 32), 8.0, 8.0, mul, add)
        at("i")
        if CFG["inv"] == "V":
            tt(sl(INV, 0, 256), sl(slot(t), 32, 48), K12, ALU.is_ge, ind=REPA)
        else:
            pi = A("PW", 0, 256)
            mm([(pi, part(BB, 0), KR, True, False)] + [(sl(pi, k, 256, 16), I1, sl(slot(t), 32, 48), False, k == 15) for k in range(16)])
            act(sl(INV, 0, 256), pi, ACT.Relu)

    def stage_c(t, p):
        d, zt = B[p], ZT[t][p]
        z = part(zt, 0)
        XC = A("XS", 0, W + POS if t else W)
        at("k" + AB[p])
        ts(d["co"], d["cq"], AC if t else 0.0, None, add)
        path = CFG["c"][p]
        for c in range(4):
            at("c%s%d" % (AB[p], c))
            lo = 512 * c
            cd, ca = sl(d["cd"], lo, lo + 512), sl(d["ca"], lo, lo + 512)
            if path[c] in "RV":
                tt(cd, XC, zt, sub, ind=part(d["co"], c, 32))
                now[1] = 2
                if path[c] == "V":
                    act(ca, cd, ACT.Abs, scale=0.5)
                else:
                    ts(ca, cd, 0.0, None, mx)
            else:
                act(cd, XC, ID, ind=part(d["co"], c, 32))
                pd = bank()
                lst = []
                for m in range(4):
                    lst += [(part(pd, m), I1, part(cd, m), True, False), (part(pd, m), NI, z, False, True)]
                mm(lst)
                act(ca, pd, ACT.Abs, scale=0.5)
            if c & 1:
                h = c >> 1
                at("q%s%d" % (AB[p], h))
                pk = A("PK%d" % h, 0, 64)
                lst = [(pk, BO, part(KM, h, 64), True, False)]
                r = [x for x in (0, 1) if path[c - 1 + x] == "R"]
                if r:
                    x0, x1 = r[0], r[-1] + 1
                    lst += [(sl(pk, 32 * x0, 32 * x1), win(MN, b), sl(d["cd"], 1024 * h + 512 * x0 + b, 1024 * h + 512 * x1, 16), False, False) for b in range(16)]
                    mm(lst)
                    lst = []
                now[1] = 1
                mm(lst + [(pk, win(M2P, b), sl(d["ca"], 1024 * h + b, 1024 * h + 1024, 16), False, b == 15) for b in range(16)])
                if h == 0:
                    act(d["k1"], pk, ID)
                else:
                    tt(d["k2"], pk, d["k1"], mn)

    def stage_m(t, p):
        d, u = B[p], part(U, p, 8)
        at("m" + AB[p])
        ts(d["b0"], u, NK0, AC if t else 0.0, mul, add)
        tt(d["bA"], d["b0"], sl(d["cq"], 0, 8), add)
        for a, b, n in (("k2", "k3", 32), ("k3", "k4", 16), ("k4", "km", 8)):
            tt(d[b], sl(d[a], 0, n), sl(d[a], n, 2 * n), mn)
        ts(d["kap"], d["km"], 255, None, band)
        tt(d["cu"], d["kap"], u, mul)
        tt(d["c"], d["cu"], d["bA"], add)
        ts(sl(d["cc"], 0, 8), d["c"], 1023, None, band); ts(sl(d["cc"], 8, 16), d["c"], 4095, None, band)
        copy(d["cco"], d["cc"])
        act(part(DD, p), A("DL", 0, ND), ID, ind=sl(d["cco"], 0, 8))
        if CFG["fuse"][p]:
            tt(d["yp"], A("DL", 0, ND), d["u32"], mul, ind=sl(d["cco"], 0, 8))
        else:
            tt(d["yp"], u32(p), part(DD, p), mul)
        ts(d["yq"], d["yp"], 5, 4095, shr, band)
        ts(d["yo"], d["yq"], K37, None, add, ind=TAU)
        at("g" + AB[p])
        act(d["xc"], A("XS", 0, W), ID, ind=sl(d["cco"], 8, 16))

    def stage_h(t, p):
        d = B[p]
        at("h" + AB[p])
        tt(d["hp"], u32(p), part(sl(slot(t), 304, 560), p), mul)
        ts(d["hq"], d["hp"], 5, 4095, shr, band)
        ts(d["ho"], d["hq"], K37, None, add, ind=TAU)

    def stage_y(t, p):
        d = B[p]
        pjh = A("PJH", 512 * p, 512 * p + 256)
        pj, ph = sl(pjh, 0, 256, 2), sl(pjh, 1, 256, 2)
        at("f" + AB[p])
        first = mm([(pjh, LJ, RC, True, False)])
        first["wr"] = [A("PJH", 512 * p, 512 * p + 512)]
        upto = mm([(pj, BIGI, sl(INV, QL * p, QL * p + QL), False, False), (ph, BIGI, sl(INV, QL * p + 1, QL * p + QL + 1), False, False)], after=[first])
        sums = [upto]
        lo = 0
        for c, ch in enumerate(CFG["ych"][p]):
            at("y%s%d" % (AB[p], c))
            act(sl(d["y"], lo, lo + ch), XE, ID, ind=sl(d["yo"], lo // 16, (lo + ch) // 16))
            lo += ch
        for c in range(4):
            pd, lo = bank(), 512 * c
            at("j%s%d" % (AB[p], c))
            mm([(pd, I1, part(d["y"], c, 512), True, False), (pd, NI, sl(d["y0"], 15 + lo, 527 + lo), False, True)])
            act(rows(part(d["ja"], c, 512), 2, 16), rows(pd, 2, 16), ACT.Abs)
            sums.append(mm([(pj, win(MP, b), part(d["ja"], b), False, False) for b in range(4 * c, 4 * c + 4)], after=[first]))
        lo = 0
        for c, ch in enumerate(CFG["hch"][p]):
            end = lo + ch == POS
            y = sl(d["y"], lo, lo + ch)
            hd, ha = sl(d["hd"], lo, lo + ch), sl(d["ha"], lo, lo + ch)
            ho = sl(d["ho"], lo // 16, (lo + ch) // 16)
            bs = range(lo // QL, (lo + ch) // QL)
            path = CFG["h"][p][c]
            at("d%s%d" % (AB[p], c))
            if path == "S":
                act(hd, XE, ID, ind=ho)
                pd = sl(bank(), 0, ch)
                mm([(pd, I1, hd, True, False), (pd, NI, y, False, True)])
                act(ha, pd, ACT.Abs, scale=0.5)
            else:
                tt(hd, XE, y, sub, ind=ho)
                if path == "V":
                    now[1] = 2
                    act(ha, hd, ACT.Abs, scale=0.5)
                else:
                    sums.append(mm([(ph, win(MP, b), part(d["hd"], b), False, False) for b in bs], after=[first]))
                    ts(ha, hd, 0.0, None, mx)
            sums.append(mm([(ph, win(M2N, b), part(d["ha"], b), False, end and b == bs[-1]) for b in bs], after=sums[:] if end else [first]))
            lo += ch

    nrem = [0]

    def send(src, dst):
        k = nrem[0]
        nrem[0] += 1
        op("G", ("r", width(src)), ("rem", dst, src, k), [src], [dst], rem=k, far=True)

    def stage_e(t, p):
        d, z = B[p], part(ZT[t][p], 0)
        at("e" + AB[p])
        pjh, sc = A("PJH", 512 * p, 512 * p + 256), part(SC, p, 256)
        op("V", ("v", 256), ("scan", sc, pjh, CODE, 2048.0 - 1017.0), [pjh, CODE], [sc])
        ts(d["eo"], sl(sc, 2, 256, 32), -0.125, B128, mul, add)
        ps = A("PJH", 512 * p + 256, 512 * p + 512)
        pz, px = part(ps, 0), part(ps, 1)
        pre = mm([(ps, HI, sl(ZT[t][p], 0, 2 * QL), True, False), (pz, NI, QUART, False, False), (px, HI, d["xc"], False, False)] if 0 else
                 [(ps, NI, QUART, True, False), (pz, HI, z, False, False), (px, HI, d["xc"], False, False)], rdx=[sc])
        act(d["ye"], d["y"], ID, ind=d["eo"])
        mm([(px, HI, d["ye"], False, False), (pz, HI, d["ye"], False, True)], after=[pre])
        at("r" + AB[p])
        if CFG["split"][p]:
            ts(part(ZX[t][p], 0), pz, ROUND1, ROUND1, add, sub)
            ts(part(ZX[t][p], 1), px, ROUND1, ROUND1, add, sub)
        else:
            ts(ZX[t][p], ps, ROUND1, ROUND1, add, sub)
        now[1] = 2
        if t + 1 < NV:
            send(part(ZX[t][p], 0), part(ZT[t + 1][p], 0))
        else:
            at("v" + AB[p])
            dma("Y", A("yz", QL * p, QL * p + QL), part(ZX[t][p], 0), 32768)

    def stage_x(t, p):
        lo = POS * p
        at("x" + AB[p])
        copy(A("XS", lo, lo + POS), part(ZX[t][p], 1), sc=part(XO, p, 8))
        if t + 1 == NV:
            at("z" + AB[p])
            dma("Y", A("yx", lo, lo + POS), A("XS", lo, lo + POS), 1 << 19)
        elif p == 0 and CFG["wrap"] == "D":
            dma("Y", A("XS", W, W + POS), A("XS", 0, POS), 1 << 19)
        elif p == 0:
            copy(A("XS", W, W + POS), part(ZX[t][p], 1), sc=part(XO, p, 8))

    def stage_w(t):
        s = slot(t)
        L, nn, Ln, Rn = sl(s, 48, 304), sl(s, 560, 576), sl(s, 576, 832), sl(s, 832, 1088)
        at("a")
        copy(KI, sl(SC, 2, 512, 32))
        ts(TK, KI, 3, None, band)
        ts(sl(FL, 32, 48), TK, 1.0, 256.0, ALU.is_lt, mul)
        if t + 1 < NV:
            mm([(A("PK0", 64, 80), ON, sl(FL, 32, 48), True, True)])
            act(junk, A("PK0", 64, 80), ID, acc=AC)
        at("p")
        tt(sl(s, 16, 32), SK, sl(SC, 2, 512, 32), sub)
        at("w")
        ts(sl(FL, 16, 32), TK, 2.0, 272.0, ALU.not_equal, mul)
        ts(sl(FL, 0, 16), TK, 2.0, 1024.0, eq, mul)
        tt(O48, FL, sl(BASE, 16, 64), add)
        copy(OO, O48)
        tt(N2, sl(s, 0, 32), sl(FL, 0, 32), add)
        tt(nn, sl(N2, 0, 16), sl(N2, 16, 32), mn)
        mm([(A("PW", b, 512, 16), part(BB, b), sl(s, 16, 48), True, True) for b in range(16)])
        act(ALT, sl(s, 48, 560), ID, ind=sl(OO, 32, 48))
        act(SG, A("PW", 0, 512), ACT.Sign, bias=R8)
        pd = A("PJH", 0, 512)
        pa, pb = part(pd, 0, 256), part(pd, 1, 256)
        mm([(pb, I1, L, True, False), (pb, NI, DD, False, True), (pa, I1, DD, True, False), (pa, NI, ALT, False, True)])
        tt(TM, pd, SG, mul)
        pa = A("PW", 0, 256)
        mm([(pa, HI, r, i == 0, i == 3) for i, r in enumerate((L, ALT, part(TM, 0, 256), part(TM, 1, 256)))])
        act(Ln, pa, ID)
        act(Rn, sl(s, 304, 832), ID, ind=sl(OO, 16, 32))
        if t + 1 < NV and CFG["inv"] == "V":
            send(sl(s, 560, 1088), sl(slot(t + 1), 32, 560))
        elif t + 1 < NV:
            send(sl(s, 576, 1088), sl(slot(t + 1), 48, 560))
            send(nn, sl(slot(t + 1), 32, 48))
        at("s")
        copy(A("DL", 0, 2 * ND), Ln, sc=sl(OO, 0, 16))
        if t + 1 == NV:
            at("l")
            dma("A", A("yl", 0, 256), Ln, 65536)
            dma("A", A("yr", 0, 256), Rn, 65536)
            pn = A("PU", 0, 256, 1, 0, 8)
            mm([(sl(pn, b, 256, 16), sl(BB, 128 * b, 128 * b + 128, 16), nn, True, True) for b in range(16)])
            act(r8(NF), pn, ID, scale=0.125)
            dma("A", A("yn", 0, 256, 1, 0, 8), r8(NF), 0)
            dma("Y", A("yd", 0, ND), A("DL", 0, ND), 1 << 18)

    def run(name, st, *a):
        k = len(ops)
        st(*a)
        for o in ops[k:]:
            o["t"] = a[0]
            o["key"] = "%s.%d" % (o["tag"], o["nth"])

    for t in range(NV):
        for name, st in (("u", stage_u), ("c", stage_c), ("m", stage_m), ("h", stage_h)):
            for p in range(NP):
                run(name, st, t, p)
        run("o", stage_o, t)
        for p in range(NP):
            run("y", stage_y, t, p)
            run("e", stage_e, t, p)
        for p in range(NP):
            run("x", stage_x, t, p)
        run("w", stage_w, t)
    return ops


def depend(ops):
    hist = {}
    for o in ops:
        hard, soft = set(), set()
        e = o["eng"]
        reads = o["rd"] + o.get("rdx", [])
        for a in reads:
            for (c0, c1, w, j) in hist.get(a[0], []):
                if w and c0 < a[2] and a[1] < c1:
                    hard.add(j)
        for a in o["wr"]:
            for (c0, c1, w, j) in hist.get(a[0], []):
                if c0 < a[2] and a[1] < c1:
                    x = ops[j]
                    if x["eng"] == e == "P":
                        if "after" not in o:
                            soft.add(j)
                    else:
                        hard.add(j)
        if "after" in o:
            soft.update(x["id"] for x in o["after"])
        for a in o["wr"]:
            h = hist.setdefault(a[0], [])
            if a[3] == 1 and a[4] == 0 and a[5] == 128 and "after" not in o:
                h[:] = [x for x in h if not (a[1] <= x[0] and x[1] <= a[2])]
            h.append((a[1], a[2], True, o["id"]))
        for a in reads:
            hist.setdefault(a[0], []).append((a[1], a[2], False, o["id"]))
        hard.discard(o["id"]); soft.discard(o["id"])
        o["hard"], o["soft"] = sorted(hard), sorted(soft - hard)
        o["q"] = "S" if e == "A" else e
        o["banks"] = sorted({(a[0], k) for a in o["rd"] + o["wr"] if a[0][0] == "P" and "#" not in a[0] for k in range(a[1] // 512, (a[2] - 1) // 512 + 1)})
        o["take"] = [a[0] for a in o["wr"] if "#" in a[0]][:1]
        o["give"] = [a[0] for a in o["rd"] if "#" in a[0]][:1]
    for o in ops:
        o["succ"] = []
    for o in ops:
        for j in o["hard"]:
            ops[j]["succ"].append((o["id"], True))
        for j in o["soft"]:
            ops[j]["succ"].append((o["id"], False))


def order(ops, cost, lat, when):
    n = len(ops)
    pr = [0.0] * n
    for o in reversed(ops):
        i = o["id"]
        if "t" in o:
            pr[i] = -1000 * (CFG["T"] * o["t"] + when[o["tag"]] + when.get(o["key"], 0) + 0.02 * o["nth"])
        else:
            pr[i] = sum(cost[i]) + lat + max([pr[k] for k, _h in o["succ"]] + [-1e9])
    lent, name = [-1, -1], {}
    left = [len(o["hard"]) + len(o["soft"]) for o in ops]
    ready = {q: [] for q in "VSPGY"}
    est, t1 = [0.0] * n, [0.0] * n
    for o in ops:
        if left[o["id"]] == 0:
            ready[o["q"]].append(o["id"])
    free = {q: 0.0 for q in ready}
    held = {}
    seq, hand = [], [()] * n

    def start(i):
        s = est[i]
        for k in ops[i]["banks"]:
            h = held.get(k)
            if h and h[0] != ops[i]["q"] and t1[h[1]] + lat > s:
                s = t1[h[1]] + lat
        if ops[i]["take"]:
            s = max(s, min(1e18 if j is None else t1[j] + lat if j >= 0 else 0 for j in lent))
        return s

    while len(seq) < n:
        best = None
        for q, r in ready.items():
            if r:
                t0 = max(free[q], min(map(start, r)))
                if best is None or t0 < best[0]:
                    best = (t0, q)
        t0, q = best
        st = {k: start(k) for k in ready[q]}
        i = max((k for k in st if st[k] <= t0 + CFG["SLACK"]), key=lambda k: pr[k])
        if st[i] > t0:
            fit = [k for k in st if st[k] <= t0 and t0 + cost[k][0] <= st[i] + CFG["TOL"]]
            if fit:
                i = max(fit, key=lambda k: pr[k])
        ready[q].remove(i)
        o = ops[i]
        s = max(free[q], st[i])
        free[q] = s + cost[i][0]
        t1[i] = free[q] + cost[i][1]
        hand[i] = tuple(held[k][1] for k in o["banks"] if k in held and held[k][0] != q)
        for k in o["banks"]:
            held[k] = (q, i)
        if o["take"]:
            k = min((k for k in (0, 1) if lent[k] is not None), key=lambda k: t1[lent[k]] if lent[k] >= 0 else 0)
            hand[i] += (lent[k],) if lent[k] >= 0 else ()
            lent[k], name[o["take"][0]] = None, k
        if o["give"]:
            lent[name[o["give"][0]]] = i
        seq.append(i)
        for k, hard in o["succ"]:
            e = t1[i] + lat if hard else s
            if e > est[k]:
                est[k] = e
            left[k] -= 1
            if left[k] == 0:
                ready[ops[k]["q"]].append(k)
    return seq, hand, name


def rename(x, name):
    if isinstance(x, (tuple, list)):
        y = [rename(v, name) for v in x]
        return tuple(y) if isinstance(x, tuple) else y
    return "PD%d" % name[x] if isinstance(x, str) and x in name else x


def replay(ops, seq, hand, cost, lat):
    free = {q: 0.0 for q in "VSPGY"}
    t1 = [0.0] * len(ops)
    for i in seq:
        o = ops[i]
        s = free[o["q"]]
        for j in o["hard"]:
            if t1[j] + lat > s:
                s = t1[j] + lat
        for j in hand[i]:
            if t1[j] + lat > s:
                s = t1[j] + lat
        free[o["q"]] = s + cost[i][0]
        t1[i] = s + cost[i][0] + cost[i][1]
    return t1


def merge(ops, rows, cost, lat, pr):
    n = len(ops)
    left = [len(o["hard"]) + len(o["soft"]) for o in ops]
    est, t1, hand, seq = [0.0] * n, [0.0] * n, [()] * n, []
    listed = {i for q in rows for i in rows[q]}
    loose = {q: sorted((o["id"] for o in ops if o["q"] == q and o["id"] not in listed), key=lambda i: pr[i]) for q in rows}
    at, free = {q: 0 for q in rows}, {q: 0.0 for q in rows}
    held, lent, name = {}, [-1, -1], {}
    while len(seq) < n:
        best = None
        for q in rows:
            pick = None
            for i in loose[q] + rows[q][at[q]:at[q] + 1]:
                if left[i]:
                    continue
                s = max([est[i], free[q]] + [t1[held[k][1]] + lat for k in ops[i]["banks"] if k in held and held[k][0] != q])
                if ops[i]["take"]:
                    back = [t1[j] + lat if j >= 0 else 0 for j in lent if j is not None]
                    if not back:
                        continue
                    s = max(s, min(back))
                if pick is None or (s - 60 < pick[0] if pr[i] < pr[pick[2]] else s + 60 < pick[0]):
                    pick = (s, q, i)
            if pick and (best is None or pick[0] < best[0]):
                best = pick
        s, q, i = best
        o = ops[i]
        if i in listed:
            at[q] += 1
        else:
            loose[q].remove(i)
        free[q] = s + cost[i][0]
        t1[i] = free[q] + cost[i][1]
        hand[i] = tuple(held[k][1] for k in o["banks"] if k in held and held[k][0] != q)
        for k in o["banks"]:
            held[k] = (q, i)
        if o["take"]:
            k = min((k for k in (0, 1) if lent[k] is not None), key=lambda k: t1[lent[k]] if lent[k] >= 0 else 0)
            hand[i] += (lent[k],) if lent[k] >= 0 else ()
            lent[k], name[o["take"][0]] = None, k
        elif o["give"]:
            lent[name[o["give"][0]]] = i
        seq.append(i)
        for k, hard in o["succ"]:
            est[k] = max(est[k], t1[i] + lat if hard else s)
            left[k] -= 1
    return seq, hand, name, t1


def plan():
    ops = build()
    depend(ops)
    lat = MODELS[0]["LAT"]
    cost = [price(o, MODELS[0]) for o in ops]
    by = {(o["key"], o["t"]): o["id"] for o in ops if "t" in o and not (o["t"] == NV - 1 and o["tag"] in CFG["last"])}
    rows = {}
    for line in ORDER.strip().splitlines():
        q, *names = line.split()
        turn = [(x.rstrip("+-"), x.count("+") - x.count("-")) for x in names]
        rows[q] = [by[k, t + d] for t in range(-1, NV + 1) for k, d in turn if (k, t + d) in by]
    listed = {i for q in rows for i in rows[q]}
    pr = [0.0] * len(ops)
    bare = [cost[o["id"]] if "t" in o else (0, 0) for o in ops]
    t0 = merge(ops, rows, bare, lat, pr)[3]
    for o in reversed(ops):
        i = o["id"]
        pr[i] = t0[i] - sum(bare[i]) if i in listed else min([pr[k] for k, _h in o["succ"]] + [max(t0) - 1500]) - sum(cost[i]) - lat
    seq, hand, name, t1 = merge(ops, rows, cost, lat, pr)
    CFG["end"] = max(t1)
    for o in ops:
        o["call"] = rename(o["call"], name)
    pos = {q: 0 for q in "VSPG"}
    known = {q: ({}, set()) for q in "VSPGY"}
    for i in seq:
        o = ops[i]
        q = o["q"]
        cnt, one = known[q]
        waits = []
        for j in sorted(set(o["hard"]) | set(hand[i]), key=lambda j: -t1[j]):
            x = ops[j]
            if "far" in x:
                if j in one:
                    continue
                one.add(j)
            else:
                if cnt.get(x["eng"], -1) >= x["pos"]:
                    continue
                cnt[x["eng"]] = x["pos"]
            waits.append(j)
            x["need"] = True
            if "rem" not in x:
                for k, v in x["clock"][0].items():
                    cnt[k] = max(cnt.get(k, -1), v)
                one.update(x["clock"][1])
        o["waits"] = waits
        o["clock"] = (dict(cnt), set(one))
        if "far" not in o:
            o["pos"] = pos[q]
            pos[q] += 1
    num = {q: 0 for q in "VSPG"}
    nd = 0
    for i in seq:
        o = ops[i]
        if "dma" in o:
            o["sem"], o["val"] = "d%d" % nd, 16
            nd += 1
        elif "rem" in o:
            o["sem"] = "r%d" % o["rem"]
        elif o.get("need"):
            num[o["eng"]] += 1
            o["sem"], o["val"] = "c" + o["eng"], num[o["eng"]]
    return ops, seq, num


PLAN = []


def rank_program(g, core, T, topo):
    rank = T.rank_of(core)
    if rank is None:
        return
    if not PLAN:
        PLAN.append(plan())
    ops, seq, num = PLAN[0]
    n = len(T.cores)
    nxt, prv = T.cores[(rank + 1) % n], T.cores[(rank - 1) % n]
    rid, pid, _se = topo.addr(nxt)
    mask = topo.mask(core, nxt)
    out_n, in_n = len(topo.engines(core, nxt)), len(topo.engines(prv, core))
    Q = {"V": g.vector, "S": g.scalar, "P": g.tensor, "G": g, "Y": g.sync}

    def ap(a, ind=None):
        if not isap(a):
            return a
        k0, k1 = a[6] if len(a) > 6 else (0, 16)
        if len(SCRATCH.get(a[0], "--")[1]) == 3:
            v = T[a[0]][:, a[1] // 16:a[2] // 16, k0:k1]
        else:
            v = T[a[0]][a[4]:a[5], a[1]:a[2]:a[3]] if a[3] != 1 else T[a[0]][a[4]:a[5], a[1]:a[2]]
        return v if ind is None else v.indirect(ap(ind))

    sent = 0
    for i in seq:
        o = ops[i]
        q = Q[o["q"]]
        for j in o["waits"]:
            x = ops[j]
            q.wait_ge(T.sem[x["sem"]], in_n if "rem" in x else x["val"])
        c = o["call"]
        k = c[0]
        if k == "copy":
            r = q.tensor_copy(ap(c[1], c[4]), ap(c[2], c[3]))
        elif k == "tt":
            r = q.tensor_tensor(ap(c[1]), ap(c[2], c[5]), ap(c[3]), c[4])
        elif k == "ts":
            if c[6] is None:
                r = q.tensor_scalar(ap(c[1]), ap(c[2], c[7]), ap(c[3]), None, c[5])
            else:
                r = q.tensor_scalar(ap(c[1]), ap(c[2], c[7]), ap(c[3]), ap(c[4]), c[5], c[6])
        elif k == "scan":
            back = lambda a: T[a[0]][:, a[2] - 1:a[1] - 1:-1] if a[1] else T[a[0]][:, a[2] - 1::-1]
            r = q.tensor_tensor_scan(back(c[1]), back(c[2]), back(c[3]), c[4], ALU.max, ALU.min)
        elif k == "memset":
            r = q.memset(ap(c[1]), c[2])
        elif k == "act":
            kw = {}
            if c[4] is not None:
                kw["bias"] = ap(c[4])
            if c[5] is not None:
                kw["scale"] = ap(c[5])
            if c[7] is not None:
                kw["accum_out"] = ap(c[7])
            r = q.activation(ap(c[1]), ap(c[2], c[6]), c[3], **kw)
        elif k == "mm":
            for m in c[1]:
                r = q.matmul(ap(m[0]), ap(m[1]), ap(m[2]), m[3], m[4])
        elif k == "iota":
            if c[1][0] == "AI":
                r = q.iota(ap(c[1]), c[2], c[3], c[4])
            else:
                r = q.iota(ap(c[1]), c[2], c[3], c[4], allow_small_or_imprecise_dtypes=True)
        elif k == "dma":
            whole = lambda a: T[a[0]][:] if a[0] in ("wt", "kap", "lim", "cnt") else ap(a)
            r = q.dma_start(whole(c[1]), whole(c[2]))
        else:
            q.remote_dma(ap(c[1]), ap(c[2]), T.sem[o["sem"]], T.sem.ls, pid, rid, mask)
            sent += out_n
            continue
        if "sem" in o:
            r.then_inc(T.sem[o["sem"]], 16 if k == "dma" else 1)
    g.wait_ge(T.sem.ls, sent)
    for o in ops:
        if "dma" in o and not o.get("need"):
            g.wait_ge(T.sem[o["sem"]], 16)
